import numpy as np, ml_dtypes
CORES = [23,119,17,113]
N = 4
BF = ml_dtypes.bfloat16
def gentries(a):
    return np.ascontiguousarray(a.reshape(8, 16, -1).transpose(0, 2, 1)).reshape(8, -1)
def gtable(e):
    e = np.asarray(e); return np.ascontiguousarray(e.reshape(8, -1, 16).transpose(0, 2, 1)).reshape(128, -1).astype(np.int32)
V, B, L = 2048, 128, 3
W = V + (N - 1) * B
def parts(rng):
    x = (3 * rng.integers(0, 256, (N, 8, 1, V)) + rng.integers(0, 256, (N, 8, 16, V)) + rng.integers(0, 2, (N, 8, 16, V))) >> 2
    t = rng.integers(1, 97, (N, 8, 16, 1)); nx = np.argsort(rng.random((N, 8, 2 * W)), axis=-1)
    sh = np.argsort(rng.random((N, 8, N - 1, V)), axis=-1)[..., :B]
    return np.minimum(x, 255), t, np.ascontiguousarray(nx), np.ascontiguousarray(sh)
def both(rng, a):
    w = rng.integers(0, 2, (len(a), 1)); return 2 * a[:, None] + np.concatenate([w, 1 - w], axis=1)
def chains(rng, g, x, t, nx, sh):
    K = min(B, (V - B) // (3 * N) // 32 * 32); n = N * K
    t[:, g] = 256 * (N - 1) + 1; o = np.argsort(rng.random((N, N - 1, B)), axis=2)
    s = np.stack([3 * n + rng.permutation(V - 3 * n)[:B] for q in range(N)])
    for q in range(N):
        sh[q, g] = s[q][o[q]]
    for r in range(N):
        u = np.concatenate([s[r, :K]] + [V + (d - 1) * B + np.flatnonzero(o[(r - d) % N, d - 1] < K) for d in range(1, N)])
        m = rng.permutation(2 * n); a = m[:n]; e = m[n:]; b = 2 * n + rng.permutation(n)
        x[r, g][:, m] = 0; x[r, g][:, b] = 255; x[r, g][:, s[r, :K]] = 255
        nx[r, g] = np.arange(2 * W)
        for i, j in ((u, a), (a, b), (b, e), (e, u)):
            w = rng.integers(0, 2, n); nx[r, g, 2 * i] = 2 * j + w; nx[r, g, 2 * i + 1] = 2 * j + 1 - w
def put(rng, y, p, nodes, order, high):
    v = rng.integers(0, 4, (4, len(nodes))); y[:, nodes] = order; y[np.ix_(p, nodes)] = 255 - v if high else v
def swell(rng, g, x, t, nx, sh):
    K = 32; n = N * K; m = N * 8; lo = 4 * n
    p = rng.permutation(16)[:4]; t[:, g, p[:2]] = 4095; t[:, g, p[2]] = 0; t[:, g, p[3]] = 301
    o = np.argsort(rng.random((N, N - 1, B)), axis=2); s = np.stack([lo + rng.permutation(V - lo)[:B] for q in range(N)]); one = int(rng.integers(0, N))
    for q in range(N):
        sh[q, g] = s[q][o[q]]
    for r in range(N):
        u = rng.permutation(np.concatenate([s[r, :K]] + [V + (d - 1) * B + np.flatnonzero(o[(r - d) % N, d - 1] < K) for d in range(1, N)]))
        w = rng.permutation(lo); v = x[r, g]; y = nx[r, g]; y[:] = np.arange(2 * W); put(rng, v, p, s[r, :K], 0, True)
        if r != one:
            a = w[:n]; e = w[n:2 * n]; b = w[2 * n:3 * n]
            put(rng, v, p, w[:2 * n], 127, False); put(rng, v, p, b, 254, True)
            for i, j in ((u, a), (a, b), (b, e), (e, u)):
                y[both(rng, i)] = both(rng, j)
        else:
            c = w[:m]; zh = w[m:2 * m]; zl = w[2 * m:3 * m]; f1 = w[3 * m:5 * m]; f2 = w[5 * m:7 * m]; a1 = w[7 * m:10 * m]; a2 = w[10 * m:13 * m]; b = w[13 * m:16 * m]
            for i, k, h in ((c, 254, True), (zh, 254, False), (zl, 0, False), (f1, 127, True), (f2, 127, True), (a1, 127, False), (a2, 127, False), (b, 254, True)):
                put(rng, v, p, i, k, h)
            ui = both(rng, u); uo = both(rng, u)
            i = both(rng, f1); j = both(rng, f1)
            y[both(rng, c).ravel()] = i[:, 0]; y[both(rng, zh).ravel()] = i[:, 1]; y[j[:, 0]] = ui[:2 * m, 0]; y[j[:, 1]] = both(rng, zl).ravel()
            i = both(rng, f2); j = both(rng, f2)
            y[uo[2 * m:, 0]] = i[:, 0]; y[both(rng, zl).ravel()] = i[:, 1]; y[j[:, 0]] = both(rng, c).ravel(); y[j[:, 1]] = both(rng, zh).ravel()
            i = np.concatenate([ui[:2 * m, 1], ui[2 * m:].ravel()]); j = np.concatenate([uo[:2 * m].ravel(), uo[2 * m:, 1]])
            y[both(rng, b).ravel()] = rng.permutation(both(rng, a1).ravel()); y[both(rng, a1).ravel()] = rng.permutation(i)
            y[j] = rng.permutation(both(rng, a2).ravel()); y[both(rng, a2).ravel()] = rng.permutation(both(rng, b).ravel())
def crowd(rng, g, x, nx, sh, two):
    k = W // 5 if two else W // 2; lo = 3 * k if two else k
    x[:, g] = rng.integers(0, 256, (16, 1))
    for q in range(N):
        s = lo + rng.permutation(V - lo)[:B]; y = nx[q, g]; y[:] = np.arange(2 * W)
        for d in range(N - 1): sh[q, g, d] = rng.permutation(s)
        if two:
            ab = k + rng.permutation(2 * k); ce = 3 * k + rng.permutation(2 * k); five = (rng.permutation(k), ab[:k], ab[k:], ce[:k], ce[k:])
            om, oa, ob, oc, oe = [both(rng, z) for z in five]; im, ia, ib, ic, ie = [both(rng, z) for z in five]
            y[oa[:, 0]] = im[:, 0]; y[oa[:, 1]] = ic[:, 1]; y[ob[:, 0]] = im[:, 1]; y[ob[:, 1]] = ie[:, 1]; y[om[:, 0]] = ic[:, 0]; y[om[:, 1]] = ie[:, 0]
            y[oc[:, 0]] = ia[:, 0]; y[oc[:, 1]] = ib[:, 0]; y[oe[:, 0]] = ia[:, 1]; y[oe[:, 1]] = ib[:, 1]
        else:
            a = rng.permutation(k); b = k + rng.permutation(k)
            y[both(rng, a)] = both(rng, b); y[both(rng, b)] = both(rng, a)
def pack(x, t, nx, sh):
    return {"x0": np.ascontiguousarray(x.reshape(N, 128, V)).astype(np.int32), "th": np.ascontiguousarray(t.reshape(N, 128, 1)).astype(np.int32),
            "nxt": np.stack([gtable(a) for a in nx]), "shw": np.stack([gtable(a.reshape(8, -1)) for a in sh])}
def setup_inputs(rng):
    return pack(*parts(rng))
def setup_inputs_flat(rng):
    x, t, nx, sh = parts(rng)
    x[:, 0] = 255; x[:, 2] = rng.integers(0, 2, (N, 16, V)); x[:, 3] = 255 * rng.integers(0, 2, (N, 16, V))
    x[:, 4] = 255 * rng.integers(0, 2, (N, 1, V)); x[:, 5] = rng.integers(0, 4, (N, 1, V)); x[:, 6] = 64 * rng.integers(0, 4, (N, 16, V))
    v = np.array([0, 1, 2, 63, 64, 65, 127, 128, 129, 191, 192, 255, 256])
    t[:, ::2] = rng.choice(v, (N, 4, 16, 1)); t[:, 3] = rng.choice(v, (N, 16, 1)); t[:, 5] = rng.choice(np.array([0, 1, 2, 3]), (N, 16, 1))
    crowd(rng, 1, x, nx, sh, True); crowd(rng, 7, x, nx, sh, False)
    return pack(x, t, nx, sh)
def setup_inputs_loops(rng):
    x, t, nx, sh = parts(rng); p = np.arange(2 * W)
    for q in range(N):
        nx[q, 1] = p; nx[q, 2] = (p ^ 2) ^ np.repeat(rng.integers(0, 2, W), 2)
        nx[q, 3] = (p + 2) % (2 * W); nx[q, 5] = np.where(p & 1 == 0, (p + 2) % (2 * W), (p - 2) % (2 * W))
        i = np.flatnonzero(rng.random(2 * W) < 0.5); nx[q, 6] = p; nx[q, 6, i] = rng.permutation(i)
    chains(rng, 0, x, t, nx, sh); chains(rng, 4, x, t, nx, sh); swell(rng, 7, x, t, nx, sh)
    return pack(x, t, nx, sh)
def setup_inputs_ends(rng):
    x, t, nx, sh = parts(rng); k = 2 * (N - 1) * B
    for q in range(N):
        for g in range(8):
            if g % 2 == 0:
                s = np.concatenate([np.array([0, V - 1]), 1 + rng.permutation(V - 2)[:B - 2]])
                for d in range(N - 1): sh[q, g, d] = rng.permutation(s)
            else:
                sh[q, g] = V - 1 - np.arange((N - 1) * B).reshape(N - 1, B)
            if g in (0, 3, 4):
                o = rng.permutation(2 * V); nx[q, g, 2 * V:] = o[:k]
                nx[q, g, :2 * V] = rng.permutation(np.concatenate([o[k:], np.arange(2 * V, 2 * W)]))
            if g == 5:
                nx[q, g] = np.concatenate([rng.permutation(2 * V), 2 * V + rng.permutation(k)])
    return pack(x, t, nx, sh)
def setup_inputs_uneven(rng):
    x, t, nx, sh = parts(rng); q = rng.permutation(N)
    x[q[0]] = rng.integers(0, 4, (8, 16, V)); t[q[1]] = 4095; t[q[2]] = 0; x[q[3]] = 255 * rng.integers(0, 2, (8, 16, V))
    return pack(x, t, nx, sh)
def setup_inputs_spread(rng):
    x, t, nx, sh = parts(rng)
    x = np.minimum((np.exp2(8 * rng.random((N, 8, 1, V))) * rng.random((N, 8, 16, V))).astype(np.int64), 255)
    t = np.minimum(np.exp2(12 * rng.random((N, 8, 16, 1))).astype(np.int64) - 1, 4095)
    return pack(x, t, nx, sh)
def check_inputs(d):
    bad = []
    for k, lo, hi in (("x0", 0, 255), ("th", 0, 4095), ("nxt", 0, 2 * W - 1), ("shw", 0, V - 1)):
        if np.min(d[k]) < lo or np.max(d[k]) > hi: bad.append("range of " + k)
    if any(np.any(np.sort(gentries(a), axis=1) != np.arange(2 * W)) for a in d["nxt"]): bad.append("nxt holds each number once")
    s = np.sort(np.stack([gentries(a) for a in d["shw"]]).reshape(N, 8, N - 1, B), axis=3)
    if np.any(s[..., 1:] == s[..., :-1]): bad.append("different nodes in a block of shw")
    return bad
def reference(x0, th, nxt, shw):
    x = np.zeros((N, 8, 16, W), np.int32); x[..., :V] = x0.reshape(N, 8, 16, V); t = th.astype(np.int32).reshape(N, 8, 16, 1)
    nx = np.stack([gentries(a) for a in nxt]).astype(np.int64); pv = np.argsort(nx, axis=2)
    sh = np.stack([gentries(a) for a in shw]).astype(np.int64).reshape(N, 8, N - 1, B)
    border = np.zeros((N, 8, V), bool); np.put_along_axis(border, sh.reshape(N, 8, -1), True, 2)
    may = np.zeros((N, 8, W), bool); may[..., :V] = ~border
    inn = np.ones((N, 8, W), bool); port = np.arange(2 * W)
    def pick(a, ports):
        return np.take_along_axis(a, (ports >> 1)[:, :, None, :], 3)
    def sum4(a, n, p):
        b = pick(a, p) + pick(a, n); return b[..., 0::2] + b[..., 1::2]
    def size(u):
        return np.add.reduce(np.minimum(np.abs(u), 255), axis=2)
    def outward(a):
        for r in range(N):
            for d in range(1, N):
                q = (r - d) % N
                a[r, :, :, V + (d - 1) * B:V + d * B] = np.take_along_axis(a[q], sh[q, :, d - 1][:, None, :], 2)
    def home(s):
        o = s[..., :V].copy()
        for r in range(N):
            for d in range(1, N):
                q = (r - d) % N; ix = sh[q, :, d - 1][:, None, :]
                np.put_along_axis(o[q], ix, np.take_along_axis(o[q], ix, 2) + s[r, :, :, V + (d - 1) * B:V + d * B], 2)
        return o
    det = np.zeros((N, 8, 16, W), np.int32); kept = []
    for lev in range(L):
        outward(x)
        a = pick(x, pv); b = pick(x, nx); a0, a1, b0, b1 = a[..., 0::2], a[..., 1::2], b[..., 0::2], b[..., 1::2]
        d = x - ((a0 + a1 + b0 + b1) >> 2)
        key = size(d).astype(np.int64) * 4096 + np.arange(W)
        k = np.minimum(np.take_along_axis(key, pv >> 1, 2), np.take_along_axis(key, nx >> 1, 2))
        lv = may & (key < np.minimum(k[..., 0::2], k[..., 1::2]))
        c = size(a0 - b1) + size(a1 - b0) < size(a0 - b0) + size(a1 - b1)
        s = np.where(lv[:, :, None, :], d >> 2, 0).astype(np.int32)
        x[..., :V] += home(sum4(s, nx, pv)) * inn[:, :, None, :V]
        det = np.where(lv[:, :, None, :], d, det); kept.append((lv, nx, pv, inn))
        l2 = np.repeat(lv, 2, axis=2); other = port ^ np.repeat(c, 2, axis=2).astype(np.int64)
        fn = np.where(l2, np.take_along_axis(nx, other, 2), port); fp = np.where(l2, np.take_along_axis(pv, other, 2), port)
        nx = np.take_along_axis(fn, nx, 2); pv = np.take_along_axis(fp, pv, 2)
        may = may & ~lv; inn = inn & ~lv
    det = np.where(np.abs(det) < t, 0, det).astype(np.int32)
    for lv, n, p, was in kept[::-1]:
        s = np.where(lv[:, :, None, :], det >> 2, 0).astype(np.int32)
        x[..., :V] -= home(sum4(s, n, p)) * was[:, :, None, :V]
        outward(x)
        x = np.where(lv[:, :, None, :], det + (sum4(x, n, p) >> 2), x).astype(np.int32)
    return {"yx": np.ascontiguousarray(x[..., :V]).reshape(N, 128, V).astype(np.float32), "yn": nx.astype(np.float32)}

@@ -1,0 +1,715 @@
+from concourse.bass import DstId, RemoteDMATransfer
+from concourse.mybir import AluOpType as OP, ActivationFunctionType as AF
+
+V, B, W, P2 = 2048, 128, 2432, 4864
+GH = 384
+MG = 12582912.0
+KP = 4096.0
+BIG = 1048576.0
+
+TU = {"CY": 0.0009, "PCY": 0.0006, "WK": 0.1, "OV": 0.05, "GA": 1.4, "TT": 1.8, "VPEN": 0.6}
+SCRATCH = {}
+for _n, _c, _t in (
+        ("xa", W, "float32"), ("key", W, "float32"), ("dd", V, "float32"),
+        ("sp1", V, "float32"), ("sp2", V, "float32"), ("dl1", V, "float32"), ("dl2", V, "float32"),
+        ("ga", P2, "float16"), ("gb", P2, "float16"), ("fnx", P2, "bfloat16"), ("fpv", P2, "bfloat16"),
+        ("nxh", P2, "bfloat16"), ("pvh", P2, "bfloat16"), ("phl", P2, "bfloat16"), ("ghl", 768, "bfloat16"),
+        ("lv1", V, "bfloat16"), ("lv2", V, "bfloat16"), ("lv3", V, "bfloat16"), ("nm", V, "bfloat16"),
+        ("tk", V, "bfloat16"), ("un", 2052, "bfloat16"), ("wz", 144, "bfloat16"), ("wq", 144, "bfloat16"),
+        ("rz", 144, "bfloat16"), ("rn", 144, "bfloat16"),
+        ("idn", 128, "bfloat16"), ("neg", 128, "bfloat16"), ("ngq", 128, "bfloat16"), ("d25", 128, "bfloat16"),
+        ("blk", 128, "bfloat16"), ("blp", 128, "bfloat16"), ("bln", 128, "bfloat16"), ("sel", 128, "bfloat16"),
+        ("seq", 128, "bfloat16"), ("mgc", 128, "bfloat16"),
+        ("idh", 128, "float16"), ("neh", 128, "float16"), ("nqh", 128, "float16"),
+        ("qr", 128, "bfloat16"), ("swp", 128, "float32"), ("one", 512, "bfloat16"), ("hlf", 128, "float32"),
+        ("pm00", 128, "float32"), ("pm01", 128, "float32"), ("pm10", 128, "float32"), ("pm11", 128, "float32"),
+        ("x0i", 2380, "int32"), ("pci", 8, "int32"), ("col", 16, "float32"), ("th32", 8, "float32"), ("ls", 24, "uint16"),
+        ("pid", 304, "float32"), ("pih", 256, "float32"), ("nxf", 304, "float32"), ("pvf", 304, "float32"),
+        ("dnn", 256, "float32"), ("dnp", 256, "float32"), ("dpn", 256, "float32"), ("dpp", 256, "float32"),
+        ("lw", 256, "float32"), ("lc", 256, "float32"), ("w0", 256, "float32"), ("w1", 256, "float32"),
+        ("hn", 256, "bfloat16"), ("hp", 256, "bfloat16"), ("ln_", 256, "bfloat16"), ("lp_", 256, "bfloat16"),
+        ("lpn", 304, "uint16"), ("lpp", 304, "uint16"),
+        ("ss", 768, "float32"), ("rs1", 768, "float32"), ("rs2", 768, "float32"),
+        ("bs", 3 * GH, "float32"), ("rb1", GH, "float32"), ("rb2", GH, "float32"),
+        ("sg1", GH, "float32"), ("sg2", GH, "float32"), ("bt", 128, "float32")):
+    SCRATCH[_n] = ("sbuf", [128, _c], _t)
+RINGS = {"f": (6, "float32"), "q": (4, "float32"), "t": (6, "bfloat16"), "m": (2, "bfloat16")}
+for _r in RINGS:
+    for _k in range(RINGS[_r][0]):
+        SCRATCH["%s%d" % (_r, _k)] = ("sbuf", [128, 512], RINGS[_r][1])
+for _k in range(8):
+    SCRATCH["p%d" % _k] = ("psum", [128, 512], "float32")
+for _k in (1, 2, 3):
+    SCRATCH["l%dn" % _k] = ("sbuf", [128, 304], "uint16")
+    SCRATCH["l%dp" % _k] = ("sbuf", [128, 304], "uint16")
+ARR = [a + str(d) for a in ("ax1_", "ax2_", "ax3_", "as1_", "as2_", "as3_", "ab3_", "ab2_") for d in (1, 2, 3)]
+SEMAPHORES = ["sv", "ss_", "st", "sg", "loc"] + ARR + ["d%d" % k for k in range(20)]
+PSUMS = ["p%d" % k for k in range(8)]
+
+
+def R(name, a, b, s=1):
+    return (name, a, b, s)
+
+
+def IND(win, off):
+    return ("ind", win, off)
+
+
+def hits(x, y):
+    if x[0] >= y[1] or y[0] >= x[1]:
+        return False
+    return not (x[2] == y[2] and x[2] > 1 and (x[0] - y[0]) % x[2])
+
+
+def ordered(prog):
+    n, WK = len(prog), TU["WK"]
+    preds, succs = [set() for _ in range(n)], [set() for _ in range(n)]
+    acc = {}
+    for i, (var, ro, ri, lat, up) in enumerate(prog):
+        e = var[0][0] if len(var) == 1 else None
+        for lst, wr in ((ro, True), (ri, False)):
+            for (nm, a, b, s) in lst:
+                ps = nm in PSUMS
+                for (j, e2, a2, b2, s2, w2) in acc.get(nm, ()):
+                    if j != i and ((ps and (e is None or e != e2)) or ((wr or w2) and hits((a, b, s), (a2, b2, s2)))):
+                        preds[i].add(j)
+        for lst, wr in ((ro, True), (ri, False)):
+            for (nm, a, b, s) in lst:
+                old = acc.get(nm, [])
+                if wr and s == 1:
+                    old = [o for o in old if not (o[2] >= a and o[3] <= b and
+                                                  (nm not in PSUMS or (e is not None and o[1] == e)))]
+                acc[nm] = old + [(i, e, a, b, s, wr)]
+    for i in range(n):
+        for j in preds[i]:
+            succs[j].add(i)
+    dur = [min(v[1] for v in p[0]) + (p[3] or 0.0) for p in prog]
+    tail = [0.0] * n
+    for i in range(n - 1, -1, -1):
+        tail[i] = prog[i][4] + dur[i] + max([tail[j] + WK for j in succs[i]] or [0.0])
+    left = [len(p) for p in preds]
+    ready = {i: 0.0 for i in range(n) if not left[i]}
+    free, out, when = {}, [], [0.0] * n
+
+    def start(i, r):
+        return min(max(r, free.get(v[0], 0.0)) for v in prog[i][0])
+    while ready:
+        t = min(start(i, r) for i, r in ready.items())
+        best = None
+        for i, r in ready.items():
+            if start(i, r) <= t + 0.02 and (best is None or (tail[i], -i) > (tail[best], -best)):
+                best = i
+        i = best
+        r = ready.pop(i)
+        var = min(prog[i][0], key=lambda v: max(r, free.get(v[0], 0.0)) + v[1] + (TU["VPEN"] if v[0] == "v" else 0.0))
+        t = max(r, free.get(var[0], 0.0))
+        if var[0] != "a":
+            free[var[0]] = t + var[1]
+        out.append(var[2])
+        for j in succs[i]:
+            when[j] = max(when[j], t + var[1] + (prog[i][3] or 0.0) + WK)
+            left[j] -= 1
+            if not left[j]:
+                ready[j] = when[j]
+    return out
+
+
+def rank_program(g, core, T, topo):
+    rank = T.rank_of(core)
+    if rank is None:
+        return
+    N = len(T.cores)
+    CY, PCY, GA = TU["CY"], TU["PCY"], TU["GA"]
+    queues = {"v": g.vector, "s": g.scalar, "t": g.tensor, "g": g, "y": g.sync}
+    semof = {"v": "sv", "s": "ss_", "t": "st", "g": "sg"}
+    tick = {"v": 0, "s": 0, "t": 0, "g": 0}
+    known = {e: {} for e in queues}
+    snaps = {}
+    acc = {}
+    prog = []
+    ndma, local, arrived = [0], [0], {}
+    first = [0.0]
+
+    def ap(v):
+        if v[0] == "ind":
+            return T[v[1][0]][:, v[1][1]:v[1][2]].indirect(T[v[2][0]][:, v[2][1]:v[2][2]])
+        n, a, b, s = v
+        return T[n][:, a:b] if s == 1 else T[n][:, a:b:s]
+
+    def need(e, outs, ins):
+        w = {}
+        for lst, wr in ((outs, True), (ins, False)):
+            for (n, a, b, s) in lst:
+                for (src, cnt, a2, b2, s2, wr2) in acc.get(n, []):
+                    if (src == e or n not in PSUMS) and (not (wr or wr2) or not hits((a, b, s), (a2, b2, s2))):
+                        continue
+                    w[src] = max(w.get(src, 0), cnt)
+        k = known[e]
+        w = {s: c for s, c in w.items() if k.get(s, 0) < c}
+        for s, c in list(w.items()):
+            if any(s2 != s and snaps[(s2, c2)].get(s, 0) >= c for s2, c2 in w.items()):
+                w.pop(s)
+        for s, c in w.items():
+            queues[e].wait_ge(T.sem[semof.get(s, s)], c)
+            for s2, c2 in [(s, c)] + list(snaps[(s, c)].items()):
+                k[s2] = max(k.get(s2, 0), c2)
+
+    def note(e, src, cnt, outs, ins):
+        snaps[(src, cnt)] = dict(known[e]) if e else {}
+        for lst, wr in ((outs, True), (ins, False)):
+            for (n, a, b, s) in lst:
+                old = acc.get(n, [])
+                if wr and s == 1:
+                    old = [o for o in old if not (o[2] >= a and o[3] <= b and (n not in PSUMS or o[0] == src))]
+                else:
+                    old = [o for o in old if not (o[0] == src and o[2:] == (a, b, s, wr))]
+                acc[n] = old + [(src, cnt, a, b, s, wr)]
+
+    def op(outs, ins, *variants):
+        ro = [v[1] if v[0] == "ind" else v for v in outs]
+        ri = [v[2] for v in outs if v[0] == "ind"]
+        for v in ins:
+            ri += [v[1], v[2]] if v[0] == "ind" else [v]
+
+        def emitter(e, calls):
+            def emit():
+                need(e, ro, ri)
+                for c in calls[:-1]:
+                    c()
+                tick[e] += 1
+                calls[-1]().then_inc(T.sem[semof[e]], 1)
+                note(e, e, tick[e], ro, ri)
+            return emit
+        prog.append(([(e, cost + TU["OV"], emitter(e, calls)) for e, calls, cost in variants], ro, ri, None, first[0]))
+
+    def num(v):
+        return 16 * (v[2][2] - v[2][1]) if v[0] == "ind" else (v[2] - v[1] + v[3] - 1) // v[3]
+
+    def tm(n, *vs):
+        two = all(SCRATCH[v[0]][2] in ("bfloat16", "float16") for v in vs)
+        return CY * max(64, n * (0.5 if two else 1))
+
+    def vcopy(o, i):
+        n = num(i)
+        op([o], [i], ("v", [lambda: g.vector.tensor_copy(ap(o), ap(i))],
+                      3.8 * CY * n if o[0] == "ind" else GA * CY * n if i[0] == "ind" else tm(n, o, i)))
+
+    def vtt(o, a, b, f):
+        op([o], [a, b], ("v", [lambda: g.vector.tensor_tensor(ap(o), ap(a), ap(b), f)],
+                         CY * max(64, num(b) * (1 if a[0] in PSUMS or b[0] in PSUMS else TU["TT"] if a[0] == "ind" else 2))))
+
+    def vts(o, a, s1, f1, s2=None, f2=None):
+        x1 = ap(s1) if isinstance(s1, tuple) else s1
+        cols = [s1] if isinstance(s1, tuple) else []
+        if f2 is None:
+            op([o], [a] + cols, ("v", [lambda: g.vector.tensor_scalar(ap(o), ap(a), x1, None, f1)], tm(num(a), o, a)))
+        else:
+            op([o], [a] + cols, ("v", [lambda: g.vector.tensor_scalar(ap(o), ap(a), x1, s2, f1, f2)], tm(num(a), o, a)))
+
+    def vset(o, c):
+        op([o], [], ("v", [lambda: g.vector.memset(ap(o), c)], tm(num(o))))
+
+    def sact(o, i, f=AF.Copy, bias=0.0, scale=1.0):
+        n = num(i)
+        col = isinstance(bias, tuple)
+        bb = ap(bias) if col else bias
+        op([o], [i] + ([bias] if col else []),
+           ("s", [lambda: g.scalar.activation(ap(o), ap(i), f, bias=bb, scale=scale)],
+            CY * (GA * n if i[0] == "ind" else max(64, n)) + 0.01))
+
+    def lin(o, i, scale=1.0, bias=0.0, relu=False):
+        n = num(i)
+        ind = i[0] == "ind"
+        sv = ("s", [lambda: g.scalar.activation(ap(o), ap(i), AF.Relu if relu else AF.Identity, bias=bias, scale=scale)],
+              CY * (GA * n if ind else max(64, n)) + 0.01)
+        tv = CY * GA * n if ind else tm(n, o, i)
+        if relu:
+            vv = ("v", [lambda: g.vector.tensor_scalar(ap(o), ap(i), 0.0, None, OP.max)], tv)
+        elif scale == 1.0 and bias == 0.0:
+            vv = ("v", [lambda: g.vector.tensor_copy(ap(o), ap(i))], tv)
+        elif scale == 1.0:
+            vv = ("v", [lambda: g.vector.tensor_scalar(ap(o), ap(i), bias, None, OP.add)], tv)
+        else:
+            vv = ("v", [lambda: g.vector.tensor_scalar(ap(o), ap(i), scale, bias, OP.mult, OP.add)], tv)
+        op([o], [i], sv, vv)
+
+    def mm(o, terms, start=True, stop=True):
+        n = len(terms)
+        op([o], [x for t in terms for x in t],
+           ("t", [lambda k=k: g.tensor.matmul(ap(o), ap(terms[k][0]), ap(terms[k][1]), start and k == 0,
+                                              stop and k == n - 1) for k in range(n)],
+            sum(max(64, num(t[1])) * (4 if SCRATCH[t[0][0]][2] == "float32" else 1) + 25 for t in terms) * PCY))
+
+    def asel(o, i, pat, cmp, base, cm):
+        op([o], [i], ("g", [lambda: g.affine_select(ap(o), ap(i), pat, cmp, 0.0, base, cm)], 0.17 + 2 * CY * num(o)))
+
+    def iota(o, pat, base, cm):
+        if SCRATCH[o[0]][2] == "int32":
+            op([o], [], ("g", [lambda: g.iota(ap(o), pat, base, cm)], 0.13 + 2 * CY * num(o)))
+        else:
+            op([o], [], ("g", [lambda: g.iota(ap(o), pat, base, cm, allow_small_or_imprecise_dtypes=True)],
+                         0.13 + 2 * CY * num(o)))
+
+    def dma(o_ap, i_ap, outs, ins):
+        def emit():
+            need("y", outs, ins)
+            s = "d%d" % ndma[0]
+            ndma[0] += 1
+            g.sync.dma_start(o_ap, i_ap).then_inc(T.sem[s], 16)
+            note("y", s, 16, outs, ins)
+        prog.append(([("y", 0.1, emit)], outs, ins, 2.5, first[0]))
+
+    peers = {d: T.cores[(rank + d) % N] for d in (1, 2, 3)}
+    homes = {d: T.cores[(rank - d) % N] for d in (1, 2, 3)}
+
+    def split(src, dsts):
+        away = [c for c in dsts if topo.chip(c) != topo.chip(src)]
+        pool = topo.engines(src, away[0])
+        n = len(pool) // len(away)
+        res = {c: pool[k * n:(k + 1) * n] for k, c in enumerate(away)}
+        for c in dsts:
+            if c not in res:
+                res[c] = [e for e in topo.engines(src, c) if e not in pool]
+        return res
+
+    def send(to, pieces, sems, ins, guard=()):
+        m = split(core, [to[d] for d in (1, 2, 3)])
+        tr = []
+        for d in (1, 2, 3):
+            rid, pid, _ = topo.addr(to[d])
+            n = len(m[to[d]]) // len(pieces)
+            for k, (sn, sc, dn, dc) in enumerate(pieces):
+                c = (d - 1) * B
+                tr.append(RemoteDMATransfer(
+                    dst_ids=[DstId(rid=rid, pnc=pid)], dma_engine_mask=sum(1 << e for e in m[to[d]][k * n:(k + 1) * n]),
+                    remote_sem=T.sem[sems + str(d)], src=T[sn][:, sc + c:sc + c + B], dst=T[dn][:, dc + c:dc + c + B]))
+                local[0] += n
+        guard = list(guard)
+
+        def emit():
+            need("g", guard, ins)
+            g.remote_dma_fused(tr, local_sem=T.sem["loc"])
+        prog.append(([("g", 1.0, emit)], guard + [("sent" + sems, 0, 1, 1)], ins, None, first[0]))
+
+    def recv(sems, frm, pieces):
+        for d in (1, 2, 3):
+            r = T.rank_of(frm[d])
+            s = 1 if frm is homes else -1
+            n = len(split(frm[d], [T.cores[(r + s * j) % N] for j in (1, 2, 3)])[core]) // len(pieces) * len(pieces)
+            c = (d - 1) * B
+            ro = [R(nm, cc + c, cc + c + B) for nm, cc in pieces]
+            arrived[sems + str(d)] = n
+            prog.append(([("a", 0.0, lambda d=d, n=n, ro=ro: note(None, sems + str(d), n, ro, []))],
+                         ro, [("sent" + sems, 0, 1, 1)], 5.0, 0.0))
+
+    turn = {r: 0 for r in RINGS}
+    pools = {"a": [0, 1, 2], "c": [0, 1, 2, 4, 5, 6, 7], "z": [0, 1, 2, 3, 4, 5, 6, 7]}
+    pool, pr = ["c"], [0]
+
+    def ring(c):
+        turn[c] = (turn[c] + 1) % RINGS[c][0]
+        return "%s%d" % (c, turn[c])
+
+    def F(n=512):
+        return R(ring("f"), 0, n)
+
+    def PB():
+        pr[0] += 1
+        return "p%d" % pools[pool[0]][pr[0] % len(pools[pool[0]])]
+
+    def PQ(n=512):
+        return R(PB(), 0, n)
+
+    CH = [(512 * k, 512 * k + 512) for k in range(4)] + [(V, W)]
+    LSB = {d: R("ls", 8 * (d - 1), 8 * d) for d in (1, 2, 3)}
+    LSA = R("ls", 0, 24)
+    THR = R("th32", 0, 1)
+    XA, KEY = R("xa", 0, W), R("key", 0, W)
+    ONE = R("one", 0, 512)
+
+    def M(name):
+        return R(name, 0, 128)
+
+    def shifted(name, k):
+        return R(name, 16 - k, 144 - k)
+
+    def lists(wf, ln):
+        pb = PQ(304)
+        for h in (0, 1):
+            mm(R(pb[0], 152 * h, 152 * h + 152), [(M("pm%d%d" % (h, c)), R(wf, c, 304, 2)) for c in (0, 1)])
+        vts(R(ln, 0, 304), pb, MG, OP.add, -MG, OP.add)
+
+    def wrap(flat, wf, lp, ln, rows="wz"):
+        pb = PQ(304)
+        mm(pb, [(shifted(rows, i), R(flat, i, P2, 16)) for i in range(16)])
+        sact(R(wf, 0, 304), pb, AF.Identity, bias=-0.5)
+        vcopy(R(lp, 0, 304), pb)
+        lists(wf, ln)
+
+    def partners(wf, dn, dp):
+        pb = PQ(256)
+        mm(pb, [(M("swp"), R(wf, 0, 256))])
+        vtt(R(dn, 0, 256), pb, R(wf, 0, 256), OP.subtract)
+        vtt(R(dp, 0, 256), R(wf, 0, 256), R("pih", 0, 256), OP.subtract)
+
+    def lst(l, c, h, k):
+        return R("l%d%s" % (l, c), 152 * h + CH[k][0] // 16, 152 * h + CH[k][1] // 16)
+
+    def pc(n, h, k):
+        a, b = CH[k]
+        o = V * h if k < 4 else V + GH * h
+        return R(n, o + a, o + b)
+
+    def chain(l, k, win, f, q, bias=0.0):
+        lin(q, IND(win, lst(l, "n", 0, k)), bias=bias)
+        for c, h in (("n", 1), ("p", 0), ("p", 1)):
+            vtt(q, IND(win, lst(l, c, h, k)), q, f)
+
+    for k in range(2):
+        dma(T.x0i[:, 1024 * k:1024 * k + 1024], T.x0[:, 1024 * k:1024 * k + 1024], [R("x0i", 1024 * k, 1024 * k + 1024)], [])
+    dma(T.x0i[:, 2352:2376], T.shw[:], [R("x0i", 2352, 2376)], [])
+    dma(T.x0i[:, 2048:2352], T.nxt[:], [R("x0i", 2048, 2352)], [])
+    dma(T.x0i[:, 2376:2377], T.th[:], [R("x0i", 2376, 2377)], [])
+    iota(R("pci", 0, 1), [[0, 1]], 0, 1)
+    iota(R("t0", 0, 512), [[64, 8], [0, 64]], 0, 0)
+    iota(R("t1", 0, 512), [[0, 8], [1, 64]], 0, 0)
+    vset(ONE, 1.0)
+    for n in ("blk", "sel", "seq"):
+        vset(M(n), 1.0)
+    vset(M("hlf"), 0.5)
+    vset(R("un", 0, 2052), 0.0)
+    for n in ("wz", "wq", "rz", "rn"):
+        vset(R(n, 0, 144), 0.0)
+    for n, lo, hi in (("sel", 0, 1), ("seq", 2, 3), ("blk", 0, 15)):
+        asel(M(n), M(n), [[-16, 8], [0, 16]], OP.is_ge, -lo, 1)
+        asel(M(n), M(n), [[16, 8], [0, 16]], OP.is_ge, hi, -1)
+    asel(M("idn"), R("one", 0, 128), [[-1, 128]], OP.is_equal, 0, 1)
+    for h in (0, 1):
+        for c in (0, 1):
+            asel(M("pm%d%d" % (h, c)), M("hlf"), [[-16, 8], [1000, 2], [-2, 8]], OP.is_equal, -h - 1000 * c, 1)
+    vts(R("pci", 1, 2), R("pci", 0, 1), 1, OP.bitwise_and)
+    vts(R("pci", 2, 3), R("pci", 0, 1), 15, OP.bitwise_and)
+    vcopy(R("col", 0, 1), R("pci", 1, 2))
+    vts(R("col", 1, 2), R("col", 0, 1), -1.0, OP.mult, 1.0, OP.add)
+    vcopy(R("col", 2, 3), R("pci", 2, 3))
+    for b in range(1, 10):
+        vts(R("col", 2 + b, 3 + b), R("col", 1, 2), 512.0 * b, OP.mult)
+    vts(R("t2", 0, 512), R("t0", 0, 512), R("col", 1, 2), OP.mult)
+    vts(R("t3", 0, 512), R("t1", 0, 512), R("col", 0, 1), OP.mult)
+    vtt(R("phl", 0, 512), R("t2", 0, 512), R("t3", 0, 512), OP.add)
+    first[0] = 100.0
+    vcopy(R("ls", 0, 24), R("x0i", 2352, 2376))
+    for k in range(2):
+        vcopy(R("xa", 1024 * k, 1024 * k + 1024), R("x0i", 1024 * k, 1024 * k + 1024))
+    sact(R("bs", 0, GH), IND(R("xa", 0, V), LSA))
+    send(peers, [("bs", 0, "xa", V)], "ax1_", [R("bs", 0, GH)])
+    recv("ax1_", homes, [("xa", V)])
+    first[0] = 0.0
+    vcopy(R("nxf", 0, 304), R("x0i", 2048, 2352))
+    vts(R("nxf", 0, 304), R("nxf", 0, 304), -0.5, OP.add)
+    vcopy(R("lpn", 0, 304), R("x0i", 2048, 2352))
+    for b in range(1, 10):
+        n = min(512, P2 - 512 * b)
+        sact(R("phl", 512 * b, 512 * b + n), R("phl", 0, n), AF.Identity, bias=R("col", 2 + b, 3 + b))
+    lists("nxf", "l1n")
+    vcopy(IND(R("pvh", 0, P2), R("lpn", 0, 256)), R("phl", 0, 4096))
+    vcopy(IND(R("pvh", 0, P2), R("lpn", 256, 304)), R("phl", 4096, P2))
+    vset(M("swp"), 1.0)
+    vset(M("qr"), 3.0 / 1024.0)
+    vset(M("mgc"), MG / 128.0)
+    vset(R("nm", 0, V), 0.0)
+    for d in (1, 2, 3):
+        vcopy(IND(R("nm", 0, V), LSB[d]), R("one", 0, 128))
+    vcopy(THR, R("x0i", 2376, 2377))
+    for n, i, c in (("neg", "idn", -1.0), ("ngq", "idn", -0.25), ("d25", "idn", 33554432.0), ("blp", "blk", 4096.0),
+                    ("bln", "blk", -4096.0)):
+        sact(M(n), M(i), scale=c)
+    sact(R("ghl", 0, 768), R("phl", 4096, P2))
+    sact(R("wz", 16, 144, 16), R("sel", 0, 128, 16))
+    sact(R("wq", 16, 144, 16), R("seq", 0, 128, 16))
+    for h in (0, 1):
+        sact(R("rz", 16 + h, 144, 16), R("blk", h, 128, 16))
+        sact(R("rn", 16 + h, 144, 16), R("blk", h, 128, 16), scale=-1.0)
+    asel(R("un", 4, 2052, 4), ONE, [[-1, 16], [-16, 8], [0, 4]], OP.is_equal, 0, 1)
+    asel(R("swp", 0, 128, 2), R("swp", 0, 128, 2), [[-2, 64]], OP.is_equal, -1, 1)
+    asel(R("swp", 1, 128, 2), R("swp", 1, 128, 2), [[-2, 64]], OP.is_equal, 0, 1)
+    iota(R("pid", 0, 304), [[16, 304]], 0, 0)
+    vts(R("pid", 0, 304), R("pid", 0, 304), R("col", 2, 3), OP.add)
+    vts(R("pih", 0, 256), R("pid", 0, 256), -0.5, OP.add)
+    vcopy(M("idh"), M("idn"))
+    vcopy(M("neh"), M("neg"))
+    vcopy(M("nqh"), M("ngq"))
+
+    for k in range(5):
+        for h in (0, 1):
+            lin(pc("fnx", h, k), IND(XA, lst(1, "n", h, k)))
+    wrap("pvh", "pvf", "lpp", "l1p")
+    partners("nxf", "dnn", "dpn")
+    partners("pvf", "dnp", "dpp")
+
+    for l in (1, 2, 3):
+        LVn = "lv%d" % l
+        srcs = {1: [("fpv", "fnx")], 2: [("ga", "gb")], 3: [("fpv", "fnx"), ("pvh", "nxh")]}[l]
+        I1, NI, NQ = [M(x) for x in (("idh", "neh", "nqh") if l == 2 else ("idn", "neg", "ngq"))]
+        pool[0] = "a"
+        zb, tk = {}, {}
+
+        def gathers(k):
+            a, b = CH[k]
+            n = b - a
+            fp, fn = srcs[0]
+            if l > 1:
+                for h in (0, 1):
+                    lin(pc(fn, h, k), IND(XA, lst(l, "n", h, k)))
+            for h in (0, 1):
+                lin(pc(fp, h, k), IND(XA, lst(l, "p", h, k)))
+            if l == 3:
+                for s, c in (("nxh", "n"), ("pvh", "p")):
+                    for h in (0, 1):
+                        lin(pc(s, h, k), IND(R("phl", W, P2), lst(l, c, h, k)), bias=-0.375)
+            zb[k] = R("p%d" % (4 + k), 0, 512) if k < 4 else PQ(n)
+            one = R("one", 0, n)
+            mm(zb[k], [(NQ, pc(p[1], h, k)) for p in srcs for h in (0, 1)] + ([(M("qr"), one)] if l < 3 else []), stop=False)
+            mm(zb[k], [(NQ, pc(p[0], h, k)) for p in srcs for h in (0, 1)] + [(M("mgc"), one)], start=False)
+            xm = F(n)
+            lin(xm, R("xa", a, b), bias=-MG)
+            vtt(zb[k], zb[k], xm, OP.add)
+
+        def sized(k):
+            return [(M("sel"), R("phl", CH[k][0], CH[k][1])), (M("blp" if l == 1 else "bln"), tk[k])]
+
+        def detail(k):
+            a, b = CH[k]
+            n, d = b - a, zb[k]
+            t = e = tk[k] = R("tk", a, b) if k < 4 else R(ring("t"), 0, n)
+            if l == 1:
+                sact(t, d, AF.Abs)
+            else:
+                e = F(n)
+                sact(e, d, AF.Abs)
+                sact(t, e, AF.Relu, bias=255.0, scale=-1.0)
+            o = PQ(n)
+            mm(o, sized(k))
+            lin(R("key", a, b), o)
+            if k == 4:
+                return
+            m, w, q, ds = R(ring("m"), 0, 512), F(), F(), PQ()
+            vts(m, e, THR, OP.is_ge)
+            if l < 3:
+                lin(w, m, bias=KP)
+            else:
+                lin(w, m, -1.0, 1.0)
+            lin(q, d, 0.25, -0.375)
+            vtt(R("dd", a, b), d, m, OP.mult)
+            vts(ds, q, MG, OP.add, -MG, OP.add)
+            vtt(d, ds, w, OP.mult)
+
+        def chosen(k):
+            a, b = CH[k]
+            f = R(ring("q"), 0, 512)
+            chain(l, k, KEY, OP.min, f)
+            o = PQ()
+            mm(o, [(M("d25"), R(x, a, b)) for x in ["nm"] + ["lv%d" % j for j in range(1, l)]] + sized(k))
+            vtt(R(LVn, a, b), o, f, OP.is_lt)
+
+        def likeness(k):
+            terms = []
+            for x, y in ((0, 0), (1, 1), (0, 1), (1, 0)):
+                u = PQ()
+                mm(u, [(I1, pc(s[0], x, k)) for s in srcs] + [(NI, pc(s[1], y, k)) for s in srcs])
+                tn = ring("t")
+                if l == 1:
+                    lin(R(tn, 0, 512), u, relu=True)
+                else:
+                    sact(R(tn, 0, 512), u, AF.Abs)
+                    sact(R(tn, 0, 512), R(tn, 0, 512), AF.Relu, bias=255.0, scale=-1.0)
+                sg = "rz" if (x == y) == (l == 1) else "rn"
+                terms += [(shifted(sg, 2 * i), R(tn, i, 512, 8)) for i in range(8)]
+            mm(R("p3", 64 * k, 64 * k + 64), terms)
+
+        def links_small():
+            lb = PB()
+            for k in range(4):
+                a, b = CH[k]
+                mm(R(lb, 64 * k, 64 * k + 64), [(shifted("rz", 2 * i), R(LVn, a + i, b, 8)) for i in range(8)])
+            lin(R("lw", 0, 256), R(lb, 0, 256), 1.0 / 16)
+            vts(R("lc", 0, 256), R("p3", 0, 256), 0.0, OP.is_gt)
+            vtt(R("lc", 0, 256), R("lc", 0, 256), R("lw", 0, 256), OP.mult)
+            for (dn, dp, h, lo) in (("dnn", "dpn", "hn", "ln_"), ("dnp", "dpp", "hp", "lp_"))[:2 if l < 3 else 1]:
+                vtt(R("w0", 0, 256), R("lc", 0, 256), R(dn, 0, 256), OP.mult)
+                vtt(R("w1", 0, 256), R("lw", 0, 256), R(dp, 0, 256), OP.mult)
+                vtt(R("w0", 0, 256), R("w0", 0, 256), R("w1", 0, 256), OP.add)
+                vtt(R("w0", 0, 256), R("w0", 0, 256), R("pid", 0, 256), OP.add)
+                lin(R(h, 0, 256), R("w0", 0, 256))
+                vtt(R(lo, 0, 256), R("w0", 0, 256), R(h, 0, 256), OP.subtract)
+
+        def unwrap():
+            if l != 2:
+                lin(R("fnx", 4096, P2), R("ghl", 0, 768))
+            for i in range(16):
+                if i % 2 == 0:
+                    bn = PB()
+                bk = R(bn, 256 * (i % 2), 256 * (i % 2) + 256)
+                mm(bk, [(R("un", 4 + 128 * i - r, 132 + 128 * i - r), R(x, 0, 256))
+                        for r, x in enumerate(("hn", "ln_", "hp", "lp_")[:4 if l < 3 else 2])])
+                lin(R("fnx", i, 4096, 16), bk)
+
+        def own(k):
+            a, b = CH[k]
+            x, b1, b2 = R("xa", a, b), PQ(), PQ()
+            if l < 3:
+                s = R("sp%d" % l, a, b)
+                chain(l, k, KEY, OP.add, s)
+                z = F()
+                lin(z, s, bias=MG * KP)
+                lin(b1, z, 1.0 / KP, -MG)
+                lin(b2, z, bias=-MG * KP)
+                vtt(x, b1, x, OP.add)
+                vtt(s, s, b2, OP.subtract)
+            else:
+                q = R(ring("q"), 0, 512)
+                lin(b2, R(LVn, a, b), -BIG)
+                vtt(x, b2, x, OP.add)
+                chain(l, k, KEY, OP.add, q)
+                vtt(x, q, x, OP.add)
+
+        def border(buf, rc):
+            for d in (1, 2, 3):
+                c = rc + (d - 1) * B
+                vtt(R("bt", 0, 128), IND(R(buf, 0, V), LSB[d]), R(rs, c, c + B), OP.add)
+                vcopy(IND(R(buf, 0, V), LSB[d]), R("bt", 0, 128))
+
+        def kept(k):
+            a, b = CH[k]
+            b2 = PQ()
+            lin(b2, R(LVn, a, b), BIG, -(BIG + MG))
+            vtt(R("dd" if l == 3 else "dl%d" % l, a, b), b2, R("dd", a, b), OP.add)
+            if l < 3:
+                b1, s = PQ(), R("sp%d" % l, a, b)
+                lin(b1, R(LVn, a, b), BIG)
+                vtt(s, b1, s, OP.add)
+
+        if l == 3:
+            for k in range(5):
+                a, b = CH[k]
+                t = R(ring("t"), 0, b - a)
+                lin(t, R("xa", a, b))
+                vtt(R("phl", W + a, W + b), R("xa", a, b), t, OP.subtract)
+        order = [4, 0, 1, 2, 3] if l > 1 else [0, 1, 2, 3, 4]
+        for i in range(6):
+            if i < 5:
+                gathers(order[i])
+            if i > 0:
+                detail(order[i - 1])
+        for k in range(4):
+            chosen(k)
+            if k < (4 if l < 3 else 2):
+                likeness(k)
+        vset(R("key", V, W), 0.0)
+        for k in range(4):
+            a, b = CH[k]
+            vtt(R("key", a, b), zb[k], R(LVn, a, b), OP.mult)
+        pool[0] = "c"
+        rs = "rs2" if l == 2 else "rs1"
+        xg = [R("xa", V, W)]
+        if l < 3:
+            q, z, b4 = F(GH), F(GH), PQ(GH)
+            chain(l, 4, KEY, OP.add, q)
+            lin(z, q, bias=MG * KP)
+            lin(b4, z, bias=-MG * KP)
+            lin(R("ss", 0, GH), z, 1.0 / KP, -MG)
+            vtt(R("ss", GH, 768), q, b4, OP.subtract)
+            send(homes, [("ss", 0, rs, 0), ("ss", GH, rs, GH)], "as%d_" % l, [R("ss", 0, 768)], xg)
+            recv("as%d_" % l, peers, [(rs, 0), (rs, GH)])
+            links_small()
+            own(0)
+            own(1)
+            unwrap()
+            own(2)
+            own(3)
+            border("xa", 0)
+            sact(R("bs", 0, GH), IND(R("xa", 0, V), LSA))
+            send(peers, [("bs", 0, "xa", V)], "ax%d_" % (l + 1), [R("bs", 0, GH)], [R("rs1", 0, 768)] if l == 2 else [])
+            recv("ax%d_" % (l + 1), homes, [("xa", V)])
+            for (o, lp) in (("nxh", "lpn"), ("pvh", "lpp")):
+                for k in range(4):
+                    lin(R(o, 1216 * k, 1216 * k + 1216), IND(R("fnx", 0, P2), R(lp, 76 * k, 76 * k + 76)))
+            wrap("nxh", "nxf", "lpn", "l%dn" % (l + 1))
+            border("sp%d" % l, GH)
+            sact(R("sg%d" % l, 0, GH), IND(R("sp%d" % l, 0, V), LSA))
+            for k in range(4):
+                kept(k)
+            wrap("pvh", "pvf", "lpp", "l%dp" % (l + 1), "wq")
+            partners("nxf", "dnn", "dpn")
+            if l < 2:
+                partners("pvf", "dnp", "dpp")
+        else:
+            chain(l, 4, KEY, OP.add, R("ss", 0, GH))
+            send(homes, [("ss", 0, rs, 0)], "as3_", [R("ss", 0, GH)], xg)
+            recv("as3_", peers, [(rs, 0)])
+            for k in range(4):
+                own(k)
+            border("xa", 0)
+            sact(R("bs", 0, GH), IND(R("xa", 0, V), LSA))
+            vtt(R("bs", GH, 2 * GH), R("bs", 0, GH), R("sg2", 0, GH), OP.subtract)
+            vtt(R("bs", 2 * GH, 3 * GH), R("bs", GH, 2 * GH), R("sg1", 0, GH), OP.subtract)
+            send(peers, [("bs", 0, "xa", V)], "ab3_", [R("bs", 0, GH)])
+            send(peers, [("bs", GH, "rb2", 0), ("bs", 2 * GH, "rb1", 0)], "ab2_", [R("bs", GH, 3 * GH)])
+            recv("ab3_", homes, [("xa", V)])
+            recv("ab2_", homes, [("rb2", 0), ("rb1", 0)])
+            for k in range(4):
+                kept(k)
+            sact(R("key", V, W), R("rb2", 0, GH))
+            likeness(2)
+            likeness(3)
+            links_small()
+            unwrap()
+
+    pool[0] = "z"
+
+    def undo(l, src, dst, dl, sp):
+        fms = {}
+        for k in range(5):
+            if k < 4:
+                z, fms[k] = R(ring("q"), 0, 512), PQ()
+                chain(l, k, R(src, 0, W), OP.add, z, -1.5)
+                lin(fms[k], z, 0.25, MG)
+            if k > 0:
+                a, b = CH[k - 1]
+                y, mx = PQ(), PQ()
+                vtt(y, fms[k - 1], R(dl, a, b), OP.add)
+                if sp is None:
+                    vtt(R(dst, a, b), y, R(src, a, b), OP.max)
+                    dma(T.yx[:, a:b], T[dst][:, a:b], [], [R(dst, a, b)])
+                else:
+                    vtt(mx, y, R(src, a, b), OP.max)
+                    vtt(R(dst, a, b), mx, R(sp, a, b), OP.subtract)
+
+    undo(3, "xa", "key", "dd", "sp2")
+    sact(R("xa", V, W), R("rb1", 0, GH))
+    for k in range(4):
+        lin(R("nxh", 1216 * k, 1216 * k + 1216), IND(R("fnx", 0, P2), R("lpn", 76 * k, 76 * k + 76)))
+    undo(2, "key", "xa", "dl2", "sp1")
+    for k in range(10):
+        a, b = 512 * k, min(512 * k + 512, P2)
+        bk = PQ(b - a)
+        mm(bk, [(M("sel"), R("nxh", a, b))])
+        o = R("dd", a, b) if k < 4 else R("sp2", a - V, b - V) if k < 8 else R("f%d" % (k - 8), 0, b - a)
+        lin(o, bk)
+        if k == 3 or k == 7:
+            nm = "dd" if k == 3 else "sp2"
+            dma(T.yn[:, b - V:b], T[nm][0:128:16, 0:V], [], [R(nm, 0, V)])
+        if k >= 8:
+            dma(T.yn[:, a:b], T[o[0]][0:128:16, 0:b - a], [], [o])
+    undo(1, "xa", "key", "dl1", None)
+
+    for emit in ordered(prog):
+        emit()
+
+    for e in ("v", "s", "t", "g"):
+        g.wait_ge(T.sem[semof[e]], tick[e])
+    for k in range(ndma[0]):
+        g.wait_ge(T.sem["d%d" % k], 16)
+    for s, n in arrived.items():
+        g.wait_ge(T.sem[s], n)
+    g.wait_ge(T.sem["loc"], local[0])

@@ -3,48 +3,50 @@ from concourse.mybir import AluOpType as OP, ActivationFunctionType as AF
 
 V, B, W, P2 = 2048, 128, 2432, 4864
 GH = 384
+C4 = W // 4
 MG = 12582912.0
 KP = 4096.0
-BIG = 1048576.0
+NO = 1216.0
+EO = 2040.0
 
-TU = {"CY": 0.0009, "PCY": 0.0006, "WK": 0.1, "OV": 0.05, "GA": 1.4, "TT": 1.8, "VPEN": 0.6}
+TU = {"CY": 0.0009, "PCY": 0.00055, "WK": 0.1, "OV": 0.05, "GA": 1.5, "TT": 1.6, "VPEN": 0.8, "EX": 5.0,
+      "PASS": 10}
+PLAN = {}
+KB = {"idn": 0, "blk": 128, "wz": 256, "wq": 400, "rz": 544, "cv0": 688, "cv1": 832, "cv2": 976, "cv3": 1120}
 SCRATCH = {}
 for _n, _c, _t in (
-        ("xa", W, "float32"), ("key", W, "float32"), ("dd", V, "float32"),
-        ("sp1", V, "float32"), ("sp2", V, "float32"), ("dl1", V, "float32"), ("dl2", V, "float32"),
-        ("ga", P2, "float16"), ("gb", P2, "float16"), ("fnx", P2, "bfloat16"), ("fpv", P2, "bfloat16"),
-        ("nxh", P2, "bfloat16"), ("pvh", P2, "bfloat16"), ("phl", P2, "bfloat16"), ("ghl", 768, "bfloat16"),
-        ("lv1", V, "bfloat16"), ("lv2", V, "bfloat16"), ("lv3", V, "bfloat16"), ("nm", V, "bfloat16"),
-        ("tk", V, "bfloat16"), ("un", 2052, "bfloat16"), ("wz", 144, "bfloat16"), ("wq", 144, "bfloat16"),
-        ("rz", 144, "bfloat16"), ("rn", 144, "bfloat16"),
-        ("idn", 128, "bfloat16"), ("neg", 128, "bfloat16"), ("ngq", 128, "bfloat16"), ("d25", 128, "bfloat16"),
-        ("blk", 128, "bfloat16"), ("blp", 128, "bfloat16"), ("bln", 128, "bfloat16"), ("sel", 128, "bfloat16"),
-        ("seq", 128, "bfloat16"), ("mgc", 128, "bfloat16"),
-        ("idh", 128, "float16"), ("neh", 128, "float16"), ("nqh", 128, "float16"),
-        ("qr", 128, "bfloat16"), ("swp", 128, "float32"), ("one", 512, "bfloat16"), ("hlf", 128, "float32"),
-        ("pm00", 128, "float32"), ("pm01", 128, "float32"), ("pm10", 128, "float32"), ("pm11", 128, "float32"),
-        ("x0i", 2380, "int32"), ("pci", 8, "int32"), ("col", 16, "float32"), ("th32", 8, "float32"), ("ls", 24, "uint16"),
-        ("pid", 304, "float32"), ("pih", 256, "float32"), ("nxf", 304, "float32"), ("pvf", 304, "float32"),
-        ("dnn", 256, "float32"), ("dnp", 256, "float32"), ("dpn", 256, "float32"), ("dpp", 256, "float32"),
-        ("lw", 256, "float32"), ("lc", 256, "float32"), ("w0", 256, "float32"), ("w1", 256, "float32"),
-        ("hn", 256, "bfloat16"), ("hp", 256, "bfloat16"), ("ln_", 256, "bfloat16"), ("lp_", 256, "bfloat16"),
-        ("lpn", 304, "uint16"), ("lpp", 304, "uint16"),
+        ("xa", W, "float32"), ("key", W, "float32"), ("yw", P2, "float32"),
+        ("sp1", V, "float32"), ("sp2", V, "float32"), ("dl1", V, "int32"), ("dl2", V, "float32"), ("dl3", V, "float32"),
+        ("ga", 2 * P2, "float16"), ("gb", 2 * P2, "float16"), ("g3", 4 * V, "float16"), ("fw", P2, "bfloat16"),
+        ("tk", V, "float16"), ("nm", V, "bfloat16"),
+        ("kb", 1264, "bfloat16"), ("kh", 1264, "float16"), ("neh", 128, "float16"), ("nqh", 128, "float16"),
+        ("rn", 144, "float16"), ("ro", 144, "float16"), ("eh", 144, "float16"),
+        ("un", 1028, "bfloat16"), ("ul", 512, "bfloat16"), ("um", 512, "bfloat16"), ("one", 512, "bfloat16"),
+        ("qr", 128, "bfloat16"), ("mgc", 128, "bfloat16"), ("cw", 128, "bfloat16"), ("pn", 128, "bfloat16"),
+        ("bl4", 128, "bfloat16"), ("swd", 128, "float32"), ("nt0", 128, "float32"), ("nt1", 128, "float32"),
+        ("nw", 144, "float32"), ("o32", 64, "float32"),
+        ("ini", 332, "int32"), ("pci", 8, "int32"), ("col", 48, "float32"), ("th32", 8, "float32"), ("ls", 24, "uint16"),
+        ("nxf", 304, "float32"), ("lw16", 304, "uint16"), ("lp", C4, "uint16"), ("pf", C4, "float32"),
+        ("n16", C4, "float16"), ("pid", 512, "float32"), ("dp", 512, "float32"), ("tb", 512, "float32"),
+        ("lw1", 512, "bfloat16"), ("lw2", 512, "bfloat16"), ("lw3", 512, "bfloat16"), ("nmq", 512, "bfloat16"),
+        ("hi", 512, "bfloat16"), ("lo", 512, "bfloat16"), ("win", 512, "bfloat16"), ("c01", 512, "bfloat16"),
         ("ss", 768, "float32"), ("rs1", 768, "float32"), ("rs2", 768, "float32"),
         ("bs", 3 * GH, "float32"), ("rb1", GH, "float32"), ("rb2", GH, "float32"),
         ("sg1", GH, "float32"), ("sg2", GH, "float32"), ("bt", 128, "float32")):
     SCRATCH[_n] = ("sbuf", [128, _c], _t)
-RINGS = {"f": (6, "float32"), "q": (4, "float32"), "t": (6, "bfloat16"), "m": (2, "bfloat16")}
+RINGS = {"f": (6, "float32"), "q": (4, "float32"), "t": (6, "float16"), "e": (2, "float16")}
 for _r in RINGS:
     for _k in range(RINGS[_r][0]):
         SCRATCH["%s%d" % (_r, _k)] = ("sbuf", [128, 512], RINGS[_r][1])
 for _k in range(8):
     SCRATCH["p%d" % _k] = ("psum", [128, 512], "float32")
 for _k in (1, 2, 3):
-    SCRATCH["l%dn" % _k] = ("sbuf", [128, 304], "uint16")
-    SCRATCH["l%dp" % _k] = ("sbuf", [128, 304], "uint16")
+    SCRATCH["l%d" % _k] = ("sbuf", [128, C4], "uint16")
 ARR = [a + str(d) for a in ("ax1_", "ax2_", "ax3_", "as1_", "as2_", "as3_", "ab3_", "ab2_") for d in (1, 2, 3)]
 SEMAPHORES = ["sv", "ss_", "st", "sg", "loc"] + ARR + ["d%d" % k for k in range(20)]
 PSUMS = ["p%d" % k for k in range(8)]
+POOL = {"size": [4, 5], "diff": [5, 6], "own": [4, 5, 6], "flat": [0, 1, 2, 3], "kept": [4, 5, 6], "undo": [0, 1, 2, 3],
+        "late": [4, 5, 6], "rem": [4, 5, 6]}
 
 
 def R(name, a, b, s=1):
@@ -87,31 +89,47 @@ def ordered(prog):
     tail = [0.0] * n
     for i in range(n - 1, -1, -1):
         tail[i] = prog[i][4] + dur[i] + max([tail[j] + WK for j in succs[i]] or [0.0])
-    left = [len(p) for p in preds]
-    ready = {i: 0.0 for i in range(n) if not left[i]}
-    free, out, when = {}, [], [0.0] * n
+    lat = [p[3] or 0.0 for p in prog]
 
-    def start(i, r):
-        return min(max(r, free.get(v[0], 0.0)) for v in prog[i][0])
-    while ready:
-        t = min(start(i, r) for i, r in ready.items())
-        best = None
-        for i, r in ready.items():
-            if start(i, r) <= t + 0.02 and (best is None or (tail[i], -i) > (tail[best], -best)):
-                best = i
-        i = best
-        r = ready.pop(i)
-        var = min(prog[i][0], key=lambda v: max(r, free.get(v[0], 0.0)) + v[1] + (TU["VPEN"] if v[0] == "v" else 0.0))
-        t = max(r, free.get(var[0], 0.0))
-        if var[0] != "a":
-            free[var[0]] = t + var[1]
-        out.append(var[2])
-        for j in succs[i]:
-            when[j] = max(when[j], t + var[1] + (prog[i][3] or 0.0) + WK)
-            left[j] -= 1
-            if not left[j]:
-                ready[j] = when[j]
-    return out
+    def place(order, before, back):
+        busy, end, pick = {}, [0.0] * n, [0] * n
+        for i in order:
+            r = max([end[j] + WK + (0.0 if back else lat[j]) for j in before[i]] or [0.0]) + (lat[i] if back else 0.0)
+            best = None
+            for k, v in enumerate(prog[i][0]):
+                t, at = r, 0
+                if v[0] != "a":
+                    iv = busy.setdefault(v[0], [])
+                    lo, hi = 0, len(iv)
+                    while lo < hi:
+                        mid = (lo + hi) // 2
+                        if iv[mid][1] <= r:
+                            lo = mid + 1
+                        else:
+                            hi = mid
+                    at = lo
+                    while at < len(iv) and iv[at][0] < t + v[1]:
+                        t = max(t, iv[at][1])
+                        at += 1
+                c = t + v[1] + (TU["VPEN"] if v[0] == "v" else 0.0)
+                if best is None or c < best[0]:
+                    best = (c, k, t, at)
+            _, k, t, at = best
+            v = prog[i][0][k]
+            if v[0] != "a":
+                busy[v[0]].insert(at, (t, t + v[1]))
+            end[i], pick[i] = t + v[1], k
+        return end, pick
+    if n not in PLAN:
+        order = sorted(range(n), key=lambda i: (-tail[i], i))
+        for _ in range(TU["PASS"]):
+            end, pick = place(order, preds, False)
+            span = max(end[i] + lat[i] for i in range(n))
+            if n not in PLAN or span < PLAN[n][0]:
+                PLAN[n] = (span, sorted(range(n), key=lambda i: (end[i] - prog[i][0][pick[i]][1], end[i], i)), pick)
+            end, pick = place(sorted(range(n), key=lambda i: (-end[i] - lat[i], -i)), succs, True)
+            order = sorted(range(n), key=lambda i: (-end[i], i))
+    return [prog[i][0][PLAN[n][2][i]][2] for i in PLAN[n][1]]
 
 
 def rank_program(g, core, T, topo):
@@ -199,22 +217,22 @@ def rank_program(g, core, T, topo):
                          CY * max(64, num(b) * (1 if a[0] in PSUMS or b[0] in PSUMS else TU["TT"] if a[0] == "ind" else 2))))
 
     def vts(o, a, s1, f1, s2=None, f2=None):
-        x1 = ap(s1) if isinstance(s1, tuple) else s1
-        cols = [s1] if isinstance(s1, tuple) else []
+        x1, x2 = [ap(s) if isinstance(s, tuple) else s for s in (s1, s2)]
+        cols = [s for s in (s1, s2) if isinstance(s, tuple)]
         if f2 is None:
             op([o], [a] + cols, ("v", [lambda: g.vector.tensor_scalar(ap(o), ap(a), x1, None, f1)], tm(num(a), o, a)))
         else:
-            op([o], [a] + cols, ("v", [lambda: g.vector.tensor_scalar(ap(o), ap(a), x1, s2, f1, f2)], tm(num(a), o, a)))
+            op([o], [a] + cols, ("v", [lambda: g.vector.tensor_scalar(ap(o), ap(a), x1, x2, f1, f2)], tm(num(a), o, a)))
 
     def vset(o, c):
-        op([o], [], ("v", [lambda: g.vector.memset(ap(o), c)], tm(num(o))))
+        op([o], [], ("v", [lambda: g.vector.memset(ap(o), c)], tm(num(o), o)))
 
     def sact(o, i, f=AF.Copy, bias=0.0, scale=1.0):
         n = num(i)
-        col = isinstance(bias, tuple)
-        bb = ap(bias) if col else bias
-        op([o], [i] + ([bias] if col else []),
-           ("s", [lambda: g.scalar.activation(ap(o), ap(i), f, bias=bb, scale=scale)],
+        cols = [c for c in (bias, scale) if isinstance(c, tuple)]
+        bb, sc = [ap(c) if isinstance(c, tuple) else c for c in (bias, scale)]
+        op([o], [i] + cols,
+           ("s", [lambda: g.scalar.activation(ap(o), ap(i), f, bias=bb, scale=sc)],
             CY * (GA * n if i[0] == "ind" else max(64, n)) + 0.01))
 
     def lin(o, i, scale=1.0, bias=0.0, relu=False):
@@ -224,7 +242,7 @@ def rank_program(g, core, T, topo):
               CY * (GA * n if ind else max(64, n)) + 0.01)
         tv = CY * GA * n if ind else tm(n, o, i)
         if relu:
-            vv = ("v", [lambda: g.vector.tensor_scalar(ap(o), ap(i), 0.0, None, OP.max)], tv)
+            vv = ("v", [lambda: g.vector.tensor_scalar(ap(o), ap(i), bias, 0.0, OP.add, OP.max)], tv)
         elif scale == 1.0 and bias == 0.0:
             vv = ("v", [lambda: g.vector.tensor_copy(ap(o), ap(i))], tv)
         elif scale == 1.0:
@@ -233,12 +251,25 @@ def rank_program(g, core, T, topo):
             vv = ("v", [lambda: g.vector.tensor_scalar(ap(o), ap(i), scale, bias, OP.mult, OP.add)], tv)
         op([o], [i], sv, vv)
 
-    def mm(o, terms, start=True, stop=True):
+    def cut(t, sign):
+        def by_vector():
+            sign[0] = 1
+            return g.vector.tensor_scalar(ap(t), ap(t), 255.0, -255.0, OP.min, OP.add)
+
+        def by_scalar():
+            sign[0] = -1
+            return g.scalar.activation(ap(t), ap(t), AF.Relu, bias=255.0, scale=-1.0)
+        op([t], [t], ("s", [by_scalar], CY * num(t) + 0.01), ("v", [by_vector], tm(num(t), t)))
+
+    def mm(o, terms, start=True, stop=True, more=()):
         n = len(terms)
-        op([o], [x for t in terms for x in t],
-           ("t", [lambda k=k: g.tensor.matmul(ap(o), ap(terms[k][0]), ap(terms[k][1]), start and k == 0,
+
+        def lhs(t):
+            return t[0]() if not isinstance(t[0], tuple) else t[0]
+        op([o], [x for t in terms for x in t if isinstance(x, tuple)] + list(more),
+           ("t", [lambda k=k: g.tensor.matmul(ap(o), ap(lhs(terms[k])), ap(terms[k][1]), start and k == 0,
                                               stop and k == n - 1) for k in range(n)],
-            sum(max(64, num(t[1])) * (4 if SCRATCH[t[0][0]][2] == "float32" else 1) + 25 for t in terms) * PCY))
+            sum(max(64, num(t[1])) * (4 if SCRATCH[t[1][0]][2] == "float32" else 1) + 25 for t in terms) * PCY))
 
     def asel(o, i, pat, cmp, base, cm):
         op([o], [i], ("g", [lambda: g.affine_select(ap(o), ap(i), pat, cmp, 0.0, base, cm)], 0.17 + 2 * CY * num(o)))
@@ -250,14 +281,14 @@ def rank_program(g, core, T, topo):
             op([o], [], ("g", [lambda: g.iota(ap(o), pat, base, cm, allow_small_or_imprecise_dtypes=True)],
                          0.13 + 2 * CY * num(o)))
 
-    def dma(o_ap, i_ap, outs, ins):
+    def dma(o_ap, i_ap, outs, ins, lat=2.5):
         def emit():
             need("y", outs, ins)
             s = "d%d" % ndma[0]
             ndma[0] += 1
             g.sync.dma_start(o_ap, i_ap).then_inc(T.sem[s], 16)
             note("y", s, 16, outs, ins)
-        prog.append(([("y", 0.1, emit)], outs, ins, 2.5, first[0]))
+        prog.append(([("y", 0.1, emit)], outs, ins, lat, first[0]))
 
     peers = {d: T.cores[(rank + d) % N] for d in (1, 2, 3)}
     homes = {d: T.cores[(rank - d) % N] for d in (1, 2, 3)}
@@ -300,25 +331,24 @@ def rank_program(g, core, T, topo):
             ro = [R(nm, cc + c, cc + c + B) for nm, cc in pieces]
             arrived[sems + str(d)] = n
             prog.append(([("a", 0.0, lambda d=d, n=n, ro=ro: note(None, sems + str(d), n, ro, []))],
-                         ro, [("sent" + sems, 0, 1, 1)], 5.0, 0.0))
+                         ro, [("sent" + sems, 0, 1, 1)], TU["EX"], 0.0))
 
-    turn = {r: 0 for r in RINGS}
-    pools = {"a": [0, 1, 2], "c": [0, 1, 2, 4, 5, 6, 7], "z": [0, 1, 2, 3, 4, 5, 6, 7]}
-    pool, pr = ["c"], [0]
+    turn = {}
 
-    def ring(c):
-        turn[c] = (turn[c] + 1) % RINGS[c][0]
-        return "%s%d" % (c, turn[c])
+    def ring(c, n=512):
+        turn[c] = (turn.get(c, 0) + 1) % RINGS[c][0]
+        return R("%s%d" % (c, turn[c]), 0, n)
 
     def F(n=512):
-        return R(ring("f"), 0, n)
+        return ring("f", n)
 
-    def PB():
-        pr[0] += 1
-        return "p%d" % pools[pool[0]][pr[0] % len(pools[pool[0]])]
+    def mask():
+        turn["m"] = (turn.get("m", 0) + 1) % 4
+        return R("nm", 512 * turn["m"], 512 * turn["m"] + 512)
 
-    def PQ(n=512):
-        return R(PB(), 0, n)
+    def PQ(pool, n=512):
+        turn[pool] = (turn.get(pool, -1) + 1) % len(POOL[pool])
+        return R("p%d" % POOL[pool][turn[pool]], 0, n)
 
     CH = [(512 * k, 512 * k + 512) for k in range(4)] + [(V, W)]
     LSB = {d: R("ls", 8 * (d - 1), 8 * d) for d in (1, 2, 3)}
@@ -326,240 +356,267 @@ def rank_program(g, core, T, topo):
     THR = R("th32", 0, 1)
     XA, KEY = R("xa", 0, W), R("key", 0, W)
     ONE = R("one", 0, 512)
+    ODD, EVEN, CPID, CTB = [R("col", c, c + 1) for c in (40, 41, 42, 43)]
 
-    def M(name):
-        return R(name, 0, 128)
+    def M(name, buf="kh"):
+        return R(buf, KB[name], KB[name] + 128) if name in KB else R(name, 0, 128)
 
-    def shifted(name, k):
+    def shifted(name, k, buf="kh"):
+        if name in KB:
+            return R(buf, KB[name] + 16 - k, KB[name] + 144 - k)
         return R(name, 16 - k, 144 - k)
 
-    def lists(wf, ln):
-        pb = PQ(304)
-        for h in (0, 1):
-            mm(R(pb[0], 152 * h, 152 * h + 152), [(M("pm%d%d" % (h, c)), R(wf, c, 304, 2)) for c in (0, 1)])
-        vts(R(ln, 0, 304), pb, MG, OP.add, -MG, OP.add)
+    def lst(l, t, k):
+        return R("l%d" % l, 152 * t + CH[k][0] // 16, 152 * t + CH[k][1] // 16)
 
-    def wrap(flat, wf, lp, ln, rows="wz"):
-        pb = PQ(304)
-        mm(pb, [(shifted(rows, i), R(flat, i, P2, 16)) for i in range(16)])
-        sact(R(wf, 0, 304), pb, AF.Identity, bias=-0.5)
-        vcopy(R(lp, 0, 304), pb)
-        lists(wf, ln)
-
-    def partners(wf, dn, dp):
-        pb = PQ(256)
-        mm(pb, [(M("swp"), R(wf, 0, 256))])
-        vtt(R(dn, 0, 256), pb, R(wf, 0, 256), OP.subtract)
-        vtt(R(dp, 0, 256), R(wf, 0, 256), R("pih", 0, 256), OP.subtract)
-
-    def lst(l, c, h, k):
-        return R("l%d%s" % (l, c), 152 * h + CH[k][0] // 16, 152 * h + CH[k][1] // 16)
-
-    def pc(n, h, k):
+    def pc(n, t, k):
         a, b = CH[k]
-        o = V * h if k < 4 else V + GH * h
+        o = V * t if k < 4 else 3 * V + GH * t
         return R(n, o + a, o + b)
 
-    def chain(l, k, win, f, q, bias=0.0):
-        lin(q, IND(win, lst(l, "n", 0, k)), bias=bias)
-        for c, h in (("n", 1), ("p", 0), ("p", 1)):
-            vtt(q, IND(win, lst(l, c, h, k)), q, f)
+    def every(n, j):
+        return R(n, j, V, 4)
 
+    def nodes(parts):
+        for pb, a, s in parts:
+            nf = F(304)
+            lin(nf, pb, 0.5, MG)
+            lin(R("n16", a, a + 303 * s + 1, s), nf, bias=-(MG + NO))
+
+    def node_lists(l, pairs):
+        for pr, bank in pairs:
+            for t in (2 * pr, 2 * pr + 1):
+                mm(R(bank, 152 * (t % 2), 152 * (t % 2) + 152),
+                   [(shifted("cv%d" % t, 4 * b), R("n16", b, C4, 4)) for b in range(4)])
+            vts(R("l%d" % l, 304 * pr, 304 * pr + 304), R(bank, 0, 304), NO, OP.add)
+
+    def tables(parts, ports):
+        nodes([p[:3] for p in parts])
+        for pb, a, s, own in parts:
+            e = a + (own - 1) * s + 1
+            lin(R("pf", a, a + 303 * s + 1, s), pb)
+            vtt(R("dp", a, e, s), R(pb[0], 0, own), R("pid", a, e, s), OP.subtract)
+        if ports:
+            vts(R("lp", 0, C4), R("pf", 0, C4), 0.5, OP.add)
+        vts(R("tb", 0, 512), R("dp", 0, 512), -1.0, OP.mult, CTB, OP.add)
+
+    def chain(l, k, win, q, bias=0.0):
+        lin(q, IND(win, lst(l, 0, k)), bias=bias)
+        for t in (1, 2, 3):
+            vtt(q, IND(win, lst(l, t, k)), q, OP.add)
+
+    def flat(mat, src, pool, use):
+        for j in range(4):
+            u = PQ(pool)
+            mm(u, [(R(mat, 128 * j, 128 * j + 128), R(src, 0, 512))])
+            use(j, u)
+
+    dma(T.ini[:, 0:304], T.nxt[:], [R("ini", 0, 304)], [], 2.2)
+    dma(T.ini[:, 304:328], T.shw[:], [R("ini", 304, 328)], [], 2.2)
     for k in range(2):
-        dma(T.x0i[:, 1024 * k:1024 * k + 1024], T.x0[:, 1024 * k:1024 * k + 1024], [R("x0i", 1024 * k, 1024 * k + 1024)], [])
-    dma(T.x0i[:, 2352:2376], T.shw[:], [R("x0i", 2352, 2376)], [])
-    dma(T.x0i[:, 2048:2352], T.nxt[:], [R("x0i", 2048, 2352)], [])
-    dma(T.x0i[:, 2376:2377], T.th[:], [R("x0i", 2376, 2377)], [])
+        dma(T.dl1[:, 1024 * k:1024 * k + 1024], T.x0[:, 1024 * k:1024 * k + 1024], [R("dl1", 1024 * k, 1024 * k + 1024)], [],
+            4.0)
+    dma(T.ini[:, 328:329], T.th[:], [R("ini", 328, 329)], [])
     iota(R("pci", 0, 1), [[0, 1]], 0, 1)
-    iota(R("t0", 0, 512), [[64, 8], [0, 64]], 0, 0)
-    iota(R("t1", 0, 512), [[0, 8], [1, 64]], 0, 0)
-    vset(ONE, 1.0)
-    for n in ("blk", "sel", "seq"):
-        vset(M(n), 1.0)
-    vset(M("hlf"), 0.5)
-    vset(R("un", 0, 2052), 0.0)
-    for n in ("wz", "wq", "rz", "rn"):
-        vset(R(n, 0, 144), 0.0)
-    for n, lo, hi in (("sel", 0, 1), ("seq", 2, 3), ("blk", 0, 15)):
-        asel(M(n), M(n), [[-16, 8], [0, 16]], OP.is_ge, -lo, 1)
-        asel(M(n), M(n), [[16, 8], [0, 16]], OP.is_ge, hi, -1)
-    asel(M("idn"), R("one", 0, 128), [[-1, 128]], OP.is_equal, 0, 1)
-    for h in (0, 1):
-        for c in (0, 1):
-            asel(M("pm%d%d" % (h, c)), M("hlf"), [[-16, 8], [1000, 2], [-2, 8]], OP.is_equal, -h - 1000 * c, 1)
+    iota(R("nm", 0, 128), [[64, 2], [0, 64]], 0, 0)
+    iota(R("nm", 128, 256), [[0, 2], [1, 64]], 0, 0)
+    iota(R("col", 0, 33), [[128, 33]], 0, 0)
     vts(R("pci", 1, 2), R("pci", 0, 1), 1, OP.bitwise_and)
-    vts(R("pci", 2, 3), R("pci", 0, 1), 15, OP.bitwise_and)
-    vcopy(R("col", 0, 1), R("pci", 1, 2))
-    vts(R("col", 1, 2), R("col", 0, 1), -1.0, OP.mult, 1.0, OP.add)
-    vcopy(R("col", 2, 3), R("pci", 2, 3))
-    for b in range(1, 10):
-        vts(R("col", 2 + b, 3 + b), R("col", 1, 2), 512.0 * b, OP.mult)
-    vts(R("t2", 0, 512), R("t0", 0, 512), R("col", 1, 2), OP.mult)
-    vts(R("t3", 0, 512), R("t1", 0, 512), R("col", 0, 1), OP.mult)
-    vtt(R("phl", 0, 512), R("t2", 0, 512), R("t3", 0, 512), OP.add)
+    vcopy(ODD, R("pci", 1, 2))
+    vts(EVEN, ODD, -1.0, OP.mult, 1.0, OP.add)
+    vts(R("col", 0, 33), R("col", 0, 33), EVEN, OP.mult)
+    vts(R("nm", 0, 128), R("nm", 0, 128), EVEN, OP.mult)
+    vts(R("nm", 128, 256), R("nm", 128, 256), -0.5, OP.add, ODD, OP.mult)
+    vtt(R("g3", 0, 128), R("nm", 0, 128), R("nm", 128, 256), OP.add)
+    for b in (1, 2, 4, 8, 16, 32):
+        n = min(128 * b, P2 - 128 * b)
+        sact(R("g3", 128 * b, 128 * b + n), R("g3", 0, n), AF.Identity, bias=R("col", b, b + 1))
+    vcopy(R("lw16", 0, 304), R("ini", 0, 304))
+    vts(R("nxf", 0, 304), R("ini", 0, 304), -0.5, OP.add)
     first[0] = 100.0
-    vcopy(R("ls", 0, 24), R("x0i", 2352, 2376))
+    vcopy(LSA, R("ini", 304, 328))
     for k in range(2):
-        vcopy(R("xa", 1024 * k, 1024 * k + 1024), R("x0i", 1024 * k, 1024 * k + 1024))
+        vts(R("xa", 1024 * k, 1024 * k + 1024), R("dl1", 1024 * k, 1024 * k + 1024), -MG, OP.add)
     sact(R("bs", 0, GH), IND(R("xa", 0, V), LSA))
     send(peers, [("bs", 0, "xa", V)], "ax1_", [R("bs", 0, GH)])
     recv("ax1_", homes, [("xa", V)])
     first[0] = 0.0
-    vcopy(R("nxf", 0, 304), R("x0i", 2048, 2352))
-    vts(R("nxf", 0, 304), R("nxf", 0, 304), -0.5, OP.add)
-    vcopy(R("lpn", 0, 304), R("x0i", 2048, 2352))
-    for b in range(1, 10):
-        n = min(512, P2 - 512 * b)
-        sact(R("phl", 512 * b, 512 * b + n), R("phl", 0, n), AF.Identity, bias=R("col", 2 + b, 3 + b))
-    lists("nxf", "l1n")
-    vcopy(IND(R("pvh", 0, P2), R("lpn", 0, 256)), R("phl", 0, 4096))
-    vcopy(IND(R("pvh", 0, P2), R("lpn", 256, 304)), R("phl", 4096, P2))
-    vset(M("swp"), 1.0)
+    for a, b in ((0, 64), (64, 128), (128, 256), (256, 304)):
+        vcopy(IND(R("fw", 0, P2), R("lw16", a, b)), R("g3", 16 * a, 16 * b))
+    vset(ONE, 1.0)
+    vset(R("o32", 0, 64), 1.0)
+    vset(R("kb", 256, 1264), 0.0)
+    vset(R("un", 0, 1028), 0.0)
+    vset(R("nw", 0, 144), 0.0)
     vset(M("qr"), 3.0 / 1024.0)
     vset(M("mgc"), MG / 128.0)
+    o128, o64, o8 = R("one", 0, 128), R("o32", 0, 64), R("one", 0, 8)
+    for c in (0, 1):
+        for h in (0, 1):
+            asel(R("nt%d" % c, h, 128, 2), o64, [[-16, 8], [-2, 4], [1000, 2]], OP.is_equal, -8 * c - h, 1)
+    for t in range(4):
+        asel(shifted("cv%d" % t, 0, "kb"), o128, [[-16, 8], [1000, 4], [-4, 4]], OP.is_equal, -t, 1)
+    lin(R("kh", KB["cv0"], 1264), R("kb", KB["cv0"], 1264))
+    asel(M("idn", "kb"), o128, [[-1, 128]], OP.is_equal, 0, 1)
+    for n, lo in (("wz", 0), ("wq", 2)):
+        o = R("kb", KB[n] + 16, KB[n] + 144, 16)
+        asel(o, o8, [[-16, 8]], OP.is_ge, -lo, 1)
+        asel(o, o, [[16, 8]], OP.is_ge, lo + 1, -1)
+    for o, pat in ((M("blk", "kb"), [[-16, 8], [0, 16]]), (shifted("rz", 0, "kb"), [[-16, 8], [-1000, 4], [0, 4]])):
+        asel(o, o128, pat, OP.is_ge, 0, 1)
+        asel(o, o, [[16, 8], [0, 16]], OP.is_ge, 15, -1)
+    lin(R("kh", 0, KB["cv0"]), R("kb", 0, KB["cv0"]))
+    for n, i, c in (("neh", "idn", -1.0), ("nqh", "idn", -0.25), ("cw", "idn", 8192.0 * EO), ("pn", "idn", -2.0 ** 30)):
+        sact(M(n), M(i, "kb"), scale=c)
+    for n, i, c in (("rn", "rz", -1.0), ("ro", "rz", -8192.0), ("eh", "wz", 4096.0)):
+        sact(R(n, 0, 144), R("kb", KB[i], KB[i] + 144), scale=c)
+    asel(M("bl4"), o128, [[-4, 32], [0, 4]], OP.is_ge, 0, 1)
+    asel(M("bl4"), M("bl4"), [[4, 32], [0, 4]], OP.is_ge, 3, -1)
+    asel(R("ul", 0, 512), ONE, [[-4, 4], [-16, 8], [0, 16]], OP.is_equal, 0, 1)
+    sact(R("um", 0, 512), R("ul", 0, 512), scale=MG)
+    for s in (0, 1):
+        asel(R("un", 4 + 2 * s, 1028, 16), R("one", 0, 64), [[-4, 4], [-1, 2], [-16, 8]], OP.is_equal, -2 * s, 1)
+    for h in (0, 1):
+        asel(R("swd", h, 128, 2), o64, [[-2, 64]], OP.is_equal, h - 1, 1)
+        asel(R("nw", 16 + h, 144, 2), o64, [[-16, 8], [1000, 2], [-4, 4]], OP.is_equal, -h, 1)
+    vtt(M("swd"), M("swd"), M("idn", "kb"), OP.subtract)
+    iota(R("pid", 0, 512), [[8, 512]], 0, 0)
+    vts(R("pci", 2, 3), R("pci", 0, 1), 2, OP.arith_shift_right, 3, OP.bitwise_and)
+    vts(CPID, R("pci", 2, 3), 2.0, OP.mult, -0.5, OP.add)
+    vts(CPID, CPID, ODD, OP.add)
+    vts(CTB, ODD, -1.0, OP.mult, 1.5, OP.add)
+    sact(R("pid", 0, 512), R("pid", 0, 512), AF.Identity, bias=CPID)
+    vcopy(THR, R("ini", 328, 329))
+    iota(R("yw", 4096, P2), [[1, 768]], 4096, 0)
+
+    for c in (0, 1):
+        mm(R("p%d" % (4 + c), 0, 304), [(M("nt%d" % c), R("nxf", 0, 304))])
+    nodes([(R("p%d" % (4 + c), 0, 304), c, 2) for c in (0, 1)])
+    node_lists(1, [(0, "p6")])
+    for k in range(5):
+        for t in (0, 1):
+            lin(pc("ga", t, k), IND(XA, lst(1, t, k)), bias=MG)
+    for c in (0, 1):
+        mm(R("p%d" % (4 + c), 0, 304), [(M("nt%d" % c), R("nxf", 0, 304))] +
+           [(shifted("wq", 2 + 4 * (i // 2) + i % 2, "kb"), R("fw", 8 * c + i, P2, 16)) for i in range(8)])
+    tables([(R("p%d" % (4 + c), 0, 304), c, 2, 256) for c in (0, 1)], True)
+    node_lists(1, [(1, "p6")])
+    lin(R("fw", 4096, P2), R("g3", 4096, P2))
     vset(R("nm", 0, V), 0.0)
     for d in (1, 2, 3):
-        vcopy(IND(R("nm", 0, V), LSB[d]), R("one", 0, 128))
-    vcopy(THR, R("x0i", 2376, 2377))
-    for n, i, c in (("neg", "idn", -1.0), ("ngq", "idn", -0.25), ("d25", "idn", 33554432.0), ("blp", "blk", 4096.0),
-                    ("bln", "blk", -4096.0)):
-        sact(M(n), M(i), scale=c)
-    sact(R("ghl", 0, 768), R("phl", 4096, P2))
-    sact(R("wz", 16, 144, 16), R("sel", 0, 128, 16))
-    sact(R("wq", 16, 144, 16), R("seq", 0, 128, 16))
-    for h in (0, 1):
-        sact(R("rz", 16 + h, 144, 16), R("blk", h, 128, 16))
-        sact(R("rn", 16 + h, 144, 16), R("blk", h, 128, 16), scale=-1.0)
-    asel(R("un", 4, 2052, 4), ONE, [[-1, 16], [-16, 8], [0, 4]], OP.is_equal, 0, 1)
-    asel(R("swp", 0, 128, 2), R("swp", 0, 128, 2), [[-2, 64]], OP.is_equal, -1, 1)
-    asel(R("swp", 1, 128, 2), R("swp", 1, 128, 2), [[-2, 64]], OP.is_equal, 0, 1)
-    iota(R("pid", 0, 304), [[16, 304]], 0, 0)
-    vts(R("pid", 0, 304), R("pid", 0, 304), R("col", 2, 3), OP.add)
-    vts(R("pih", 0, 256), R("pid", 0, 256), -0.5, OP.add)
-    vcopy(M("idh"), M("idn"))
-    vcopy(M("neh"), M("neg"))
-    vcopy(M("nqh"), M("ngq"))
+        vcopy(IND(R("nm", 0, V), LSB[d]), o128)
+    mm(R("p7", 0, 512), [(shifted("rz", 4 * j, "kb"), every("nm", j)) for j in range(4)])
+    lin(R("nmq", 0, 512), R("p7", 0, 512), -65.0 / 16, 1.0)
 
-    for k in range(5):
-        for h in (0, 1):
-            lin(pc("fnx", h, k), IND(XA, lst(1, "n", h, k)))
-    wrap("pvh", "pvf", "lpp", "l1p")
-    partners("nxf", "dnn", "dpn")
-    partners("pvf", "dnp", "dpp")
-
+    I1, NI, NQ = M("idn"), M("neh"), M("nqh")
     for l in (1, 2, 3):
-        LVn = "lv%d" % l
-        srcs = {1: [("fpv", "fnx")], 2: [("ga", "gb")], 3: [("fpv", "fnx"), ("pvh", "nxh")]}[l]
-        I1, NI, NQ = [M(x) for x in (("idh", "neh", "nqh") if l == 2 else ("idn", "neg", "ngq"))]
-        pool[0] = "a"
+        srcs = ["ga"] if l < 3 else ["ga", "gb"]
+        gk = "gb" if l < 3 else "g3"
+        LW = R("lw%d" % l, 0, 512)
+        dl, p0 = "dl%d" % l, "sp%d" % l if l < 3 else "yw"
         zb, tk = {}, {}
 
         def gathers(k):
             a, b = CH[k]
             n = b - a
-            fp, fn = srcs[0]
-            if l > 1:
-                for h in (0, 1):
-                    lin(pc(fn, h, k), IND(XA, lst(l, "n", h, k)))
-            for h in (0, 1):
-                lin(pc(fp, h, k), IND(XA, lst(l, "p", h, k)))
+            for t in range(4):
+                if l > 1 or t > 1:
+                    lin(pc("ga", t, k), IND(XA, lst(l, t, k)), bias=MG)
             if l == 3:
-                for s, c in (("nxh", "n"), ("pvh", "p")):
-                    for h in (0, 1):
-                        lin(pc(s, h, k), IND(R("phl", W, P2), lst(l, c, h, k)), bias=-0.375)
-            zb[k] = R("p%d" % (4 + k), 0, 512) if k < 4 else PQ(n)
+                for t in range(4):
+                    lin(pc("gb", t, k), IND(R("fw", 0, W), lst(l, t, k)), bias=-0.375)
+            zb[k] = R("p%d" % k, 0, n)
             one = R("one", 0, n)
-            mm(zb[k], [(NQ, pc(p[1], h, k)) for p in srcs for h in (0, 1)] + ([(M("qr"), one)] if l < 3 else []), stop=False)
-            mm(zb[k], [(NQ, pc(p[0], h, k)) for p in srcs for h in (0, 1)] + [(M("mgc"), one)], start=False)
-            xm = F(n)
-            lin(xm, R("xa", a, b), bias=-MG)
-            vtt(zb[k], zb[k], xm, OP.add)
+            mm(zb[k], [(NQ, pc(s, t, k)) for s in srcs for t in (0, 1)] + ([(M("qr"), one)] if l < 3 else []), stop=False)
+            mm(zb[k], [(NQ, pc(s, t, k)) for s in srcs for t in (2, 3)] + [(M("mgc"), one)], start=False)
+            vtt(zb[k], zb[k], R("xa", a, b), OP.add)
 
         def sized(k):
-            return [(M("sel"), R("phl", CH[k][0], CH[k][1])), (M("blp" if l == 1 else "bln"), tk[k])]
+            a, b = CH[k]
+            n = b - a
+            t = e = tk[k] = R("tk", a, b) if k < 4 else ring("t", n)
+            if l > 1:
+                e = ring("e", n) if l == 2 else F(n)
+            sact(e, zb[k], AF.Abs)
+            if l > 1:
+                vts(t, e, 255.0, OP.min)
+            o = PQ("size", n) if k < 4 else R("p5", 0, n)
+            mm(o, [(M("blk"), t)])
+            lin(R("key", a, b), o, bias=-EO)
+            if k < 4:
+                tk[k] = mask()
+                vts(tk[k], e, THR, OP.is_ge)
 
         def detail(k):
             a, b = CH[k]
-            n, d = b - a, zb[k]
-            t = e = tk[k] = R("tk", a, b) if k < 4 else R(ring("t"), 0, n)
-            if l == 1:
-                sact(t, d, AF.Abs)
-            else:
-                e = F(n)
-                sact(e, d, AF.Abs)
-                sact(t, e, AF.Relu, bias=255.0, scale=-1.0)
-            o = PQ(n)
-            mm(o, sized(k))
-            lin(R("key", a, b), o)
-            if k == 4:
-                return
-            m, w, q, ds = R(ring("m"), 0, 512), F(), F(), PQ()
-            vts(m, e, THR, OP.is_ge)
+            d, m, q = zb[k], tk[k], F()
+            vtt(R(dl, a, b), d, m, OP.mult)
             if l < 3:
+                w = F()
                 lin(w, m, bias=KP)
+                lin(q, d, 0.25, -0.375)
+                vts(d, q, MG, OP.add, -MG, OP.add)
+                vtt(R(p0, a, b), d, w, OP.mult)
             else:
-                lin(w, m, -1.0, 1.0)
-            lin(q, d, 0.25, -0.375)
-            vtt(R("dd", a, b), d, m, OP.mult)
-            vts(ds, q, MG, OP.add, -MG, OP.add)
-            vtt(d, ds, w, OP.mult)
+                vtt(d, d, R(dl, a, b), OP.subtract)
+                lin(q, d, 0.25, -0.375)
+                vts(R(p0, a, b), q, MG, OP.add, -MG, OP.add)
 
-        def chosen(k):
-            a, b = CH[k]
-            f = R(ring("q"), 0, 512)
-            chain(l, k, KEY, OP.min, f)
-            o = PQ()
-            mm(o, [(M("d25"), R(x, a, b)) for x in ["nm"] + ["lv%d" % j for j in range(1, l)]] + sized(k))
-            vtt(R(LVn, a, b), o, f, OP.is_lt)
+        def chosen():
+            for t in range(4):
+                for a in (0, 64):
+                    lin(R(gk, V * t + 16 * a, V * t + 16 * a + 1024), IND(KEY, R("l%d" % l, 152 * t + a, 152 * t + a + 64)))
+            o = R("p4", 0, 512)
+            mm(o, [(M("cw"), R("nmq", 0, 512))] + [(M("pn"), R("lw%d" % j, 0, 512)) for j in range(1, l)] +
+               [(shifted("ro", 4 * j), every("tk", j)) for j in range(4)], stop=False)
+            for t in range(4):
+                mm(o, [(shifted("eh", 4 * j + t), R(gk, V * t + j, V * t + V, 4)) for j in range(4)], False, t == 3)
+            vtt(R("win", 0, 512), o, R("tb", 0, 512), OP.is_gt)
+            mm(o, [(M("bl4"), R("win", 0, 512))])
+            lin(LW, o, bias=-3.0, relu=True)
 
         def likeness(k):
             terms = []
             for x, y in ((0, 0), (1, 1), (0, 1), (1, 0)):
-                u = PQ()
-                mm(u, [(I1, pc(s[0], x, k)) for s in srcs] + [(NI, pc(s[1], y, k)) for s in srcs])
-                tn = ring("t")
+                u, tn, sign = PQ("diff"), ring("t"), [1]
+                mm(u, [(I1, pc(s, 2 + x, k)) for s in srcs] + [(NI, pc(s, y, k)) for s in srcs])
                 if l == 1:
-                    lin(R(tn, 0, 512), u, relu=True)
+                    lin(tn, u, relu=True)
                 else:
-                    sact(R(tn, 0, 512), u, AF.Abs)
-                    sact(R(tn, 0, 512), R(tn, 0, 512), AF.Relu, bias=255.0, scale=-1.0)
-                sg = "rz" if (x == y) == (l == 1) else "rn"
-                terms += [(shifted(sg, 2 * i), R(tn, i, 512, 8)) for i in range(8)]
-            mm(R("p3", 64 * k, 64 * k + 64), terms)
+                    sact(tn, u, AF.Abs)
+                    cut(tn, sign)
+                terms += [(lambda j=j, sign=sign, same=x == y: shifted("rz" if same == (sign[0] > 0) else "rn", 4 * j),
+                           R(tn[0], j, 512, 4)) for j in range(4)]
+            mm(R("p7", 128 * k, 128 * k + 128), terms, more=[R("kh", KB["rz"], KB["rz"] + 144), R("rn", 0, 144)])
 
-        def links_small():
-            lb = PB()
-            for k in range(4):
-                a, b = CH[k]
-                mm(R(lb, 64 * k, 64 * k + 64), [(shifted("rz", 2 * i), R(LVn, a + i, b, 8)) for i in range(8)])
-            lin(R("lw", 0, 256), R(lb, 0, 256), 1.0 / 16)
-            vts(R("lc", 0, 256), R("p3", 0, 256), 0.0, OP.is_gt)
-            vtt(R("lc", 0, 256), R("lc", 0, 256), R("lw", 0, 256), OP.mult)
-            for (dn, dp, h, lo) in (("dnn", "dpn", "hn", "ln_"), ("dnp", "dpp", "hp", "lp_"))[:2 if l < 3 else 1]:
-                vtt(R("w0", 0, 256), R("lc", 0, 256), R(dn, 0, 256), OP.mult)
-                vtt(R("w1", 0, 256), R("lw", 0, 256), R(dp, 0, 256), OP.mult)
-                vtt(R("w0", 0, 256), R("w0", 0, 256), R("w1", 0, 256), OP.add)
-                vtt(R("w0", 0, 256), R("w0", 0, 256), R("pid", 0, 256), OP.add)
-                lin(R(h, 0, 256), R("w0", 0, 256))
-                vtt(R(lo, 0, 256), R("w0", 0, 256), R(h, 0, 256), OP.subtract)
+        def links():
+            o, c = R("p7", 0, 512), R("c01", 0, 512)
+            vts(c, o, 0.0, OP.is_gt)
+            mm(o, [(M("swd"), R("pf", 0, 512))])
+            vtt(o, o, c, OP.mult)
+            vtt(o, o, R("dp", 0, 512), OP.add)
+            vtt(o, o, LW, OP.mult)
+            vtt(o, o, R("pid", 0, 512), OP.add)
+            lin(R("hi", 0, 512), o)
+            vtt(R("lo", 0, 512), o, R("hi", 0, 512), OP.subtract)
 
-        def unwrap():
-            if l != 2:
-                lin(R("fnx", 4096, P2), R("ghl", 0, 768))
-            for i in range(16):
-                if i % 2 == 0:
-                    bn = PB()
-                bk = R(bn, 256 * (i % 2), 256 * (i % 2) + 256)
-                mm(bk, [(R("un", 4 + 128 * i - r, 132 + 128 * i - r), R(x, 0, 256))
-                        for r, x in enumerate(("hn", "ln_", "hp", "lp_")[:4 if l < 3 else 2])])
-                lin(R("fnx", i, 4096, 16), bk)
+        def unwrap(pool):
+            for i in range(8):
+                bk = PQ(pool)
+                mm(bk, [(R("un", 4 + 128 * i - r, 132 + 128 * i - r), R(x, 0, 512))
+                        for r, x in ((0, "hi"), (1 if l < 3 else 0, "lo"))])
+                if l < 3:
+                    lin(R("fw", i, 4096, 8), bk)
+                else:
+                    lin(R("yw", i, 4096, 8), bk, bias=0.5)
 
         def own(k):
             a, b = CH[k]
-            x, b1, b2 = R("xa", a, b), PQ(), PQ()
+            x = R("xa", a, b)
             if l < 3:
+                b1, b2 = PQ("own"), PQ("own")
                 s = R("sp%d" % l, a, b)
-                chain(l, k, KEY, OP.add, s)
+                chain(l, k, KEY, s)
                 z = F()
                 lin(z, s, bias=MG * KP)
                 lin(b1, z, 1.0 / KP, -MG)
@@ -567,11 +624,9 @@ def rank_program(g, core, T, topo):
                 vtt(x, b1, x, OP.add)
                 vtt(s, s, b2, OP.subtract)
             else:
-                q = R(ring("q"), 0, 512)
-                lin(b2, R(LVn, a, b), -BIG)
-                vtt(x, b2, x, OP.add)
-                chain(l, k, KEY, OP.add, q)
-                vtt(x, q, x, OP.add)
+                q = ring("q")
+                for t in range(4):
+                    vtt(q if t < 3 else x, IND(KEY, lst(l, t, k)), q if t else x, OP.add)
 
         def border(buf, rc):
             for d in (1, 2, 3):
@@ -579,74 +634,70 @@ def rank_program(g, core, T, topo):
                 vtt(R("bt", 0, 128), IND(R(buf, 0, V), LSB[d]), R(rs, c, c + B), OP.add)
                 vcopy(IND(R(buf, 0, V), LSB[d]), R("bt", 0, 128))
 
-        def kept(k):
-            a, b = CH[k]
-            b2 = PQ()
-            lin(b2, R(LVn, a, b), BIG, -(BIG + MG))
-            vtt(R("dd" if l == 3 else "dl%d" % l, a, b), b2, R("dd", a, b), OP.add)
-            if l < 3:
-                b1, s = PQ(), R("sp%d" % l, a, b)
-                lin(b1, R(LVn, a, b), BIG)
-                vtt(s, b1, s, OP.add)
+        def kept():
+            def use(j, u):
+                vtt(every(dl, j), u, every(dl, j), OP.add)
+                if l < 3:
+                    vtt(every("sp%d" % l, j), u, every("sp%d" % l, j), OP.add)
+            flat("um", LW[0], "kept", use)
 
         if l == 3:
             for k in range(5):
                 a, b = CH[k]
-                t = R(ring("t"), 0, b - a)
-                lin(t, R("xa", a, b))
-                vtt(R("phl", W + a, W + b), R("xa", a, b), t, OP.subtract)
-        order = [4, 0, 1, 2, 3] if l > 1 else [0, 1, 2, 3, 4]
-        for i in range(6):
-            if i < 5:
-                gathers(order[i])
-            if i > 0:
-                detail(order[i - 1])
+                t, tp = ring("t", b - a), PQ("rem", b - a)
+                lin(t, R("xa", a, b), bias=MG)
+                lin(tp, t, bias=-MG)
+                vtt(R("fw", a, b), R("xa", a, b), tp, OP.subtract)
+        for k in ([4, 0, 1, 2, 3] if l > 1 else [0, 1, 2, 4, 3]):
+            gathers(k)
+            sized(k)
         for k in range(4):
-            chosen(k)
-            if k < (4 if l < 3 else 2):
+            detail(k)
+        chosen()
+        if l < 3:
+            for k in range(4):
                 likeness(k)
         vset(R("key", V, W), 0.0)
-        for k in range(4):
-            a, b = CH[k]
-            vtt(R("key", a, b), zb[k], R(LVn, a, b), OP.mult)
-        pool[0] = "c"
+        flat("ul", LW[0], "flat", lambda j, u: vtt(every("key", j), u, every(p0, j), OP.mult))
         rs = "rs2" if l == 2 else "rs1"
         xg = [R("xa", V, W)]
         if l < 3:
-            q, z, b4 = F(GH), F(GH), PQ(GH)
-            chain(l, 4, KEY, OP.add, q)
+            q, z, b4 = F(GH), F(GH), PQ("own", GH)
+            chain(l, 4, KEY, q)
             lin(z, q, bias=MG * KP)
             lin(b4, z, bias=-MG * KP)
             lin(R("ss", 0, GH), z, 1.0 / KP, -MG)
             vtt(R("ss", GH, 768), q, b4, OP.subtract)
             send(homes, [("ss", 0, rs, 0), ("ss", GH, rs, GH)], "as%d_" % l, [R("ss", 0, 768)], xg)
             recv("as%d_" % l, peers, [(rs, 0), (rs, GH)])
-            links_small()
-            own(0)
-            own(1)
-            unwrap()
-            own(2)
-            own(3)
+            links()
+            unwrap("flat")
+            for k in range(4):
+                own(k)
             border("xa", 0)
             sact(R("bs", 0, GH), IND(R("xa", 0, V), LSA))
             send(peers, [("bs", 0, "xa", V)], "ax%d_" % (l + 1), [R("bs", 0, GH)], [R("rs1", 0, 768)] if l == 2 else [])
             recv("ax%d_" % (l + 1), homes, [("xa", V)])
-            for (o, lp) in (("nxh", "lpn"), ("pvh", "lpp")):
-                for k in range(4):
-                    lin(R(o, 1216 * k, 1216 * k + 1216), IND(R("fnx", 0, P2), R(lp, 76 * k, 76 * k + 76)))
-            wrap("nxh", "nxf", "lpn", "l%dn" % (l + 1))
+            for k in range(8):
+                lin(R("gb", 1216 * k, 1216 * k + 1216), IND(R("fw", 0, P2), R("lp", 76 * k, 76 * k + 76)))
+            for hf in (0, 1):
+                mm(R("p%d" % hf, 0, 304), [(shifted("wz" if i % 4 < 2 else "wq", i), R("gb", P2 * hf + i, P2 * hf + P2, 16))
+                                          for i in range(16)])
             border("sp%d" % l, GH)
             sact(R("sg%d" % l, 0, GH), IND(R("sp%d" % l, 0, V), LSA))
-            for k in range(4):
-                kept(k)
-            wrap("pvh", "pvf", "lpp", "l%dp" % (l + 1), "wq")
-            partners("nxf", "dnn", "dpn")
-            if l < 2:
-                partners("pvf", "dnp", "dpp")
+            kept()
+            tables([(R("p0", 0, 304), 0, 1, 304), (R("p1", 0, 304), 304, 1, 208)], l < 2)
+            node_lists(l + 1, [(0, "p2"), (1, "p3")])
+            if l == 2:
+                bk = PQ("kept", 304)
+                mm(bk, [(shifted("nw", 8 * c), R("pf", c, C4, 2)) for c in (0, 1)])
+                vts(R("lw16", 0, 304), bk, 0.5, OP.add)
         else:
-            chain(l, 4, KEY, OP.add, R("ss", 0, GH))
+            chain(l, 4, KEY, R("ss", 0, GH))
             send(homes, [("ss", 0, rs, 0)], "as3_", [R("ss", 0, GH)], xg)
             recv("as3_", peers, [(rs, 0)])
+            lin(R("win", 0, 512), LW, -1.0, 1.0)
+            flat("um", "win", "flat", lambda j, u: vtt(every("xa", j), u, every("xa", j), OP.add))
             for k in range(4):
                 own(k)
             border("xa", 0)
@@ -657,51 +708,36 @@ def rank_program(g, core, T, topo):
             send(peers, [("bs", GH, "rb2", 0), ("bs", 2 * GH, "rb1", 0)], "ab2_", [R("bs", GH, 3 * GH)])
             recv("ab3_", homes, [("xa", V)])
             recv("ab2_", homes, [("rb2", 0), ("rb1", 0)])
-            for k in range(4):
-                kept(k)
+            flat("um", LW[0], "flat", lambda j, u: vtt(every(dl, j), u, every(dl, j), OP.add))
             sact(R("key", V, W), R("rb2", 0, GH))
-            likeness(2)
-            likeness(3)
-            links_small()
-            unwrap()
+            for k in range(4):
+                likeness(k)
+            links()
+            unwrap("late")
 
-    pool[0] = "z"
+    def undo(l, src, dst, sp):
+        for k in range(4):
+            a, b = CH[k]
+            z, y = ring("q"), PQ("undo")
+            chain(l, k, R(src, 0, W), z, -1.5)
+            lin(y, z, 0.25, -MG)
+            vtt(y, y, R("dl%d" % l, a, b), OP.add)
+            if sp is None:
+                vtt(R(dst, a, b), y, R(src, a, b), OP.max)
+                dma(T.yx[:, a:b], T[dst][:, a:b], [], [R(dst, a, b)])
+            else:
+                vtt(y, y, R(src, a, b), OP.max)
+                vtt(R(dst, a, b), y, R(sp, a, b), OP.subtract)
 
-    def undo(l, src, dst, dl, sp):
-        fms = {}
-        for k in range(5):
-            if k < 4:
-                z, fms[k] = R(ring("q"), 0, 512), PQ()
-                chain(l, k, R(src, 0, W), OP.add, z, -1.5)
-                lin(fms[k], z, 0.25, MG)
-            if k > 0:
-                a, b = CH[k - 1]
-                y, mx = PQ(), PQ()
-                vtt(y, fms[k - 1], R(dl, a, b), OP.add)
-                if sp is None:
-                    vtt(R(dst, a, b), y, R(src, a, b), OP.max)
-                    dma(T.yx[:, a:b], T[dst][:, a:b], [], [R(dst, a, b)])
-                else:
-                    vtt(mx, y, R(src, a, b), OP.max)
-                    vtt(R(dst, a, b), mx, R(sp, a, b), OP.subtract)
-
-    undo(3, "xa", "key", "dd", "sp2")
+    undo(3, "xa", "key", "sp2")
     sact(R("xa", V, W), R("rb1", 0, GH))
-    for k in range(4):
-        lin(R("nxh", 1216 * k, 1216 * k + 1216), IND(R("fnx", 0, P2), R("lpn", 76 * k, 76 * k + 76)))
-    undo(2, "key", "xa", "dl2", "sp1")
-    for k in range(10):
-        a, b = 512 * k, min(512 * k + 512, P2)
-        bk = PQ(b - a)
-        mm(bk, [(M("sel"), R("nxh", a, b))])
-        o = R("dd", a, b) if k < 4 else R("sp2", a - V, b - V) if k < 8 else R("f%d" % (k - 8), 0, b - a)
-        lin(o, bk)
-        if k == 3 or k == 7:
-            nm = "dd" if k == 3 else "sp2"
-            dma(T.yn[:, b - V:b], T[nm][0:128:16, 0:V], [], [R(nm, 0, V)])
-        if k >= 8:
-            dma(T.yn[:, a:b], T[o[0]][0:128:16, 0:b - a], [], [o])
-    undo(1, "xa", "key", "dl1", None)
+    for nm, a, n in (("dl3", 0, V), ("sp2", V, V), ("rs2", 2 * V, 768)):
+        for c in range(0, n, 1024):
+            e = min(c + 1024, n)
+            lin(R(nm, c, e), IND(R("yw", 0, P2), R("lw16", (a + c) // 16, (a + e) // 16)))
+        dma(T.yn[:, a:a + n], T[nm][0:128:16, 0:n], [], [R(nm, 0, n)])
+    undo(2, "key", "xa", "sp1")
+    undo(1, "xa", "key", None)
 
     for emit in ordered(prog):
         emit()

@@ -9,32 +9,39 @@ KP = 4096.0
 NO = 1216.0
 EO = 2040.0
 
-TU = {"CY": 0.0009, "PCY": 0.00055, "WK": 0.1, "OV": 0.05, "GA": 1.5, "TT": 1.6, "VPEN": 0.8, "EX": 5.0,
-      "PASS": 10}
+TU = {"CY": 0.0009, "PCY": 0.00045, "WK": 0.1, "OV": 0.05, "GA": 1.5, "TT": 1.6, "VPEN": 0.3, "EX": 5.0,
+      "PASS": 8, "SLK": 10.0, "LA": 0.02, "MIX": 1.0, "PB": 1.7, "WB": 0.5, "BK": 10.0, "BL": 0.0, "B3": 0.0,
+      "TRY": [(s, v, m) for s in (3.0, 10.0) for v in (0.2, 0.4) for m in (0.5, 1.0)], "CLIMB": 1500, "STEP": 10.0,
+      "CASES": [(1.0, 1.0, 0.08, 1.0), (0.6, 2.0, 0.1, 1.0), (0.4, 1.0, 0.1, 2.5), (0.4, 1.0, 0.35, 1.3)], "BG": 10.0, "MGC": [], "PG": [], "C3": [0, 1, 2, 3, 4],
+      "HU": [[], [0, 1, 2, 3], [0, 1, 2, 3]], "HC": [], "SC": [32, 64, 128, 192, 256, 304], "PD": 1.5, "BF": 0, "WA": 0, "WC": 0, "WU": 0, "W3": 0}
 PLAN = {}
-KB = {"idn": 0, "blk": 128, "wz": 256, "wq": 400, "rz": 544, "cv0": 688, "cv1": 832, "cv2": 976, "cv3": 1120}
+KB = {"idn": 0, "blk": 128, "wz": 256, "wq": 400, "rz": 544, "cv0": 688, "cv1": 832, "cv2": 976, "cv3": 1120,
+      "pm0": 1264, "pm1": 1408}
 SCRATCH = {}
 for _n, _c, _t in (
-        ("xa", W, "float32"), ("key", W, "float32"), ("yw", P2, "float32"),
-        ("sp1", V, "float32"), ("sp2", V, "float32"), ("dl1", V, "int32"), ("dl2", V, "float32"), ("dl3", V, "float32"),
+        ("wa", W + 2 * V, "float32"), ("wk", W + V, "float32"), ("yw", P2, "float32"),
+        ("sp1", V + 8, "float32"), ("sp2", V + 8, "float32"), ("vim", 128, "float32"), ("sz", 128, "uint16"), ("x0i", V, "int32"), ("vid", 128, "float32"),
+        ("s1", 128, "uint16"), ("s2", 128, "uint16"), ("s3", 128, "uint16"),
         ("ga", 2 * P2, "float16"), ("gb", 2 * P2, "float16"), ("g3", 4 * V, "float16"), ("fw", P2, "bfloat16"),
         ("tk", V, "float16"), ("nm", V, "bfloat16"),
-        ("kb", 1264, "bfloat16"), ("kh", 1264, "float16"), ("neh", 128, "float16"), ("nqh", 128, "float16"),
+        ("kb", 1552, "bfloat16"), ("kh", 1552, "float16"), ("neh", 128, "float16"), ("nqh", 128, "float16"),
         ("rn", 144, "float16"), ("ro", 144, "float16"), ("eh", 144, "float16"),
-        ("un", 1028, "bfloat16"), ("ul", 512, "bfloat16"), ("um", 512, "bfloat16"), ("one", 512, "bfloat16"),
-        ("qr", 128, "bfloat16"), ("mgc", 128, "bfloat16"), ("cw", 128, "bfloat16"), ("pn", 128, "bfloat16"),
+        ("un", 1028, "bfloat16"), ("ul", 512, "bfloat16"), ("one", 512, "bfloat16"),
+        ("mgc", 128, "bfloat16"), ("cw", 128, "bfloat16"), ("pn", 128, "bfloat16"),
         ("bl4", 128, "bfloat16"), ("swd", 128, "float32"), ("nt0", 128, "float32"), ("nt1", 128, "float32"),
         ("nw", 144, "float32"), ("o32", 64, "float32"),
         ("ini", 332, "int32"), ("pci", 8, "int32"), ("col", 48, "float32"), ("th32", 8, "float32"), ("ls", 24, "uint16"),
         ("nxf", 304, "float32"), ("lw16", 304, "uint16"), ("lp", C4, "uint16"), ("pf", C4, "float32"),
-        ("n16", C4, "float16"), ("pid", 512, "float32"), ("dp", 512, "float32"), ("tb", 512, "float32"),
+        ("n16", C4, "float16"), ("pid", 512, "float32"), ("dp", 512, "float32"), ("hc", 128, "bfloat16"),
         ("lw1", 512, "bfloat16"), ("lw2", 512, "bfloat16"), ("lw3", 512, "bfloat16"), ("nmq", 512, "bfloat16"),
         ("hi", 512, "bfloat16"), ("lo", 512, "bfloat16"), ("win", 512, "bfloat16"), ("c01", 512, "bfloat16"),
-        ("ss", 768, "float32"), ("rs1", 768, "float32"), ("rs2", 768, "float32"),
-        ("bs", 3 * GH, "float32"), ("rb1", GH, "float32"), ("rb2", GH, "float32"),
-        ("sg1", GH, "float32"), ("sg2", GH, "float32"), ("bt", 128, "float32")):
+        ("sh", 768, "float16"), ("rs1", 768, "float16"), ("rs2", 768, "float16"), ("ss", GH, "float32"),
+        ("rs3", GH, "float32"), ("bs", 3 * GH, "float32"), ("rb", 768, "float32"),
+        ("sg1", GH, "float32"), ("sg2", GH, "float32"), ("bt", 256, "float32")):
     SCRATCH[_n] = ("sbuf", [128, _c], _t)
-RINGS = {"f": (6, "float32"), "q": (4, "float32"), "t": (6, "float16"), "e": (2, "float16")}
+PART = {"dl3": ("wa", 0), "xa": ("wa", V), "dl1": ("wa", V + W), "key": ("wk", 0), "dl2": ("wk", W)}
+SCRATCH["fr"] = ("sbuf", [128, 3072], "float32")
+RINGS = { "t": (6, "float16"), "e": (2, "float16")}
 for _r in RINGS:
     for _k in range(RINGS[_r][0]):
         SCRATCH["%s%d" % (_r, _k)] = ("sbuf", [128, 512], RINGS[_r][1])
@@ -50,7 +57,8 @@ POOL = {"size": [4, 5], "diff": [5, 6], "own": [4, 5, 6], "flat": [0, 1, 2, 3], 
 
 
 def R(name, a, b, s=1):
-    return (name, a, b, s)
+    name, o = PART.get(name, (name, 0))
+    return (name, o + a, o + b, s)
 
 
 def IND(win, off):
@@ -88,47 +96,79 @@ def ordered(prog):
     dur = [min(v[1] for v in p[0]) + (p[3] or 0.0) for p in prog]
     tail = [0.0] * n
     for i in range(n - 1, -1, -1):
-        tail[i] = prog[i][4] + dur[i] + max([tail[j] + WK for j in succs[i]] or [0.0])
+        tail[i] = dur[i] + max([tail[j] + WK for j in succs[i]] or [0.0])
     lat = [p[3] or 0.0 for p in prog]
 
-    def place(order, before, back):
-        busy, end, pick = {}, [0.0] * n, [0] * n
-        for i in order:
-            r = max([end[j] + WK + (0.0 if back else lat[j]) for j in before[i]] or [0.0]) + (lat[i] if back else 0.0)
+    def replay(seq, pick, pe, wk, ex):
+        free, end = {e: 0.0 for e in "vstgy"}, [0.0] * n
+        for i in seq:
+            e, t = prog[i][0][pick[i]][:2]
+            r = max([end[j] for j in preds[i]] or [0.0])
+            if e != "a":
+                r = free[e] = max(r, free[e]) + (t * pe if e == "t" else t)
+            end[i] = r + wk + lat[i] * ex
+        return max(end)
+
+    def worth(seq, pick):
+        return sum(c[0] * replay(seq, pick, *c[1:]) for c in TU["CASES"])
+
+    def run(key, before, after, back):
+        left = [len(p) for p in before]
+        at = [lat[i] if back else 0.0 for i in range(n)]
+        ready = [i for i in range(n) if not left[i]]
+        free, end, pick, seq = {e: 0.0 for e in "vstgya"}, [0.0] * n, [0] * n, []
+        while ready:
             best = None
-            for k, v in enumerate(prog[i][0]):
-                t, at = r, 0
-                if v[0] != "a":
-                    iv = busy.setdefault(v[0], [])
-                    lo, hi = 0, len(iv)
-                    while lo < hi:
-                        mid = (lo + hi) // 2
-                        if iv[mid][1] <= r:
-                            lo = mid + 1
-                        else:
-                            hi = mid
-                    at = lo
-                    while at < len(iv) and iv[at][0] < t + v[1]:
-                        t = max(t, iv[at][1])
-                        at += 1
-                c = t + v[1] + (TU["VPEN"] if v[0] == "v" else 0.0)
-                if best is None or c < best[0]:
-                    best = (c, k, t, at)
-            _, k, t, at = best
+            t0 = min(max(at[i], min(free[v[0]] for v in prog[i][0])) for i in ready)
+            for i in ready:
+                for k, v in enumerate(prog[i][0]):
+                    t = max(at[i], free[v[0]])
+                    c = key[i] + (TU["SLK"] if v[0] == "v" and len(prog[i][0]) > 1 else 0.0)
+                    if t <= t0 + TU["LA"] and (best is None or (c, t) < best[0]):
+                        best = ((c, t), i, k, t)
+            _, i, k, t = best
             v = prog[i][0][k]
+            if len(prog[i][0]) > 1 and v[0] == "v":
+                v2 = prog[i][0][0]
+                t2 = max(at[i], free["s"])
+                if t2 + v2[1] < t + v[1] + TU["VPEN"]:
+                    k, v, t = 0, v2, t2
             if v[0] != "a":
-                busy[v[0]].insert(at, (t, t + v[1]))
+                free[v[0]] = t + v[1]
             end[i], pick[i] = t + v[1], k
-        return end, pick
+            ready.remove(i)
+            seq.append(i)
+            for j in after[i]:
+                at[j] = max(at[j], end[i] + WK + (lat[j] if back else lat[i]))
+                left[j] -= 1
+                if not left[j]:
+                    ready.append(j)
+        return end, pick, seq
     if n not in PLAN:
-        order = sorted(range(n), key=lambda i: (-tail[i], i))
-        for _ in range(TU["PASS"]):
-            end, pick = place(order, preds, False)
-            span = max(end[i] + lat[i] for i in range(n))
-            if n not in PLAN or span < PLAN[n][0]:
-                PLAN[n] = (span, sorted(range(n), key=lambda i: (end[i] - prog[i][0][pick[i]][1], end[i], i)), pick)
-            end, pick = place(sorted(range(n), key=lambda i: (-end[i] - lat[i], -i)), succs, True)
-            order = sorted(range(n), key=lambda i: (-end[i], i))
+        for TU["SLK"], TU["VPEN"], mix in TU["TRY"]:
+            key = [-tail[i] - prog[i][4] for i in range(n)]
+            for _ in range(TU["PASS"]):
+                end, pick, seq = run(key, preds, succs, False)
+                span = worth(seq, pick)
+                if n not in PLAN or span < PLAN[n][0]:
+                    PLAN[n] = (span, seq, pick, key, TU["SLK"], TU["VPEN"])
+                end = run([-end[i] - lat[i] for i in range(n)], succs, preds, True)[0]
+                key = [(1 - mix) * key[i] - mix * (end[i] + prog[i][4]) for i in range(n)]
+        seed = [1]
+
+        def draw():
+            seed[0] = (seed[0] * 1103515245 + 12345) % 2147483648
+            return seed[0] / 2147483648.0
+        TU["SLK"], TU["VPEN"] = PLAN[n][4:]
+        for _ in range(TU["CLIMB"]):
+            key = list(PLAN[n][3])
+            a, w, d = int(draw() * n), 3 + int(draw() * 37), (2 * draw() - 1) * TU["STEP"]
+            for i in range(a, min(n, a + w)):
+                key[i] += d
+            end, pick, seq = run(key, preds, succs, False)
+            span = worth(seq, pick)
+            if span <= PLAN[n][0]:
+                PLAN[n] = (span, seq, pick, key) + PLAN[n][4:]
     return [prog[i][0][PLAN[n][2][i]][2] for i in PLAN[n][1]]
 
 
@@ -146,6 +186,7 @@ def rank_program(g, core, T, topo):
     acc = {}
     prog = []
     ndma, local, arrived = [0], [0], {}
+    slow = [1.0]
     first = [0.0]
 
     def ap(v):
@@ -214,15 +255,16 @@ def rank_program(g, core, T, topo):
 
     def vtt(o, a, b, f):
         op([o], [a, b], ("v", [lambda: g.vector.tensor_tensor(ap(o), ap(a), ap(b), f)],
-                         CY * max(64, num(b) * (1 if a[0] in PSUMS or b[0] in PSUMS else TU["TT"] if a[0] == "ind" else 2))))
+                         CY * max(64, num(b) * (3.8 if o[0] == "ind" else 1 if a[0] in PSUMS or b[0] in PSUMS else TU["TT"] if a[0] == "ind" else 2))))
 
     def vts(o, a, s1, f1, s2=None, f2=None):
         x1, x2 = [ap(s) if isinstance(s, tuple) else s for s in (s1, s2)]
         cols = [s for s in (s1, s2) if isinstance(s, tuple)]
+        t = GA * CY * num(a) if a[0] == "ind" else tm(num(a), o, a)
         if f2 is None:
-            op([o], [a] + cols, ("v", [lambda: g.vector.tensor_scalar(ap(o), ap(a), x1, None, f1)], tm(num(a), o, a)))
+            op([o], [a] + cols, ("v", [lambda: g.vector.tensor_scalar(ap(o), ap(a), x1, None, f1)], t))
         else:
-            op([o], [a] + cols, ("v", [lambda: g.vector.tensor_scalar(ap(o), ap(a), x1, x2, f1, f2)], tm(num(a), o, a)))
+            op([o], [a] + cols, ("v", [lambda: g.vector.tensor_scalar(ap(o), ap(a), x1, x2, f1, f2)], t))
 
     def vset(o, c):
         op([o], [], ("v", [lambda: g.vector.memset(ap(o), c)], tm(num(o), o)))
@@ -269,7 +311,7 @@ def rank_program(g, core, T, topo):
         op([o], [x for t in terms for x in t if isinstance(x, tuple)] + list(more),
            ("t", [lambda k=k: g.tensor.matmul(ap(o), ap(lhs(terms[k])), ap(terms[k][1]), start and k == 0,
                                               stop and k == n - 1) for k in range(n)],
-            sum(max(64, num(t[1])) * (4 if SCRATCH[t[1][0]][2] == "float32" else 1) + 25 for t in terms) * PCY))
+            sum(max(64, num(t[1])) * (4 if SCRATCH[t[1][0]][2] == "float32" else 1) + 25 for t in terms) * PCY * slow[0]))
 
     def asel(o, i, pat, cmp, base, cm):
         op([o], [i], ("g", [lambda: g.affine_select(ap(o), ap(i), pat, cmp, 0.0, base, cm)], 0.17 + 2 * CY * num(o)))
@@ -303,18 +345,17 @@ def rank_program(g, core, T, topo):
                 res[c] = [e for e in topo.engines(src, c) if e not in pool]
         return res
 
-    def send(to, pieces, sems, ins, guard=()):
+    def send(to, piece, sems, guard=()):
         m = split(core, [to[d] for d in (1, 2, 3)])
-        tr = []
+        sn, sc, dn, dc, w = piece
+        tr, ins = [], [R(sn, sc, sc + 3 * w)]
         for d in (1, 2, 3):
             rid, pid, _ = topo.addr(to[d])
-            n = len(m[to[d]]) // len(pieces)
-            for k, (sn, sc, dn, dc) in enumerate(pieces):
-                c = (d - 1) * B
-                tr.append(RemoteDMATransfer(
-                    dst_ids=[DstId(rid=rid, pnc=pid)], dma_engine_mask=sum(1 << e for e in m[to[d]][k * n:(k + 1) * n]),
-                    remote_sem=T.sem[sems + str(d)], src=T[sn][:, sc + c:sc + c + B], dst=T[dn][:, dc + c:dc + c + B]))
-                local[0] += n
+            c = (d - 1) * w
+            tr.append(RemoteDMATransfer(
+                dst_ids=[DstId(rid=rid, pnc=pid)], dma_engine_mask=sum(1 << e for e in m[to[d]]),
+                remote_sem=T.sem[sems + str(d)], src=ap(R(sn, sc + c, sc + c + w)), dst=ap(R(dn, dc + c, dc + c + w))))
+            local[0] += len(m[to[d]])
         guard = list(guard)
 
         def emit():
@@ -322,13 +363,13 @@ def rank_program(g, core, T, topo):
             g.remote_dma_fused(tr, local_sem=T.sem["loc"])
         prog.append(([("g", 1.0, emit)], guard + [("sent" + sems, 0, 1, 1)], ins, None, first[0]))
 
-    def recv(sems, frm, pieces):
+    def recv(sems, frm, piece):
         for d in (1, 2, 3):
             r = T.rank_of(frm[d])
             s = 1 if frm is homes else -1
-            n = len(split(frm[d], [T.cores[(r + s * j) % N] for j in (1, 2, 3)])[core]) // len(pieces) * len(pieces)
-            c = (d - 1) * B
-            ro = [R(nm, cc + c, cc + c + B) for nm, cc in pieces]
+            n = len(split(frm[d], [T.cores[(r + s * j) % N] for j in (1, 2, 3)])[core])
+            nm, cc, w = piece
+            ro = [R(nm, cc + (d - 1) * w, cc + d * w)]
             arrived[sems + str(d)] = n
             prog.append(([("a", 0.0, lambda d=d, n=n, ro=ro: note(None, sems + str(d), n, ro, []))],
                          ro, [("sent" + sems, 0, 1, 1)], TU["EX"], 0.0))
@@ -340,7 +381,13 @@ def rank_program(g, core, T, topo):
         return R("%s%d" % (c, turn[c]), 0, n)
 
     def F(n=512):
-        return ring("f", n)
+        k = turn.get("f", 0)
+        k = (k + k % 2 if n > 512 else k) % 6
+        turn["f"] = k + (n + 511) // 512
+        return R("fr", 512 * k, 512 * k + n)
+
+    def wide(k, on):
+        return [k] if k == 4 or not on else [] if k % 2 else [5 + k // 2]
 
     def mask():
         turn["m"] = (turn.get("m", 0) + 1) % 4
@@ -350,7 +397,7 @@ def rank_program(g, core, T, topo):
         turn[pool] = (turn.get(pool, -1) + 1) % len(POOL[pool])
         return R("p%d" % POOL[pool][turn[pool]], 0, n)
 
-    CH = [(512 * k, 512 * k + 512) for k in range(4)] + [(V, W)]
+    CH = [(512 * k, 512 * k + 512) for k in range(4)] + [(V, W), (0, 1024), (1024, V)]
     LSB = {d: R("ls", 8 * (d - 1), 8 * d) for d in (1, 2, 3)}
     LSA = R("ls", 0, 24)
     THR = R("th32", 0, 1)
@@ -371,7 +418,7 @@ def rank_program(g, core, T, topo):
 
     def pc(n, t, k):
         a, b = CH[k]
-        o = V * t if k < 4 else 3 * V + GH * t
+        o = V * t if k != 4 else 3 * V + GH * t
         return R(n, o + a, o + b)
 
     def every(n, j):
@@ -390,20 +437,27 @@ def rank_program(g, core, T, topo):
                    [(shifted("cv%d" % t, 4 * b), R("n16", b, C4, 4)) for b in range(4)])
             vts(R("l%d" % l, 304 * pr, 304 * pr + 304), R(bank, 0, 304), NO, OP.add)
 
-    def tables(parts, ports):
-        nodes([p[:3] for p in parts])
+    def tables(parts, ports, halves=True):
+        nodes([p[:3] for p in parts] * halves)
         for pb, a, s, own in parts:
             e = a + (own - 1) * s + 1
             lin(R("pf", a, a + 303 * s + 1, s), pb)
-            vtt(R("dp", a, e, s), R(pb[0], 0, own), R("pid", a, e, s), OP.subtract)
+            vtt(R("dp", a, e, s), R("pid", a, e, s), R(pb[0], 0, own), OP.subtract)
         if ports:
             vts(R("lp", 0, C4), R("pf", 0, C4), 0.5, OP.add)
-        vts(R("tb", 0, 512), R("dp", 0, 512), -1.0, OP.mult, CTB, OP.add)
 
-    def chain(l, k, win, q, bias=0.0):
+    def chain(l, k, win, q, bias=0.0, bank=None):
         lin(q, IND(win, lst(l, 0, k)), bias=bias)
-        for t in (1, 2, 3):
-            vtt(q, IND(win, lst(l, t, k)), q, OP.add)
+        if bank is None:
+            for t in (1, 2, 3):
+                vtt(q, IND(win, lst(l, t, k)), q, OP.add)
+            return
+        h = F(num(q))
+        lin(h, IND(win, lst(l, 2, k)))
+        vtt(h, IND(win, lst(l, 3, k)), h, OP.add)
+        vtt(q, IND(win, lst(l, 1, k)), q, OP.add)
+        sact(bank, h)
+        vtt(q, bank, q, OP.add)
 
     def flat(mat, src, pool, use):
         for j in range(4):
@@ -414,7 +468,7 @@ def rank_program(g, core, T, topo):
     dma(T.ini[:, 0:304], T.nxt[:], [R("ini", 0, 304)], [], 2.2)
     dma(T.ini[:, 304:328], T.shw[:], [R("ini", 304, 328)], [], 2.2)
     for k in range(2):
-        dma(T.dl1[:, 1024 * k:1024 * k + 1024], T.x0[:, 1024 * k:1024 * k + 1024], [R("dl1", 1024 * k, 1024 * k + 1024)], [],
+        dma(T.x0i[:, 1024 * k:1024 * k + 1024], T.x0[:, 1024 * k:1024 * k + 1024], [R("x0i", 1024 * k, 1024 * k + 1024)], [],
             4.0)
     dma(T.ini[:, 328:329], T.th[:], [R("ini", 328, 329)], [])
     iota(R("pci", 0, 1), [[0, 1]], 0, 1)
@@ -436,19 +490,18 @@ def rank_program(g, core, T, topo):
     first[0] = 100.0
     vcopy(LSA, R("ini", 304, 328))
     for k in range(2):
-        vts(R("xa", 1024 * k, 1024 * k + 1024), R("dl1", 1024 * k, 1024 * k + 1024), -MG, OP.add)
+        vts(R("xa", 1024 * k, 1024 * k + 1024), R("x0i", 1024 * k, 1024 * k + 1024), -MG, OP.add)
     sact(R("bs", 0, GH), IND(R("xa", 0, V), LSA))
-    send(peers, [("bs", 0, "xa", V)], "ax1_", [R("bs", 0, GH)])
-    recv("ax1_", homes, [("xa", V)])
+    send(peers, ("bs", 0, "xa", V, B), "ax1_")
+    recv("ax1_", homes, ("xa", V, B))
     first[0] = 0.0
-    for a, b in ((0, 64), (64, 128), (128, 256), (256, 304)):
+    for a, b in zip([0] + TU["SC"], TU["SC"]):
         vcopy(IND(R("fw", 0, P2), R("lw16", a, b)), R("g3", 16 * a, 16 * b))
     vset(ONE, 1.0)
     vset(R("o32", 0, 64), 1.0)
-    vset(R("kb", 256, 1264), 0.0)
+    vset(R("kb", 256, 1552), 0.0)
     vset(R("un", 0, 1028), 0.0)
     vset(R("nw", 0, 144), 0.0)
-    vset(M("qr"), 3.0 / 1024.0)
     vset(M("mgc"), MG / 128.0)
     o128, o64, o8 = R("one", 0, 128), R("o32", 0, 64), R("one", 0, 8)
     for c in (0, 1):
@@ -457,6 +510,9 @@ def rank_program(g, core, T, topo):
     for t in range(4):
         asel(shifted("cv%d" % t, 0, "kb"), o128, [[-16, 8], [1000, 4], [-4, 4]], OP.is_equal, -t, 1)
     lin(R("kh", KB["cv0"], 1264), R("kb", KB["cv0"], 1264))
+    for h in (0, 1):
+        asel(shifted("pm%d" % h, 0, "kb"), o128, [[-16, 8], [1000, 2], [-2, 8]], OP.is_equal, -h, 1)
+    lin(R("kh", 1264, 1552), R("kb", 1264, 1552))
     asel(M("idn", "kb"), o128, [[-1, 128]], OP.is_equal, 0, 1)
     for n, lo in (("wz", 0), ("wq", 2)):
         o = R("kb", KB[n] + 16, KB[n] + 144, 16)
@@ -473,7 +529,13 @@ def rank_program(g, core, T, topo):
     asel(M("bl4"), o128, [[-4, 32], [0, 4]], OP.is_ge, 0, 1)
     asel(M("bl4"), M("bl4"), [[4, 32], [0, 4]], OP.is_ge, 3, -1)
     asel(R("ul", 0, 512), ONE, [[-4, 4], [-16, 8], [0, 16]], OP.is_equal, 0, 1)
-    sact(R("um", 0, 512), R("ul", 0, 512), scale=MG)
+    iota(R("vid", 0, 128), [[16, 128]], 0, 0)
+    vts(R("pci", 3, 4), R("pci", 0, 1), 15, OP.bitwise_and)
+    vcopy(R("col", 44, 45), R("pci", 3, 4))
+    sact(R("vid", 0, 128), R("vid", 0, 128), AF.Identity, bias=R("col", 44, 45))
+    lin(R("vim", 0, 128), R("vid", 0, 128), bias=-float(V))
+    for n in ("sp1", "sp2"):
+        vset(R(n, V, V + 8), 0.0)
     for s in (0, 1):
         asel(R("un", 4 + 2 * s, 1028, 16), R("one", 0, 64), [[-4, 4], [-1, 2], [-16, 8]], OP.is_equal, -2 * s, 1)
     for h in (0, 1):
@@ -484,21 +546,25 @@ def rank_program(g, core, T, topo):
     vts(R("pci", 2, 3), R("pci", 0, 1), 2, OP.arith_shift_right, 3, OP.bitwise_and)
     vts(CPID, R("pci", 2, 3), 2.0, OP.mult, -0.5, OP.add)
     vts(CPID, CPID, ODD, OP.add)
-    vts(CTB, ODD, -1.0, OP.mult, 1.5, OP.add)
+    vts(CTB, ODD, -1.0, OP.mult, -1.0, OP.add)
+    vts(M("hc"), M("swd"), 0.0, OP.max, CTB, OP.mult)
+    vtt(M("cw"), M("cw"), M("hc"), OP.add)
     sact(R("pid", 0, 512), R("pid", 0, 512), AF.Identity, bias=CPID)
     vcopy(THR, R("ini", 328, 329))
     iota(R("yw", 4096, P2), [[1, 768]], 4096, 0)
 
-    for c in (0, 1):
-        mm(R("p%d" % (4 + c), 0, 304), [(M("nt%d" % c), R("nxf", 0, 304))])
-    nodes([(R("p%d" % (4 + c), 0, 304), c, 2) for c in (0, 1)])
-    node_lists(1, [(0, "p6")])
-    for k in range(5):
+    vts(R("ini", 0, 304), R("ini", 0, 304), 1, OP.arith_shift_right)
+    vts(R("n16", 0, 304), R("ini", 0, 304), -NO, OP.add)
+    for h in (0, 1):
+        mm(R("p6", 152 * h, 152 * h + 152), [(shifted("pm%d" % h, 8 * c), R("n16", c, 304, 2)) for c in (0, 1)])
+    vts(R("l1", 0, 304), R("p6", 0, 304), NO, OP.add)
+    for k in (5, 6, 4):
         for t in (0, 1):
             lin(pc("ga", t, k), IND(XA, lst(1, t, k)), bias=MG)
     for c in (0, 1):
-        mm(R("p%d" % (4 + c), 0, 304), [(M("nt%d" % c), R("nxf", 0, 304))] +
-           [(shifted("wq", 2 + 4 * (i // 2) + i % 2, "kb"), R("fw", 8 * c + i, P2, 16)) for i in range(8)])
+        mm(R("p%d" % (4 + c), 0, 304), [(M("nt%d" % c), R("nxf", 0, 304))], stop=False)
+        mm(R("p%d" % (4 + c), 0, 304),
+           [(shifted("wq", 2 + 4 * (i // 2) + i % 2, "kb"), R("fw", 8 * c + i, P2, 16)) for i in range(8)], start=False)
     tables([(R("p%d" % (4 + c), 0, 304), c, 2, 256) for c in (0, 1)], True)
     node_lists(1, [(1, "p6")])
     lin(R("fw", 4096, P2), R("g3", 4096, P2))
@@ -513,22 +579,24 @@ def rank_program(g, core, T, topo):
         srcs = ["ga"] if l < 3 else ["ga", "gb"]
         gk = "gb" if l < 3 else "g3"
         LW = R("lw%d" % l, 0, 512)
-        dl, p0 = "dl%d" % l, "sp%d" % l if l < 3 else "yw"
+        dl, p0 = "dl%d" % l, "sp%d" % l if l < 3 else "x0i"
         zb, tk = {}, {}
 
         def gathers(k):
             a, b = CH[k]
             n = b - a
-            for t in range(4):
-                if l > 1 or t > 1:
-                    lin(pc("ga", t, k), IND(XA, lst(l, t, k)), bias=MG)
-            if l == 3:
+            for c in wide(k, TU["WA"]):
                 for t in range(4):
-                    lin(pc("gb", t, k), IND(R("fw", 0, W), lst(l, t, k)), bias=-0.375)
+                    if l < 3 and t == 2:
+                        vts(pc("ga", t, c), IND(XA, lst(l, t, c)), MG, OP.add, -1.5, OP.add)
+                    elif l > 1 or t > 1:
+                        lin(pc("ga", t, c), IND(XA, lst(l, t, c)), bias=MG)
+                    if l == 3:
+                        lin(pc("gb", t, c), IND(R("fw", 0, W), lst(l, t, c)), bias=-0.375)
             zb[k] = R("p%d" % k, 0, n)
             one = R("one", 0, n)
-            mm(zb[k], [(NQ, pc(s, t, k)) for s in srcs for t in (0, 1)] + ([(M("qr"), one)] if l < 3 else []), stop=False)
-            mm(zb[k], [(NQ, pc(s, t, k)) for s in srcs for t in (2, 3)] + [(M("mgc"), one)], start=False)
+            mm(zb[k], [(NQ, pc(s, t, k)) for s in srcs for t in (0, 1)], stop=False)
+            mm(zb[k], [(NQ, pc(s, t, k)) for s in srcs for t in (2, 3)] + [(M("mgc"), one)] * (k < 4 and l in TU["MGC"]), start=False)
             vtt(zb[k], zb[k], R("xa", a, b), OP.add)
 
         def sized(k):
@@ -537,7 +605,9 @@ def rank_program(g, core, T, topo):
             t = e = tk[k] = R("tk", a, b) if k < 4 else ring("t", n)
             if l > 1:
                 e = ring("e", n) if l == 2 else F(n)
-            sact(e, zb[k], AF.Abs)
+            sact(e, zb[k], AF.Abs, bias=0.0 if k < 4 and l in TU["MGC"] else MG)
+            if k < 4 and l not in TU["MGC"]:
+                lin(zb[k], zb[k], bias=MG)
             if l > 1:
                 vts(t, e, 255.0, OP.min)
             o = PQ("size", n) if k < 4 else R("p5", 0, n)
@@ -549,18 +619,14 @@ def rank_program(g, core, T, topo):
 
         def detail(k):
             a, b = CH[k]
-            d, m, q = zb[k], tk[k], F()
+            d, m, q = zb[k], tk[k], R("x0i", a, b)
             vtt(R(dl, a, b), d, m, OP.mult)
-            if l < 3:
-                w = F()
-                lin(w, m, bias=KP)
-                lin(q, d, 0.25, -0.375)
-                vts(d, q, MG, OP.add, -MG, OP.add)
-                vtt(R(p0, a, b), d, w, OP.mult)
-            else:
+            if l == 3:
                 vtt(d, d, R(dl, a, b), OP.subtract)
-                lin(q, d, 0.25, -0.375)
-                vts(R(p0, a, b), q, MG, OP.add, -MG, OP.add)
+            vts(q, d, 0.25, OP.mult, -0.375, OP.add)
+            if l < 3:
+                lin(d, m, bias=KP)
+                vtt(R(p0, a, b), d, q, OP.mult)
 
         def chosen():
             for t in range(4):
@@ -571,30 +637,33 @@ def rank_program(g, core, T, topo):
                [(shifted("ro", 4 * j), every("tk", j)) for j in range(4)], stop=False)
             for t in range(4):
                 mm(o, [(shifted("eh", 4 * j + t), R(gk, V * t + j, V * t + V, 4)) for j in range(4)], False, t == 3)
-            vtt(R("win", 0, 512), o, R("tb", 0, 512), OP.is_gt)
+            vtt(R("win", 0, 512), o, R("dp", 0, 512), OP.is_ge)
             mm(o, [(M("bl4"), R("win", 0, 512))])
             lin(LW, o, bias=-3.0, relu=True)
 
         def likeness(k):
             terms = []
+            first[0] = TU["BL"] if l < 3 else TU["B3"]
             for x, y in ((0, 0), (1, 1), (0, 1), (1, 0)):
                 u, tn, sign = PQ("diff"), ring("t"), [1]
                 mm(u, [(I1, pc(s, 2 + x, k)) for s in srcs] + [(NI, pc(s, y, k)) for s in srcs])
+                shift = 1.5 if l < 3 and x == 0 else 0.0
                 if l == 1:
-                    lin(tn, u, relu=True)
+                    lin(tn, u, bias=shift, relu=True)
                 else:
-                    sact(tn, u, AF.Abs)
+                    sact(tn, u, AF.Abs, bias=shift)
                     cut(tn, sign)
                 terms += [(lambda j=j, sign=sign, same=x == y: shifted("rz" if same == (sign[0] > 0) else "rn", 4 * j),
                            R(tn[0], j, 512, 4)) for j in range(4)]
             mm(R("p7", 128 * k, 128 * k + 128), terms, more=[R("kh", KB["rz"], KB["rz"] + 144), R("rn", 0, 144)])
+            first[0] = 0.0
 
         def links():
             o, c = R("p7", 0, 512), R("c01", 0, 512)
             vts(c, o, 0.0, OP.is_gt)
             mm(o, [(M("swd"), R("pf", 0, 512))])
             vtt(o, o, c, OP.mult)
-            vtt(o, o, R("dp", 0, 512), OP.add)
+            vtt(o, o, R("dp", 0, 512), OP.subtract)
             vtt(o, o, LW, OP.mult)
             vtt(o, o, R("pid", 0, 512), OP.add)
             lin(R("hi", 0, 512), o)
@@ -616,30 +685,49 @@ def rank_program(g, core, T, topo):
             if l < 3:
                 b1, b2 = PQ("own"), PQ("own")
                 s = R("sp%d" % l, a, b)
-                chain(l, k, KEY, s)
+                for c in wide(k, TU["WC"]):
+                    chain(l, c, KEY, R("sp%d" % l, *CH[c]), 0.0, b1 if k in TU["HC"] else None)
                 z = F()
                 lin(z, s, bias=MG * KP)
                 lin(b1, z, 1.0 / KP, -MG)
                 lin(b2, z, bias=-MG * KP)
                 vtt(x, b1, x, OP.add)
                 vtt(s, s, b2, OP.subtract)
+            elif k not in TU["C3"]:
+                q = F(b - a) if k < 4 else R("ss", 0, GH)
+                chain(l, k, KEY, q, MG if k < 4 else 0.0)
+                if k < 4:
+                    vtt(x, q, x, OP.add)
             else:
-                q = ring("q")
-                for t in range(4):
-                    vtt(q if t < 3 else x, IND(KEY, lst(l, t, k)), q if t else x, OP.add)
+                o = PQ("flat", b - a)
+                gs = [R("g3", V * t + a, V * t + b) if k < 4 else ring("t", GH) for t in range(4)]
+                for c in wide(k, TU["W3"]):
+                    for t in range(4):
+                        lin(gs[t] if k == 4 else pc("g3", t, c), IND(KEY, lst(l, t, c)))
+                mm(o, [(I1, s) for s in gs] + ([(M("mgc"), ONE)] if k < 4 else []))
+                if k < 4:
+                    vtt(x, o, x, OP.add)
+                else:
+                    lin(R("ss", 0, GH), o)
 
         def border(buf, rc):
             for d in (1, 2, 3):
-                c = rc + (d - 1) * B
-                vtt(R("bt", 0, 128), IND(R(buf, 0, V), LSB[d]), R(rs, c, c + B), OP.add)
-                vcopy(IND(R(buf, 0, V), LSB[d]), R("bt", 0, 128))
+                s, bt = 2 if l < 3 else 1, R("bt", B * rc, B * rc + B)
+                vtt(bt, IND(R(buf, 0, V), LSB[d]), R(rs, rc + (d - 1) * s * B, d * s * B, s), OP.add)
+                vcopy(IND(R(buf, 0, V), LSB[d]), bt)
 
         def kept():
-            def use(j, u):
-                vtt(every(dl, j), u, every(dl, j), OP.add)
-                if l < 3:
-                    vtt(every("sp%d" % l, j), u, every("sp%d" % l, j), OP.add)
-            flat("um", LW[0], "kept", use)
+            o, s = PQ("kept", 128), F(128)
+            mm(o, [(shifted("cv0", 4 * b, "kb"), R(LW[0], b, 512, 4)) for b in range(4)])
+            if l in TU["PG"]:
+                s2 = F(128)
+                vtt(s2, o, R("vim", 0, 128), OP.mult)
+                vts(R("sz", 0, 128), s2, float(V), OP.add)
+                for a in range(0, 128, 32):
+                    lin(R("key", 16 * a, 16 * a + 512), IND(R(p0, 0, V + 8), R("sz", a, a + 32)))
+            lin(o, o, float(W if l < 3 else -V), float(0 if l < 3 else V))
+            vtt(s, o, R("vid", 0, 128), OP.add)
+            vcopy(R("s%d" % l, 0, 128), s)
 
         if l == 3:
             for k in range(5):
@@ -658,34 +746,42 @@ def rank_program(g, core, T, topo):
             for k in range(4):
                 likeness(k)
         vset(R("key", V, W), 0.0)
-        flat("ul", LW[0], "flat", lambda j, u: vtt(every("key", j), u, every(p0, j), OP.mult))
-        rs = "rs2" if l == 2 else "rs1"
+        if l in TU["PG"]:
+            kept()
+        else:
+            flat("ul", LW[0], "flat", lambda j, u: vtt(every("key", j), u, every(p0, j), OP.mult))
+        rs = "rs%d" % l
         xg = [R("xa", V, W)]
         if l < 3:
             q, z, b4 = F(GH), F(GH), PQ("own", GH)
+            first[0] = TU["BG"]
             chain(l, 4, KEY, q)
             lin(z, q, bias=MG * KP)
             lin(b4, z, bias=-MG * KP)
-            lin(R("ss", 0, GH), z, 1.0 / KP, -MG)
-            vtt(R("ss", GH, 768), q, b4, OP.subtract)
-            send(homes, [("ss", 0, rs, 0), ("ss", GH, rs, GH)], "as%d_" % l, [R("ss", 0, 768)], xg)
-            recv("as%d_" % l, peers, [(rs, 0), (rs, GH)])
+            lin(R("sh", 0, 768, 2), z, 1.0 / KP, -MG)
+            vtt(R("sh", 1, 768, 2), q, b4, OP.subtract)
+            send(homes, ("sh", 0, rs, 0, 2 * B), "as%d_" % l, xg)
+            first[0] = 0.0
+            recv("as%d_" % l, peers, (rs, 0, 2 * B))
+            first[0] = TU["BK"]
             links()
             unwrap("flat")
+            first[0] = 0.0
             for k in range(4):
                 own(k)
             border("xa", 0)
             sact(R("bs", 0, GH), IND(R("xa", 0, V), LSA))
-            send(peers, [("bs", 0, "xa", V)], "ax%d_" % (l + 1), [R("bs", 0, GH)], [R("rs1", 0, 768)] if l == 2 else [])
-            recv("ax%d_" % (l + 1), homes, [("xa", V)])
+            send(peers, ("bs", 0, "xa", V, B), "ax%d_" % (l + 1))
+            recv("ax%d_" % (l + 1), homes, ("xa", V, B))
             for k in range(8):
                 lin(R("gb", 1216 * k, 1216 * k + 1216), IND(R("fw", 0, P2), R("lp", 76 * k, 76 * k + 76)))
             for hf in (0, 1):
                 mm(R("p%d" % hf, 0, 304), [(shifted("wz" if i % 4 < 2 else "wq", i), R("gb", P2 * hf + i, P2 * hf + P2, 16))
                                           for i in range(16)])
-            border("sp%d" % l, GH)
+            border("sp%d" % l, 1)
             sact(R("sg%d" % l, 0, GH), IND(R("sp%d" % l, 0, V), LSA))
-            kept()
+            if l not in TU["PG"]:
+                kept()
             tables([(R("p0", 0, 304), 0, 1, 304), (R("p1", 0, 304), 304, 1, 208)], l < 2)
             node_lists(l + 1, [(0, "p2"), (1, "p3")])
             if l == 2:
@@ -693,23 +789,22 @@ def rank_program(g, core, T, topo):
                 mm(bk, [(shifted("nw", 8 * c), R("pf", c, C4, 2)) for c in (0, 1)])
                 vts(R("lw16", 0, 304), bk, 0.5, OP.add)
         else:
-            chain(l, 4, KEY, R("ss", 0, GH))
-            send(homes, [("ss", 0, rs, 0)], "as3_", [R("ss", 0, GH)], xg)
-            recv("as3_", peers, [(rs, 0)])
-            lin(R("win", 0, 512), LW, -1.0, 1.0)
-            flat("um", "win", "flat", lambda j, u: vtt(every("xa", j), u, every("xa", j), OP.add))
+            own(4)
+            send(homes, ("ss", 0, rs, 0, B), "as3_", xg)
+            recv("as3_", peers, (rs, 0, B))
             for k in range(4):
                 own(k)
             border("xa", 0)
             sact(R("bs", 0, GH), IND(R("xa", 0, V), LSA))
-            vtt(R("bs", GH, 2 * GH), R("bs", 0, GH), R("sg2", 0, GH), OP.subtract)
-            vtt(R("bs", 2 * GH, 3 * GH), R("bs", GH, 2 * GH), R("sg1", 0, GH), OP.subtract)
-            send(peers, [("bs", 0, "xa", V)], "ab3_", [R("bs", 0, GH)])
-            send(peers, [("bs", GH, "rb2", 0), ("bs", 2 * GH, "rb1", 0)], "ab2_", [R("bs", GH, 3 * GH)])
-            recv("ab3_", homes, [("xa", V)])
-            recv("ab2_", homes, [("rb2", 0), ("rb1", 0)])
-            flat("um", LW[0], "flat", lambda j, u: vtt(every(dl, j), u, every(dl, j), OP.add))
-            sact(R("key", V, W), R("rb2", 0, GH))
+            vtt(R("bs", GH, 3 * GH, 2), R("bs", 0, GH), R("sg2", 0, GH), OP.subtract)
+            vtt(R("bs", GH + 1, 3 * GH, 2), R("bs", GH, 3 * GH, 2), R("sg1", 0, GH), OP.subtract)
+            send(peers, ("bs", 0, "xa", V, B), "ab3_")
+            send(peers, ("bs", GH, "rb", 0, 2 * B), "ab2_")
+            recv("ab3_", homes, ("xa", V, B))
+            recv("ab2_", homes, ("rb", 0, 2 * B))
+            kept()
+            lin(R("key", V, W), R("rb", 0, 768, 2))
+            slow[0] = TU["PD"]
             for k in range(4):
                 likeness(k)
             links()
@@ -718,24 +813,30 @@ def rank_program(g, core, T, topo):
     def undo(l, src, dst, sp):
         for k in range(4):
             a, b = CH[k]
-            z, y = ring("q"), PQ("undo")
-            chain(l, k, R(src, 0, W), z, -1.5)
-            lin(y, z, 0.25, -MG)
-            vtt(y, y, R("dl%d" % l, a, b), OP.add)
+            y, dl = PQ("undo"), R("dl%d" % l, a, b)
+            for c in wide(k, TU["WU"]):
+                z, z0 = F(CH[c][1] - a), a
+                chain(l, c, R(src, 0, W), z, -1.5, y if k in TU["HU"][l - 1] else None)
+                lin(z, z, 0.25, MG)
+            lin(y, R(z[0], z[1] + a - z0, z[1] + b - z0), bias=-MG)
+            vtt(dl, y, dl, OP.add)
+        both = R("dl3", 0, V + W) if l == 3 else R(src, 0, W + V)
+        for k in (range(4) if sp is None or not TU["WU"] else (5, 6)):
+            a, b = CH[k]
+            pick = IND(both, R("s%d" % l, a // 16, b // 16))
             if sp is None:
-                vtt(R(dst, a, b), y, R(src, a, b), OP.max)
-                dma(T.yx[:, a:b], T[dst][:, a:b], [], [R(dst, a, b)])
+                lin(R(dst, a, b), pick)
+                dma(T.yx[:, a:b], ap(R(dst, a, b)), [], [R(dst, a, b)])
             else:
-                vtt(y, y, R(src, a, b), OP.max)
-                vtt(R(dst, a, b), y, R(sp, a, b), OP.subtract)
+                vtt(R(dst, a, b), pick, R(sp, a, b), OP.subtract)
 
     undo(3, "xa", "key", "sp2")
-    sact(R("xa", V, W), R("rb1", 0, GH))
-    for nm, a, n in (("dl3", 0, V), ("sp2", V, V), ("rs2", 2 * V, 768)):
+    lin(R("xa", V, W), R("rb", 1, 768, 2))
+    for nm, a, n in (("dl3", 0, V), ("sp2", V, V), ("rb", 2 * V, 768)):
         for c in range(0, n, 1024):
             e = min(c + 1024, n)
             lin(R(nm, c, e), IND(R("yw", 0, P2), R("lw16", (a + c) // 16, (a + e) // 16)))
-        dma(T.yn[:, a:a + n], T[nm][0:128:16, 0:n], [], [R(nm, 0, n)])
+        dma(T.yn[:, a:a + n], T[R(nm, 0, n)[0]][0:128:16, 0:n], [], [R(nm, 0, n)])
     undo(2, "key", "xa", "sp1")
     undo(1, "xa", "key", None)
 

@@ -11,8 +11,8 @@ EO = 2040.0
 
 TU = {"CY": 0.0009, "PCY": 0.00045, "WK": 0.1, "OV": 0.05, "GA": 1.5, "TT": 1.6, "VPEN": 0.3, "EX": 5.0,
       "PASS": 8, "SLK": 10.0, "LA": 0.02, "MIX": 1.0, "PB": 1.7, "WB": 0.5, "BK": 10.0, "BL": 0.0, "B3": 0.0,
-      "TRY": [(s, v, m) for s in (3.0, 10.0) for v in (0.2, 0.4) for m in (0.5, 1.0)], "CLIMB": 1500, "STEP": 10.0,
-      "CASES": [(1.0, 1.0, 0.08, 1.0), (0.6, 2.0, 0.1, 1.0), (0.4, 1.0, 0.1, 2.5), (0.4, 1.0, 0.35, 1.3)], "BG": 10.0, "MGC": [], "PG": [], "C3": [0, 1, 2, 3, 4],
+      "TRY": [(3.0, 0.2, 1.0), (10.0, 0.4, 0.5), (10.0, 0.2, 1.0)], "CLIMB": 400, "STEP": 10.0, "MEND": 30000, "FLIP": 0.4, "HOT": 0.15,
+      "CASES": [(1.0, 1.0, 0.08, 1.0), (0.6, 2.0, 0.1, 1.0), (0.4, 1.0, 0.1, 2.5), (0.4, 1.0, 0.35, 1.3)], "BG": 10.0, "DA": [], "LK": 4, "AC": 0, "DW": 32, "LATE": [2, 1], "WB4": [0, 1, 2, 3], "ORD": [0, 1, 4, 2, 3], "SG": [], "PG": [], "C3": [0, 1, 2, 3, 4],
       "HU": [[], [0, 1, 2, 3], [0, 1, 2, 3]], "HC": [], "SC": [32, 64, 128, 192, 256, 304], "PD": 1.5, "BF": 0, "WA": 0, "WC": 0, "WU": 0, "W3": 0}
 PLAN = {}
 KB = {"idn": 0, "blk": 128, "wz": 256, "wq": 400, "rz": 544, "cv0": 688, "cv1": 832, "cv2": 976, "cv3": 1120,
@@ -20,28 +20,29 @@ KB = {"idn": 0, "blk": 128, "wz": 256, "wq": 400, "rz": 544, "cv0": 688, "cv1": 
 SCRATCH = {}
 for _n, _c, _t in (
         ("wa", W + 2 * V, "float32"), ("wk", W + V, "float32"), ("yw", P2, "float32"),
-        ("sp1", V + 8, "float32"), ("sp2", V + 8, "float32"), ("vim", 128, "float32"), ("sz", 128, "uint16"), ("x0i", V, "int32"), ("vid", 128, "float32"),
+        ("sp1", V, "float32"), ("sp2", V, "float32"), ("x0i", W, "int32"), ("vid", 128, "float32"),
         ("s1", 128, "uint16"), ("s2", 128, "uint16"), ("s3", 128, "uint16"),
         ("ga", 2 * P2, "float16"), ("gb", 2 * P2, "float16"), ("g3", 4 * V, "float16"), ("fw", P2, "bfloat16"),
-        ("tk", V, "float16"), ("nm", V, "bfloat16"),
+        ("tk", V, "float16"), ("nm", W, "bfloat16"), ("nhh", 128, "float16"),
         ("kb", 1552, "bfloat16"), ("kh", 1552, "float16"), ("neh", 128, "float16"), ("nqh", 128, "float16"),
         ("rn", 144, "float16"), ("ro", 144, "float16"), ("eh", 144, "float16"),
         ("un", 1028, "bfloat16"), ("ul", 512, "bfloat16"), ("one", 512, "bfloat16"),
-        ("mgc", 128, "bfloat16"), ("cw", 128, "bfloat16"), ("pn", 128, "bfloat16"),
+        ("cw", 128, "bfloat16"), ("pn", 128, "bfloat16"),
         ("bl4", 128, "bfloat16"), ("swd", 128, "float32"), ("nt0", 128, "float32"), ("nt1", 128, "float32"),
         ("nw", 144, "float32"), ("o32", 64, "float32"),
         ("ini", 332, "int32"), ("pci", 8, "int32"), ("col", 48, "float32"), ("th32", 8, "float32"), ("ls", 24, "uint16"),
-        ("nxf", 304, "float32"), ("lw16", 304, "uint16"), ("lp", C4, "uint16"), ("pf", C4, "float32"),
+        ("lw16", 304, "uint16"), ("lp", C4, "uint16"), ("pf", C4, "float32"),
         ("n16", C4, "float16"), ("pid", 512, "float32"), ("dp", 512, "float32"), ("hc", 128, "bfloat16"),
         ("lw1", 512, "bfloat16"), ("lw2", 512, "bfloat16"), ("lw3", 512, "bfloat16"), ("nmq", 512, "bfloat16"),
-        ("hi", 512, "bfloat16"), ("lo", 512, "bfloat16"), ("win", 512, "bfloat16"), ("c01", 512, "bfloat16"),
+        ("hi", 512, "bfloat16"), ("lo", 512, "bfloat16"), ("c01", 512, "bfloat16"),
         ("sh", 768, "float16"), ("rs1", 768, "float16"), ("rs2", 768, "float16"), ("ss", GH, "float32"),
         ("rs3", GH, "float32"), ("bs", 3 * GH, "float32"), ("rb", 768, "float32"),
         ("sg1", GH, "float32"), ("sg2", GH, "float32"), ("bt", 256, "float32")):
     SCRATCH[_n] = ("sbuf", [128, _c], _t)
-PART = {"dl3": ("wa", 0), "xa": ("wa", V), "dl1": ("wa", V + W), "key": ("wk", 0), "dl2": ("wk", W)}
+PART = {"dl3": ("wa", 0), "xa": ("wa", V), "dl1": ("wa", V + W), "key": ("wk", 0), "dl2": ("wk", W),
+        "nxf": ("sg2", 0)}
 SCRATCH["fr"] = ("sbuf", [128, 3072], "float32")
-RINGS = { "t": (6, "float16"), "e": (2, "float16")}
+RINGS = {"t": (8, "float16"), "e": (2, "float16")}
 for _r in RINGS:
     for _k in range(RINGS[_r][0]):
         SCRATCH["%s%d" % (_r, _k)] = ("sbuf", [128, 512], RINGS[_r][1])
@@ -53,7 +54,7 @@ ARR = [a + str(d) for a in ("ax1_", "ax2_", "ax3_", "as1_", "as2_", "as3_", "ab3
 SEMAPHORES = ["sv", "ss_", "st", "sg", "loc"] + ARR + ["d%d" % k for k in range(20)]
 PSUMS = ["p%d" % k for k in range(8)]
 POOL = {"size": [4, 5], "diff": [5, 6], "own": [4, 5, 6], "flat": [0, 1, 2, 3], "kept": [4, 5, 6], "undo": [0, 1, 2, 3],
-        "late": [4, 5, 6], "rem": [4, 5, 6]}
+        "late": [4, 5, 6], "sums": [0, 1, 2, 3]}
 
 
 def R(name, a, b, s=1):
@@ -98,19 +99,31 @@ def ordered(prog):
     for i in range(n - 1, -1, -1):
         tail[i] = dur[i] + max([tail[j] + WK for j in succs[i]] or [0.0])
     lat = [p[3] or 0.0 for p in prog]
+    ways = [[v[:2] for v in p[0]] for p in prog]
+    near = [[j for j in p if lat[j] or not any(j in preds[k] for k in p)] for p in preds]
 
-    def replay(seq, pick, pe, wk, ex):
-        free, end = {e: 0.0 for e in "vstgy"}, [0.0] * n
-        for i in seq:
-            e, t = prog[i][0][pick[i]][:2]
-            r = max([end[j] for j in preds[i]] or [0.0])
+    def replay(seq, pick, pe, wk, ex, a=0, known=None):
+        free, end = {e: 0.0 for e in "vstgya"}, list(known) if a else [0.0] * n
+        for i in seq[:a]:
+            free[ways[i][pick[i]][0]] = i + 1
+        for e in "vstgy" * (a > 0):
+            i = free[e] - 1
+            free[e] = end[i] - wk - lat[i] * ex if free[e] else 0.0
+        for i in seq[a:]:
+            e, t = ways[i][pick[i]]
+            r = 0.0
+            for j in near[i]:
+                if end[j] > r:
+                    r = end[j]
             if e != "a":
-                r = free[e] = max(r, free[e]) + (t * pe if e == "t" else t)
+                if free[e] > r:
+                    r = free[e]
+                r = free[e] = r + (t * pe if e == "t" else t)
             end[i] = r + wk + lat[i] * ex
-        return max(end)
+        return end
 
     def worth(seq, pick):
-        return sum(c[0] * replay(seq, pick, *c[1:]) for c in TU["CASES"])
+        return sum(c[0] * max(replay(seq, pick, *c[1:])) for c in TU["CASES"])
 
     def run(key, before, after, back):
         left = [len(p) for p in before]
@@ -169,6 +182,68 @@ def ordered(prog):
             span = worth(seq, pick)
             if span <= PLAN[n][0]:
                 PLAN[n] = (span, seq, pick, key) + PLAN[n][4:]
+        span, seq, pick = PLAN[n][:3]
+        pre, ends = near, [replay(seq, pick, *c[1:]) for c in TU["CASES"]]
+        for step in range(TU["MEND"]):
+            if step % 8 == 0:
+                pe, wk, ex = TU["CASES"][int(draw() * len(TU["CASES"]))][1:]
+                free, last, end, why = {e: 0.0 for e in "vstgy"}, {}, [0.0] * n, [None] * n
+                for i in seq:
+                    e, t = prog[i][0][pick[i]][:2]
+                    r = 0.0
+                    for j in pre[i]:
+                        if end[j] > r:
+                            r, why[i] = end[j], (j, False)
+                    if e != "a":
+                        if free[e] > r:
+                            r, why[i] = free[e], (last[e], True)
+                        r = free[e] = r + (t * pe if e == "t" else t)
+                        last[e] = i
+                    end[i] = r + wk + lat[i] * ex
+                i, pairs = max(range(n), key=lambda j: end[j]), []
+                while why[i]:
+                    if why[i][1]:
+                        pairs.append((why[i][0], i))
+                    i = why[i][0]
+            p, i = pairs[int(draw() * len(pairs))]
+            u, seq2, pick2 = draw(), seq, pick
+            if u < TU["FLIP"]:
+                j = p if u < TU["FLIP"] / 2 else i
+                if len(prog[j][0]) < 2:
+                    continue
+                pick2 = list(pick)
+                pick2[j], a = 1 - pick[j], seq.index(j)
+            else:
+                a, b = seq.index(p), seq.index(i)
+                if a >= b:
+                    continue
+                if u < (1 + TU["FLIP"]) / 2:
+                    up, rest, todo = [], [], {i}
+                    for j in reversed(seq[a:b + 1]):
+                        if j in todo:
+                            up.append(j)
+                            todo |= preds[j]
+                        else:
+                            rest.append(j)
+                    if p in todo:
+                        continue
+                    seq2 = seq[:a] + up[::-1] + rest[::-1] + seq[b + 1:]
+                else:
+                    b = min(n - 1, b + int(draw() * 30))
+                    down, rest, todo = [], [], {p}
+                    for j in seq[a:b + 1]:
+                        if j in todo:
+                            down.append(j)
+                            todo |= succs[j]
+                        else:
+                            rest.append(j)
+                    seq2 = seq[:a] + rest + down + seq[b + 1:]
+            ends2 = [replay(seq2, pick2, *c[1:], a, e) for c, e in zip(TU["CASES"], ends)]
+            s2 = sum(c[0] * max(e) for c, e in zip(TU["CASES"], ends2))
+            if s2 <= span + TU["HOT"] * (1 - step / TU["MEND"]):
+                span, seq, pick, ends = s2, seq2, pick2, ends2
+                if span < PLAN[n][0]:
+                    PLAN[n] = (span, seq, pick)
     return [prog[i][0][PLAN[n][2][i]][2] for i in PLAN[n][1]]
 
 
@@ -414,7 +489,8 @@ def rank_program(g, core, T, topo):
         return R(name, 16 - k, 144 - k)
 
     def lst(l, t, k):
-        return R("l%d" % l, 152 * t + CH[k][0] // 16, 152 * t + CH[k][1] // 16)
+        o = 64 * t if CH[k][0] < 1024 else 192 + 88 * t
+        return R("l%d" % l, o + CH[k][0] // 16, o + CH[k][1] // 16)
 
     def pc(n, t, k):
         a, b = CH[k]
@@ -426,38 +502,39 @@ def rank_program(g, core, T, topo):
 
     def nodes(parts):
         for pb, a, s in parts:
-            nf = F(304)
+            nf = F(num(pb))
             lin(nf, pb, 0.5, MG)
-            lin(R("n16", a, a + 303 * s + 1, s), nf, bias=-(MG + NO))
+            lin(R("n16", a, a + (num(pb) - 1) * s + 1, s), nf, bias=-(MG + NO))
 
-    def node_lists(l, pairs):
-        for pr, bank in pairs:
-            for t in (2 * pr, 2 * pr + 1):
-                mm(R(bank, 152 * (t % 2), 152 * (t % 2) + 152),
-                   [(shifted("cv%d" % t, 4 * b), R("n16", b, C4, 4)) for b in range(4)])
-            vts(R("l%d" % l, 304 * pr, 304 * pr + 304), R(bank, 0, 304), NO, OP.add)
+    def node_lists(l, part, ts, bank, mat="cv", s=4):
+        a, n = (0, 64) if part == 0 else (64, 88)
+        for i, t in enumerate(ts):
+            mm(R(bank, n * i, n * i + n),
+               [(shifted(mat + str(t), 16 // s * b), R("n16", s * a + b, s * (a + n), s)) for b in range(s)])
+        o = 4 * a + n * ts[0]
+        vts(R("l%d" % l, o, o + n * len(ts)), R(bank, 0, n * len(ts)), NO, OP.add)
 
     def tables(parts, ports, halves=True):
         nodes([p[:3] for p in parts] * halves)
         for pb, a, s, own in parts:
             e = a + (own - 1) * s + 1
-            lin(R("pf", a, a + 303 * s + 1, s), pb)
+            lin(R("pf", a, a + (num(pb) - 1) * s + 1, s), pb)
             vtt(R("dp", a, e, s), R("pid", a, e, s), R(pb[0], 0, own), OP.subtract)
         if ports:
             vts(R("lp", 0, C4), R("pf", 0, C4), 0.5, OP.add)
 
-    def chain(l, k, win, q, bias=0.0, bank=None):
+    def chain(l, k, win, q, bias=0.0, bank=None, out=None):
         lin(q, IND(win, lst(l, 0, k)), bias=bias)
         if bank is None:
             for t in (1, 2, 3):
-                vtt(q, IND(win, lst(l, t, k)), q, OP.add)
+                vtt(out if out and t == 3 else q, IND(win, lst(l, t, k)), q, OP.add)
             return
         h = F(num(q))
         lin(h, IND(win, lst(l, 2, k)))
         vtt(h, IND(win, lst(l, 3, k)), h, OP.add)
         vtt(q, IND(win, lst(l, 1, k)), q, OP.add)
         sact(bank, h)
-        vtt(q, bank, q, OP.add)
+        vtt(out or q, bank, q, OP.add)
 
     def flat(mat, src, pool, use):
         for j in range(4):
@@ -486,11 +563,11 @@ def rank_program(g, core, T, topo):
         n = min(128 * b, P2 - 128 * b)
         sact(R("g3", 128 * b, 128 * b + n), R("g3", 0, n), AF.Identity, bias=R("col", b, b + 1))
     vcopy(R("lw16", 0, 304), R("ini", 0, 304))
-    vts(R("nxf", 0, 304), R("ini", 0, 304), -0.5, OP.add)
+    lin(R("nxf", 0, 304), R("ini", 0, 304), bias=-0.5)
     first[0] = 100.0
     vcopy(LSA, R("ini", 304, 328))
     for k in range(2):
-        vts(R("xa", 1024 * k, 1024 * k + 1024), R("x0i", 1024 * k, 1024 * k + 1024), -MG, OP.add)
+        lin(R("xa", 1024 * k, 1024 * k + 1024), R("x0i", 1024 * k, 1024 * k + 1024))
     sact(R("bs", 0, GH), IND(R("xa", 0, V), LSA))
     send(peers, ("bs", 0, "xa", V, B), "ax1_")
     recv("ax1_", homes, ("xa", V, B))
@@ -502,7 +579,6 @@ def rank_program(g, core, T, topo):
     vset(R("kb", 256, 1552), 0.0)
     vset(R("un", 0, 1028), 0.0)
     vset(R("nw", 0, 144), 0.0)
-    vset(M("mgc"), MG / 128.0)
     o128, o64, o8 = R("one", 0, 128), R("o32", 0, 64), R("one", 0, 8)
     for c in (0, 1):
         for h in (0, 1):
@@ -522,20 +598,17 @@ def rank_program(g, core, T, topo):
         asel(o, o128, pat, OP.is_ge, 0, 1)
         asel(o, o, [[16, 8], [0, 16]], OP.is_ge, 15, -1)
     lin(R("kh", 0, KB["cv0"]), R("kb", 0, KB["cv0"]))
-    for n, i, c in (("neh", "idn", -1.0), ("nqh", "idn", -0.25), ("cw", "idn", 8192.0 * EO), ("pn", "idn", -2.0 ** 30)):
+    for n, i, c in (("neh", "idn", -1.0), ("nqh", "idn", -0.25), ("nhh", "idn", -0.5), ("cw", "idn", 8192.0 * EO), ("pn", "idn", -2.0 ** 30)):
         sact(M(n), M(i, "kb"), scale=c)
     for n, i, c in (("rn", "rz", -1.0), ("ro", "rz", -8192.0), ("eh", "wz", 4096.0)):
         sact(R(n, 0, 144), R("kb", KB[i], KB[i] + 144), scale=c)
     asel(M("bl4"), o128, [[-4, 32], [0, 4]], OP.is_ge, 0, 1)
     asel(M("bl4"), M("bl4"), [[4, 32], [0, 4]], OP.is_ge, 3, -1)
     asel(R("ul", 0, 512), ONE, [[-4, 4], [-16, 8], [0, 16]], OP.is_equal, 0, 1)
-    iota(R("vid", 0, 128), [[16, 128]], 0, 0)
+    iota(R("vid", 0, 128), [[0, 4], [16, 32]], 0, 0)
     vts(R("pci", 3, 4), R("pci", 0, 1), 15, OP.bitwise_and)
     vcopy(R("col", 44, 45), R("pci", 3, 4))
     sact(R("vid", 0, 128), R("vid", 0, 128), AF.Identity, bias=R("col", 44, 45))
-    lin(R("vim", 0, 128), R("vid", 0, 128), bias=-float(V))
-    for n in ("sp1", "sp2"):
-        vset(R(n, V, V + 8), 0.0)
     for s in (0, 1):
         asel(R("un", 4 + 2 * s, 1028, 16), R("one", 0, 64), [[-4, 4], [-1, 2], [-16, 8]], OP.is_equal, -2 * s, 1)
     for h in (0, 1):
@@ -553,20 +626,19 @@ def rank_program(g, core, T, topo):
     vcopy(THR, R("ini", 328, 329))
     iota(R("yw", 4096, P2), [[1, 768]], 4096, 0)
 
-    vts(R("ini", 0, 304), R("ini", 0, 304), 1, OP.arith_shift_right)
-    vts(R("n16", 0, 304), R("ini", 0, 304), -NO, OP.add)
-    for h in (0, 1):
-        mm(R("p6", 152 * h, 152 * h + 152), [(shifted("pm%d" % h, 8 * c), R("n16", c, 304, 2)) for c in (0, 1)])
-    vts(R("l1", 0, 304), R("p6", 0, 304), NO, OP.add)
+    nodes([(R("nxf", 0, 304), 0, 1)])
+    for part in (0, 1):
+        node_lists(1, part, (0, 1), "p%d" % (6 + part), "pm", 2)
     for k in (5, 6, 4):
         for t in (0, 1):
-            lin(pc("ga", t, k), IND(XA, lst(1, t, k)), bias=MG)
+            lin(pc("ga", t, k), IND(XA, lst(1, t, k)), bias=-1.5 * (t == 0))
     for c in (0, 1):
         mm(R("p%d" % (4 + c), 0, 304), [(M("nt%d" % c), R("nxf", 0, 304))], stop=False)
         mm(R("p%d" % (4 + c), 0, 304),
            [(shifted("wq", 2 + 4 * (i // 2) + i % 2, "kb"), R("fw", 8 * c + i, P2, 16)) for i in range(8)], start=False)
     tables([(R("p%d" % (4 + c), 0, 304), c, 2, 256) for c in (0, 1)], True)
-    node_lists(1, [(1, "p6")])
+    for part in (0, 1):
+        node_lists(1, part, (2, 3), "p%d" % (6 + part))
     lin(R("fw", 4096, P2), R("g3", 4096, P2))
     vset(R("nm", 0, V), 0.0)
     for d in (1, 2, 3):
@@ -587,17 +659,17 @@ def rank_program(g, core, T, topo):
             n = b - a
             for c in wide(k, TU["WA"]):
                 for t in range(4):
-                    if l < 3 and t == 2:
-                        vts(pc("ga", t, c), IND(XA, lst(l, t, c)), MG, OP.add, -1.5, OP.add)
+                    if l in TU["DA"] and t == 3 and k < 4:
+                        vtt(pc("ga", t, c), IND(XA, lst(l, t, c)), pc("ga", 2, c), OP.subtract)
                     elif l > 1 or t > 1:
-                        lin(pc("ga", t, c), IND(XA, lst(l, t, c)), bias=MG)
+                        lin(pc("ga", t, c), IND(XA, lst(l, t, c)), bias=-1.5 * (l < 3 and t == 0))
                     if l == 3:
-                        lin(pc("gb", t, c), IND(R("fw", 0, W), lst(l, t, c)), bias=-0.375)
+                        lin(pc("gb", t, c), IND(R("nm", 0, W), lst(l, t, c)), bias=-0.375)
             zb[k] = R("p%d" % k, 0, n)
-            one = R("one", 0, n)
             mm(zb[k], [(NQ, pc(s, t, k)) for s in srcs for t in (0, 1)], stop=False)
-            mm(zb[k], [(NQ, pc(s, t, k)) for s in srcs for t in (2, 3)] + [(M("mgc"), one)] * (k < 4 and l in TU["MGC"]), start=False)
-            vtt(zb[k], zb[k], R("xa", a, b), OP.add)
+            mm(zb[k], [(M("nhh") if l in TU["DA"] and t == 2 and k < 4 else NQ, pc(s, t, k)) for s in srcs for t in (2, 3)],
+               start=False)
+            vtt(R("x0i", a, b), zb[k], R("xa", a, b), OP.add)
 
         def sized(k):
             a, b = CH[k]
@@ -605,49 +677,52 @@ def rank_program(g, core, T, topo):
             t = e = tk[k] = R("tk", a, b) if k < 4 else ring("t", n)
             if l > 1:
                 e = ring("e", n) if l == 2 else F(n)
-            sact(e, zb[k], AF.Abs, bias=0.0 if k < 4 and l in TU["MGC"] else MG)
-            if k < 4 and l not in TU["MGC"]:
-                lin(zb[k], zb[k], bias=MG)
+            sact(e, R("x0i", a, b), AF.Abs)
             if l > 1:
                 vts(t, e, 255.0, OP.min)
             o = PQ("size", n) if k < 4 else R("p5", 0, n)
             mm(o, [(M("blk"), t)])
             lin(R("key", a, b), o, bias=-EO)
             if k < 4:
-                tk[k] = mask()
-                vts(tk[k], e, THR, OP.is_ge)
+                vts(zb[k], e, THR, OP.is_ge, 0.25, OP.mult)
 
         def detail(k):
             a, b = CH[k]
-            d, m, q = zb[k], tk[k], R("x0i", a, b)
-            vtt(R(dl, a, b), d, m, OP.mult)
-            if l == 3:
-                vtt(d, d, R(dl, a, b), OP.subtract)
-            vts(q, d, 0.25, OP.mult, -0.375, OP.add)
+            d, m = R("x0i", a, b), zb[k]
+            vtt(R(dl, a, b), m, d, OP.mult)
+            vts(d, d, 2, OP.arith_shift_right)
             if l < 3:
-                lin(d, m, bias=KP)
-                vtt(R(p0, a, b), d, q, OP.mult)
+                lin(m, m, bias=KP / 4)
+            else:
+                lin(m, m, -4.0, 1.0)
+            vtt(R(p0, a, b), m, d, OP.mult)
 
         def chosen():
             for t in range(4):
-                for a in (0, 64):
-                    lin(R(gk, V * t + 16 * a, V * t + 16 * a + 1024), IND(KEY, R("l%d" % l, 152 * t + a, 152 * t + a + 64)))
+                for c in (5, 6):
+                    lin(pc(gk, t, c), IND(KEY, lst(l, t, c)))
             o = R("p4", 0, 512)
             mm(o, [(M("cw"), R("nmq", 0, 512))] + [(M("pn"), R("lw%d" % j, 0, 512)) for j in range(1, l)] +
                [(shifted("ro", 4 * j), every("tk", j)) for j in range(4)], stop=False)
             for t in range(4):
                 mm(o, [(shifted("eh", 4 * j + t), R(gk, V * t + j, V * t + V, 4)) for j in range(4)], False, t == 3)
-            vtt(R("win", 0, 512), o, R("dp", 0, 512), OP.is_ge)
-            mm(o, [(M("bl4"), R("win", 0, 512))])
+            vtt(R("c01", 0, 512), o, R("dp", 0, 512), OP.is_ge)
+            mm(o, [(M("bl4"), R("c01", 0, 512))])
             lin(LW, o, bias=-3.0, relu=True)
 
         def likeness(k):
             terms = []
             first[0] = TU["BL"] if l < 3 else TU["B3"]
-            for x, y in ((0, 0), (1, 1), (0, 1), (1, 0)):
-                u, tn, sign = PQ("diff"), ring("t"), [1]
-                mm(u, [(I1, pc(s, 2 + x, k)) for s in srcs] + [(NI, pc(s, y, k)) for s in srcs])
-                shift = 1.5 if l < 3 and x == 0 else 0.0
+            us = {}
+            for x, y in ((0, 0), (0, 1), (1, 0), (1, 1)):
+                tn, sign = ring("t"), [1]
+                if l in TU["DA"] and x:
+                    u = us[y]
+                    mm(u, [(I1, pc("ga", 3, k))], start=False)
+                else:
+                    u = us[y] = PQ("diff" if k < TU["LK"] or l == 3 else "flat")
+                    mm(u, [(I1, pc(s, 2 + x, k)) for s in srcs] + [(NI, pc(s, y, k)) for s in srcs], stop=l not in TU["DA"])
+                shift = -1.5 if l < 3 and y == 0 else 0.0
                 if l == 1:
                     lin(tn, u, bias=shift, relu=True)
                 else:
@@ -660,7 +735,11 @@ def rank_program(g, core, T, topo):
 
         def links():
             o, c = R("p7", 0, 512), R("c01", 0, 512)
-            vts(c, o, 0.0, OP.is_gt)
+            if l in TU["SG"]:
+                sact(c, o, AF.Sign, bias=-0.5)
+                sact(c, c, AF.Relu)
+            else:
+                vts(c, o, 0.0, OP.is_gt)
             mm(o, [(M("swd"), R("pf", 0, 512))])
             vtt(o, o, c, OP.mult)
             vtt(o, o, R("dp", 0, 512), OP.subtract)
@@ -683,82 +762,83 @@ def rank_program(g, core, T, topo):
             a, b = CH[k]
             x = R("xa", a, b)
             if l < 3:
-                b1, b2 = PQ("own"), PQ("own")
+                b1 = PQ("own")
                 s = R("sp%d" % l, a, b)
                 for c in wide(k, TU["WC"]):
                     chain(l, c, KEY, R("sp%d" % l, *CH[c]), 0.0, b1 if k in TU["HC"] else None)
                 z = F()
-                lin(z, s, bias=MG * KP)
-                lin(b1, z, 1.0 / KP, -MG)
-                lin(b2, z, bias=-MG * KP)
+                lin(z, s, bias=MG * KP / 4)
+                lin(b1, z, 4.0 / KP, -MG)
                 vtt(x, b1, x, OP.add)
-                vtt(s, s, b2, OP.subtract)
-            elif k not in TU["C3"]:
-                q = F(b - a) if k < 4 else R("ss", 0, GH)
-                chain(l, k, KEY, q, MG if k < 4 else 0.0)
-                if k < 4:
-                    vtt(x, q, x, OP.add)
+                if l not in TU["LATE"]:
+                    b2 = PQ("own")
+                    lin(b2, z, bias=-MG * KP / 4)
+                    vtt(s, s, b2, OP.subtract)
             else:
                 o = PQ("flat", b - a)
                 gs = [R("g3", V * t + a, V * t + b) if k < 4 else ring("t", GH) for t in range(4)]
                 for c in wide(k, TU["W3"]):
                     for t in range(4):
                         lin(gs[t] if k == 4 else pc("g3", t, c), IND(KEY, lst(l, t, c)))
-                mm(o, [(I1, s) for s in gs] + ([(M("mgc"), ONE)] if k < 4 else []))
+                mm(o, [(NQ, s) for s in gs])
                 if k < 4:
-                    vtt(x, o, x, OP.add)
+                    vtt(x, x, o, OP.subtract)
                 else:
-                    lin(R("ss", 0, GH), o)
+                    lin(R("ss", 0, GH), o, -1.0)
 
-        def border(buf, rc):
+        def sums(j):
+            for k in range(4 * (j in TU["LATE"])):
+                s, z, b2 = R("sp%d" % j, *CH[k]), F(), PQ("sums")
+                lin(z, s, bias=MG * KP / 4)
+                lin(b2, z, bias=-MG * KP / 4)
+                vtt(s, s, b2, OP.subtract)
+            border("sp%d" % j, 1, "rs%d" % j)
+            sact(R("sg%d" % j, 0, GH), IND(R("sp%d" % j, 0, V), LSA))
+
+        def border(buf, rc, rs="rs%d" % l):
             for d in (1, 2, 3):
-                s, bt = 2 if l < 3 else 1, R("bt", B * rc, B * rc + B)
+                s, bt = 1 if rs == "rs3" else 2, R("bt", B * rc, B * rc + B)
                 vtt(bt, IND(R(buf, 0, V), LSB[d]), R(rs, rc + (d - 1) * s * B, d * s * B, s), OP.add)
                 vcopy(IND(R(buf, 0, V), LSB[d]), bt)
 
         def kept():
             o, s = PQ("kept", 128), F(128)
             mm(o, [(shifted("cv0", 4 * b, "kb"), R(LW[0], b, 512, 4)) for b in range(4)])
-            if l in TU["PG"]:
-                s2 = F(128)
-                vtt(s2, o, R("vim", 0, 128), OP.mult)
-                vts(R("sz", 0, 128), s2, float(V), OP.add)
-                for a in range(0, 128, 32):
-                    lin(R("key", 16 * a, 16 * a + 512), IND(R(p0, 0, V + 8), R("sz", a, a + 32)))
             lin(o, o, float(W if l < 3 else -V), float(0 if l < 3 else V))
             vtt(s, o, R("vid", 0, 128), OP.add)
             vcopy(R("s%d" % l, 0, 128), s)
 
         if l == 3:
-            for k in range(5):
-                a, b = CH[k]
-                t, tp = ring("t", b - a), PQ("rem", b - a)
-                lin(t, R("xa", a, b), bias=MG)
-                lin(tp, t, bias=-MG)
-                vtt(R("fw", a, b), R("xa", a, b), tp, OP.subtract)
-        for k in ([4, 0, 1, 2, 3] if l > 1 else [0, 1, 2, 4, 3]):
+            iota(R("nm", 0, V), [[0, V]], 0, 0)
+            for src, o in ((R("bs", 0, GH), R("c01", 0, GH)), (R("xa", V, W), R("nm", V, W))):
+                t = ring("t", GH)
+                lin(t, src)
+                vtt(o, src, t, OP.subtract)
+                for d in (1, 2, 3) * (o[0] == "c01"):
+                    vcopy(IND(R("nm", 0, V), LSB[d]), R("c01", (d - 1) * B, d * B))
+        for k in (TU["ORD"] if l > 1 else [0, 1, 2, 4, 3]):
             gathers(k)
             sized(k)
         for k in range(4):
             detail(k)
+            if l == 3:
+                lin(R("xa", *CH[k]), R("xa", *CH[k]), 0.25)
         chosen()
-        if l < 3:
-            for k in range(4):
-                likeness(k)
-        vset(R("key", V, W), 0.0)
-        if l in TU["PG"]:
-            kept()
-        else:
-            flat("ul", LW[0], "flat", lambda j, u: vtt(every("key", j), u, every(p0, j), OP.mult))
+        for k in range(TU["LK"] * (l < 3)):
+            likeness(k)
+        iota(R("key", V, W), [[0, GH]], 0, 0)
+        flat("ul", LW[0], "flat", lambda j, u: vtt(every("key", j), u, every(p0, j), OP.mult))
+        for k in range(TU["LK"], 4 * (l < 3)):
+            likeness(k)
         rs = "rs%d" % l
         xg = [R("xa", V, W)]
         if l < 3:
             q, z, b4 = F(GH), F(GH), PQ("own", GH)
             first[0] = TU["BG"]
             chain(l, 4, KEY, q)
-            lin(z, q, bias=MG * KP)
-            lin(b4, z, bias=-MG * KP)
-            lin(R("sh", 0, 768, 2), z, 1.0 / KP, -MG)
+            lin(z, q, bias=MG * KP / 4)
+            lin(b4, z, bias=-MG * KP / 4)
+            lin(R("sh", 0, 768, 2), z, 4.0 / KP, -MG)
             vtt(R("sh", 1, 768, 2), q, b4, OP.subtract)
             send(homes, ("sh", 0, rs, 0, 2 * B), "as%d_" % l, xg)
             first[0] = 0.0
@@ -773,17 +853,16 @@ def rank_program(g, core, T, topo):
             sact(R("bs", 0, GH), IND(R("xa", 0, V), LSA))
             send(peers, ("bs", 0, "xa", V, B), "ax%d_" % (l + 1))
             recv("ax%d_" % (l + 1), homes, ("xa", V, B))
-            for k in range(8):
-                lin(R("gb", 1216 * k, 1216 * k + 1216), IND(R("fw", 0, P2), R("lp", 76 * k, 76 * k + 76)))
-            for hf in (0, 1):
-                mm(R("p%d" % hf, 0, 304), [(shifted("wz" if i % 4 < 2 else "wq", i), R("gb", P2 * hf + i, P2 * hf + P2, 16))
-                                          for i in range(16)])
-            border("sp%d" % l, 1)
-            sact(R("sg%d" % l, 0, GH), IND(R("sp%d" % l, 0, V), LSA))
-            if l not in TU["PG"]:
-                kept()
-            tables([(R("p0", 0, 304), 0, 1, 304), (R("p1", 0, 304), 304, 1, 208)], l < 2)
-            node_lists(l + 1, [(0, "p2"), (1, "p3")])
+            for a in range(0, C4, TU["DW"]):
+                lin(R("gb", 16 * a, 16 * (a + TU["DW"])), IND(R("fw", 0, P2), R("lp", a, a + TU["DW"])))
+            for part, (a, b) in enumerate(((0, 256), (256, C4))):
+                bk = R("p%d" % TU["WB4"][part], 0, b - a)
+                mm(bk, [(shifted("wz" if i % 4 < 2 else "wq", i), R("gb", 16 * a + i, 16 * b, 16)) for i in range(16)])
+                tables([(bk, a, 1, 256)], l < 2 and part == 1)
+                node_lists(l + 1, part, range(4), "p%d" % TU["WB4"][2 + part])
+            if l not in TU["LATE"]:
+                sums(l)
+            kept()
             if l == 2:
                 bk = PQ("kept", 304)
                 mm(bk, [(shifted("nw", 8 * c), R("pf", c, C4, 2)) for c in (0, 1)])
@@ -794,11 +873,21 @@ def rank_program(g, core, T, topo):
             recv("as3_", peers, (rs, 0, B))
             for k in range(4):
                 own(k)
-            border("xa", 0)
-            sact(R("bs", 0, GH), IND(R("xa", 0, V), LSA))
+            if TU["AC"]:
+                iota(R("yw", 0, V), [[0, V]], 0, 0)
+                border("yw", 0)
+                lin(R("rs3", 0, GH), IND(R("yw", 0, V), LSA))
+                vtt(R("bs", 0, GH), IND(R("xa", 0, V), LSA), R("rs3", 0, GH), OP.add)
+                for d in (1, 2, 3):
+                    vcopy(IND(R("xa", 0, V), LSB[d]), R("bs", (d - 1) * B, d * B))
+            else:
+                border("xa", 0)
+                sact(R("bs", 0, GH), IND(R("xa", 0, V), LSA))
+            send(peers, ("bs", 0, "xa", V, B), "ab3_")
+            for j in TU["LATE"]:
+                sums(j)
             vtt(R("bs", GH, 3 * GH, 2), R("bs", 0, GH), R("sg2", 0, GH), OP.subtract)
             vtt(R("bs", GH + 1, 3 * GH, 2), R("bs", GH, 3 * GH, 2), R("sg1", 0, GH), OP.subtract)
-            send(peers, ("bs", 0, "xa", V, B), "ab3_")
             send(peers, ("bs", GH, "rb", 0, 2 * B), "ab2_")
             recv("ab3_", homes, ("xa", V, B))
             recv("ab2_", homes, ("rb", 0, 2 * B))
@@ -811,21 +900,16 @@ def rank_program(g, core, T, topo):
             unwrap("late")
 
     def undo(l, src, dst, sp):
-        for k in range(4):
+        for k in (range(4) if l < 3 else (3, 2, 1, 0)):
             a, b = CH[k]
             y, dl = PQ("undo"), R("dl%d" % l, a, b)
-            for c in wide(k, TU["WU"]):
-                z, z0 = F(CH[c][1] - a), a
-                chain(l, c, R(src, 0, W), z, -1.5, y if k in TU["HU"][l - 1] else None)
-                lin(z, z, 0.25, MG)
-            lin(y, R(z[0], z[1] + a - z0, z[1] + b - z0), bias=-MG)
+            chain(l, k, R(src, 0, W), F(), -0.375, y if k in TU["HU"][l - 1] else None, R("x0i", a, b))
+            lin(y, R("x0i", a, b), 0.25)
             vtt(dl, y, dl, OP.add)
-        both = R("dl3", 0, V + W) if l == 3 else R(src, 0, W + V)
-        for k in (range(4) if sp is None or not TU["WU"] else (5, 6)):
-            a, b = CH[k]
+            both = R("dl3", a, V + b) if l == 3 else R(src, a, W + b)
             pick = IND(both, R("s%d" % l, a // 16, b // 16))
             if sp is None:
-                lin(R(dst, a, b), pick)
+                lin(R(dst, a, b), pick, 4.0)
                 dma(T.yx[:, a:b], ap(R(dst, a, b)), [], [R(dst, a, b)])
             else:
                 vtt(R(dst, a, b), pick, R(sp, a, b), OP.subtract)

from concourse.bass import DstId, RemoteDMATransfer
from concourse.mybir import AluOpType as OP, ActivationFunctionType as AF

V, B, W, P2 = 2048, 128, 2432, 4864
GH = 384
C4 = W // 4
MG = 12582912.0
KP = 4096.0
NO = 1216.0
EO = 2040.0

TU = {"CY": 0.0009, "PCY": 0.00045, "WK": 0.1, "OV": 0.05, "GA": 1.5, "TT": 1.6, "VPEN": 0.3, "EX": 5.0,
      "PASS": 8, "SLK": 10.0, "LA": 0.02, "MIX": 1.0, "PB": 1.7, "WB": 0.5, "BK": 10.0, "BL": 0.0, "B3": 0.0,
      "TRY": [(3.0, 0.2, 1.0), (10.0, 0.4, 0.5), (10.0, 0.2, 1.0)], "CLIMB": 400, "STEP": 10.0, "MEND": 30000, "FLIP": 0.4, "HOT": 0.15,
      "CASES": [(1.0, 1.0, 0.08, 1.0), (0.6, 2.0, 0.1, 1.0), (0.4, 1.0, 0.1, 2.5), (0.4, 1.0, 0.35, 1.3)], "BG": 10.0, "DA": [], "LK": 4, "AC": 0, "DW": 32, "LATE": [2, 1], "WB4": [0, 1, 2, 3], "ORD": [0, 1, 4, 2, 3], "SG": [], "PG": [], "C3": [0, 1, 2, 3, 4],
      "HU": [[], [0, 1, 2, 3], [0, 1, 2, 3]], "HC": [], "SC": [32, 64, 128, 192, 256, 304], "PD": 1.5, "BF": 0, "WA": 0, "WC": 0, "WU": 0, "W3": 0}
PLAN = {}
KB = {"idn": 0, "blk": 128, "wz": 256, "wq": 400, "rz": 544, "cv0": 688, "cv1": 832, "cv2": 976, "cv3": 1120,
      "pm0": 1264, "pm1": 1408}
SCRATCH = {}
for _n, _c, _t in (
        ("wa", W + 2 * V, "float32"), ("wk", W + V, "float32"), ("yw", P2, "float32"),
        ("sp1", V, "float32"), ("sp2", V, "float32"), ("x0i", W, "int32"), ("vid", 128, "float32"),
        ("s1", 128, "uint16"), ("s2", 128, "uint16"), ("s3", 128, "uint16"),
        ("ga", 2 * P2, "float16"), ("gb", 2 * P2, "float16"), ("g3", 4 * V, "float16"), ("fw", P2, "bfloat16"),
        ("tk", V, "float16"), ("nm", W, "bfloat16"), ("nhh", 128, "float16"),
        ("kb", 1552, "bfloat16"), ("kh", 1552, "float16"), ("neh", 128, "float16"), ("nqh", 128, "float16"),
        ("rn", 144, "float16"), ("ro", 144, "float16"), ("eh", 144, "float16"),
        ("un", 1028, "bfloat16"), ("ul", 512, "bfloat16"), ("one", 512, "bfloat16"),
        ("cw", 128, "bfloat16"), ("pn", 128, "bfloat16"),
        ("bl4", 128, "bfloat16"), ("swd", 128, "float32"), ("nt0", 128, "float32"), ("nt1", 128, "float32"),
        ("nw", 144, "float32"), ("o32", 64, "float32"),
        ("ini", 332, "int32"), ("pci", 8, "int32"), ("col", 48, "float32"), ("th32", 8, "float32"), ("ls", 24, "uint16"),
        ("lw16", 304, "uint16"), ("lp", C4, "uint16"), ("pf", C4, "float32"),
        ("n16", C4, "float16"), ("pid", 512, "float32"), ("dp", 512, "float32"), ("hc", 128, "bfloat16"),
        ("lw1", 512, "bfloat16"), ("lw2", 512, "bfloat16"), ("lw3", 512, "bfloat16"), ("nmq", 512, "bfloat16"),
        ("hi", 512, "bfloat16"), ("lo", 512, "bfloat16"), ("c01", 512, "bfloat16"),
        ("sh", 768, "float16"), ("rs1", 768, "float16"), ("rs2", 768, "float16"), ("ss", GH, "float32"),
        ("rs3", GH, "float32"), ("bs", 3 * GH, "float32"), ("rb", 768, "float32"),
        ("sg1", GH, "float32"), ("sg2", GH, "float32"), ("bt", 256, "float32")):
    SCRATCH[_n] = ("sbuf", [128, _c], _t)
PART = {"dl3": ("wa", 0), "xa": ("wa", V), "dl1": ("wa", V + W), "key": ("wk", 0), "dl2": ("wk", W),
        "nxf": ("sg2", 0)}
SCRATCH["fr"] = ("sbuf", [128, 3072], "float32")
RINGS = {"t": (8, "float16"), "e": (2, "float16")}
for _r in RINGS:
    for _k in range(RINGS[_r][0]):
        SCRATCH["%s%d" % (_r, _k)] = ("sbuf", [128, 512], RINGS[_r][1])
for _k in range(8):
    SCRATCH["p%d" % _k] = ("psum", [128, 512], "float32")
for _k in (1, 2, 3):
    SCRATCH["l%d" % _k] = ("sbuf", [128, C4], "uint16")
ARR = [a + str(d) for a in ("ax1_", "ax2_", "ax3_", "as1_", "as2_", "as3_", "ab3_", "ab2_") for d in (1, 2, 3)]
SEMAPHORES = ["sv", "ss_", "st", "sg", "loc"] + ARR + ["d%d" % k for k in range(20)]
PSUMS = ["p%d" % k for k in range(8)]
POOL = {"size": [4, 5], "diff": [5, 6], "own": [4, 5, 6], "flat": [0, 1, 2, 3], "kept": [4, 5, 6], "undo": [0, 1, 2, 3],
        "late": [4, 5, 6], "sums": [0, 1, 2, 3]}


def R(name, a, b, s=1):
    name, o = PART.get(name, (name, 0))
    return (name, o + a, o + b, s)


def IND(win, off):
    return ("ind", win, off)


def hits(x, y):
    if x[0] >= y[1] or y[0] >= x[1]:
        return False
    return not (x[2] == y[2] and x[2] > 1 and (x[0] - y[0]) % x[2])


def ordered(prog):
    n, WK = len(prog), TU["WK"]
    preds, succs = [set() for _ in range(n)], [set() for _ in range(n)]
    acc = {}
    for i, (var, ro, ri, lat, up) in enumerate(prog):
        e = var[0][0] if len(var) == 1 else None
        for lst, wr in ((ro, True), (ri, False)):
            for (nm, a, b, s) in lst:
                ps = nm in PSUMS
                for (j, e2, a2, b2, s2, w2) in acc.get(nm, ()):
                    if j != i and ((ps and (e is None or e != e2)) or ((wr or w2) and hits((a, b, s), (a2, b2, s2)))):
                        preds[i].add(j)
        for lst, wr in ((ro, True), (ri, False)):
            for (nm, a, b, s) in lst:
                old = acc.get(nm, [])
                if wr and s == 1:
                    old = [o for o in old if not (o[2] >= a and o[3] <= b and
                                                  (nm not in PSUMS or (e is not None and o[1] == e)))]
                acc[nm] = old + [(i, e, a, b, s, wr)]
    for i in range(n):
        for j in preds[i]:
            succs[j].add(i)
    dur = [min(v[1] for v in p[0]) + (p[3] or 0.0) for p in prog]
    tail = [0.0] * n
    for i in range(n - 1, -1, -1):
        tail[i] = dur[i] + max([tail[j] + WK for j in succs[i]] or [0.0])
    lat = [p[3] or 0.0 for p in prog]
    ways = [[v[:2] for v in p[0]] for p in prog]
    near = [[j for j in p if lat[j] or not any(j in preds[k] for k in p)] for p in preds]

    def replay(seq, pick, pe, wk, ex, a=0, known=None):
        free, end = {e: 0.0 for e in "vstgya"}, list(known) if a else [0.0] * n
        for i in seq[:a]:
            free[ways[i][pick[i]][0]] = i + 1
        for e in "vstgy" * (a > 0):
            i = free[e] - 1
            free[e] = end[i] - wk - lat[i] * ex if free[e] else 0.0
        for i in seq[a:]:
            e, t = ways[i][pick[i]]
            r = 0.0
            for j in near[i]:
                if end[j] > r:
                    r = end[j]
            if e != "a":
                if free[e] > r:
                    r = free[e]
                r = free[e] = r + (t * pe if e == "t" else t)
            end[i] = r + wk + lat[i] * ex
        return end

    def worth(seq, pick):
        return sum(c[0] * max(replay(seq, pick, *c[1:])) for c in TU["CASES"])

    def run(key, before, after, back):
        left = [len(p) for p in before]
        at = [lat[i] if back else 0.0 for i in range(n)]
        ready = [i for i in range(n) if not left[i]]
        free, end, pick, seq = {e: 0.0 for e in "vstgya"}, [0.0] * n, [0] * n, []
        while ready:
            best = None
            t0 = min(max(at[i], min(free[v[0]] for v in prog[i][0])) for i in ready)
            for i in ready:
                for k, v in enumerate(prog[i][0]):
                    t = max(at[i], free[v[0]])
                    c = key[i] + (TU["SLK"] if v[0] == "v" and len(prog[i][0]) > 1 else 0.0)
                    if t <= t0 + TU["LA"] and (best is None or (c, t) < best[0]):
                        best = ((c, t), i, k, t)
            _, i, k, t = best
            v = prog[i][0][k]
            if len(prog[i][0]) > 1 and v[0] == "v":
                v2 = prog[i][0][0]
                t2 = max(at[i], free["s"])
                if t2 + v2[1] < t + v[1] + TU["VPEN"]:
                    k, v, t = 0, v2, t2
            if v[0] != "a":
                free[v[0]] = t + v[1]
            end[i], pick[i] = t + v[1], k
            ready.remove(i)
            seq.append(i)
            for j in after[i]:
                at[j] = max(at[j], end[i] + WK + (lat[j] if back else lat[i]))
                left[j] -= 1
                if not left[j]:
                    ready.append(j)
        return end, pick, seq
    if n not in PLAN:
        for TU["SLK"], TU["VPEN"], mix in TU["TRY"]:
            key = [-tail[i] - prog[i][4] for i in range(n)]
            for _ in range(TU["PASS"]):
                end, pick, seq = run(key, preds, succs, False)
                span = worth(seq, pick)
                if n not in PLAN or span < PLAN[n][0]:
                    PLAN[n] = (span, seq, pick, key, TU["SLK"], TU["VPEN"])
                end = run([-end[i] - lat[i] for i in range(n)], succs, preds, True)[0]
                key = [(1 - mix) * key[i] - mix * (end[i] + prog[i][4]) for i in range(n)]
        seed = [1]

        def draw():
            seed[0] = (seed[0] * 1103515245 + 12345) % 2147483648
            return seed[0] / 2147483648.0
        TU["SLK"], TU["VPEN"] = PLAN[n][4:]
        for _ in range(TU["CLIMB"]):
            key = list(PLAN[n][3])
            a, w, d = int(draw() * n), 3 + int(draw() * 37), (2 * draw() - 1) * TU["STEP"]
            for i in range(a, min(n, a + w)):
                key[i] += d
            end, pick, seq = run(key, preds, succs, False)
            span = worth(seq, pick)
            if span <= PLAN[n][0]:
                PLAN[n] = (span, seq, pick, key) + PLAN[n][4:]
        span, seq, pick = PLAN[n][:3]
        pre, ends = near, [replay(seq, pick, *c[1:]) for c in TU["CASES"]]
        for step in range(TU["MEND"]):
            if step % 8 == 0:
                pe, wk, ex = TU["CASES"][int(draw() * len(TU["CASES"]))][1:]
                free, last, end, why = {e: 0.0 for e in "vstgy"}, {}, [0.0] * n, [None] * n
                for i in seq:
                    e, t = prog[i][0][pick[i]][:2]
                    r = 0.0
                    for j in pre[i]:
                        if end[j] > r:
                            r, why[i] = end[j], (j, False)
                    if e != "a":
                        if free[e] > r:
                            r, why[i] = free[e], (last[e], True)
                        r = free[e] = r + (t * pe if e == "t" else t)
                        last[e] = i
                    end[i] = r + wk + lat[i] * ex
                i, pairs = max(range(n), key=lambda j: end[j]), []
                while why[i]:
                    if why[i][1]:
                        pairs.append((why[i][0], i))
                    i = why[i][0]
            p, i = pairs[int(draw() * len(pairs))]
            u, seq2, pick2 = draw(), seq, pick
            if u < TU["FLIP"]:
                j = p if u < TU["FLIP"] / 2 else i
                if len(prog[j][0]) < 2:
                    continue
                pick2 = list(pick)
                pick2[j], a = 1 - pick[j], seq.index(j)
            else:
                a, b = seq.index(p), seq.index(i)
                if a >= b:
                    continue
                if u < (1 + TU["FLIP"]) / 2:
                    up, rest, todo = [], [], {i}
                    for j in reversed(seq[a:b + 1]):
                        if j in todo:
                            up.append(j)
                            todo |= preds[j]
                        else:
                            rest.append(j)
                    if p in todo:
                        continue
                    seq2 = seq[:a] + up[::-1] + rest[::-1] + seq[b + 1:]
                else:
                    b = min(n - 1, b + int(draw() * 30))
                    down, rest, todo = [], [], {p}
                    for j in seq[a:b + 1]:
                        if j in todo:
                            down.append(j)
                            todo |= succs[j]
                        else:
                            rest.append(j)
                    seq2 = seq[:a] + rest + down + seq[b + 1:]
            ends2 = [replay(seq2, pick2, *c[1:], a, e) for c, e in zip(TU["CASES"], ends)]
            s2 = sum(c[0] * max(e) for c, e in zip(TU["CASES"], ends2))
            if s2 <= span + TU["HOT"] * (1 - step / TU["MEND"]):
                span, seq, pick, ends = s2, seq2, pick2, ends2
                if span < PLAN[n][0]:
                    PLAN[n] = (span, seq, pick)
    return [prog[i][0][PLAN[n][2][i]][2] for i in PLAN[n][1]]


def rank_program(g, core, T, topo):
    rank = T.rank_of(core)
    if rank is None:
        return
    N = len(T.cores)
    CY, PCY, GA = TU["CY"], TU["PCY"], TU["GA"]
    queues = {"v": g.vector, "s": g.scalar, "t": g.tensor, "g": g, "y": g.sync}
    semof = {"v": "sv", "s": "ss_", "t": "st", "g": "sg"}
    tick = {"v": 0, "s": 0, "t": 0, "g": 0}
    known = {e: {} for e in queues}
    snaps = {}
    acc = {}
    prog = []
    ndma, local, arrived = [0], [0], {}
    slow = [1.0]
    first = [0.0]

    def ap(v):
        if v[0] == "ind":
            return T[v[1][0]][:, v[1][1]:v[1][2]].indirect(T[v[2][0]][:, v[2][1]:v[2][2]])
        n, a, b, s = v
        return T[n][:, a:b] if s == 1 else T[n][:, a:b:s]

    def need(e, outs, ins):
        w = {}
        for lst, wr in ((outs, True), (ins, False)):
            for (n, a, b, s) in lst:
                for (src, cnt, a2, b2, s2, wr2) in acc.get(n, []):
                    if (src == e or n not in PSUMS) and (not (wr or wr2) or not hits((a, b, s), (a2, b2, s2))):
                        continue
                    w[src] = max(w.get(src, 0), cnt)
        k = known[e]
        w = {s: c for s, c in w.items() if k.get(s, 0) < c}
        for s, c in list(w.items()):
            if any(s2 != s and snaps[(s2, c2)].get(s, 0) >= c for s2, c2 in w.items()):
                w.pop(s)
        for s, c in w.items():
            queues[e].wait_ge(T.sem[semof.get(s, s)], c)
            for s2, c2 in [(s, c)] + list(snaps[(s, c)].items()):
                k[s2] = max(k.get(s2, 0), c2)

    def note(e, src, cnt, outs, ins):
        snaps[(src, cnt)] = dict(known[e]) if e else {}
        for lst, wr in ((outs, True), (ins, False)):
            for (n, a, b, s) in lst:
                old = acc.get(n, [])
                if wr and s == 1:
                    old = [o for o in old if not (o[2] >= a and o[3] <= b and (n not in PSUMS or o[0] == src))]
                else:
                    old = [o for o in old if not (o[0] == src and o[2:] == (a, b, s, wr))]
                acc[n] = old + [(src, cnt, a, b, s, wr)]

    def op(outs, ins, *variants):
        ro = [v[1] if v[0] == "ind" else v for v in outs]
        ri = [v[2] for v in outs if v[0] == "ind"]
        for v in ins:
            ri += [v[1], v[2]] if v[0] == "ind" else [v]

        def emitter(e, calls):
            def emit():
                need(e, ro, ri)
                for c in calls[:-1]:
                    c()
                tick[e] += 1
                calls[-1]().then_inc(T.sem[semof[e]], 1)
                note(e, e, tick[e], ro, ri)
            return emit
        prog.append(([(e, cost + TU["OV"], emitter(e, calls)) for e, calls, cost in variants], ro, ri, None, first[0]))

    def num(v):
        return 16 * (v[2][2] - v[2][1]) if v[0] == "ind" else (v[2] - v[1] + v[3] - 1) // v[3]

    def tm(n, *vs):
        two = all(SCRATCH[v[0]][2] in ("bfloat16", "float16") for v in vs)
        return CY * max(64, n * (0.5 if two else 1))

    def vcopy(o, i):
        n = num(i)
        op([o], [i], ("v", [lambda: g.vector.tensor_copy(ap(o), ap(i))],
                      3.8 * CY * n if o[0] == "ind" else GA * CY * n if i[0] == "ind" else tm(n, o, i)))

    def vtt(o, a, b, f):
        op([o], [a, b], ("v", [lambda: g.vector.tensor_tensor(ap(o), ap(a), ap(b), f)],
                         CY * max(64, num(b) * (3.8 if o[0] == "ind" else 1 if a[0] in PSUMS or b[0] in PSUMS else TU["TT"] if a[0] == "ind" else 2))))

    def vts(o, a, s1, f1, s2=None, f2=None):
        x1, x2 = [ap(s) if isinstance(s, tuple) else s for s in (s1, s2)]
        cols = [s for s in (s1, s2) if isinstance(s, tuple)]
        t = GA * CY * num(a) if a[0] == "ind" else tm(num(a), o, a)
        if f2 is None:
            op([o], [a] + cols, ("v", [lambda: g.vector.tensor_scalar(ap(o), ap(a), x1, None, f1)], t))
        else:
            op([o], [a] + cols, ("v", [lambda: g.vector.tensor_scalar(ap(o), ap(a), x1, x2, f1, f2)], t))

    def vset(o, c):
        op([o], [], ("v", [lambda: g.vector.memset(ap(o), c)], tm(num(o), o)))

    def sact(o, i, f=AF.Copy, bias=0.0, scale=1.0):
        n = num(i)
        cols = [c for c in (bias, scale) if isinstance(c, tuple)]
        bb, sc = [ap(c) if isinstance(c, tuple) else c for c in (bias, scale)]
        op([o], [i] + cols,
           ("s", [lambda: g.scalar.activation(ap(o), ap(i), f, bias=bb, scale=sc)],
            CY * (GA * n if i[0] == "ind" else max(64, n)) + 0.01))

    def lin(o, i, scale=1.0, bias=0.0, relu=False):
        n = num(i)
        ind = i[0] == "ind"
        sv = ("s", [lambda: g.scalar.activation(ap(o), ap(i), AF.Relu if relu else AF.Identity, bias=bias, scale=scale)],
              CY * (GA * n if ind else max(64, n)) + 0.01)
        tv = CY * GA * n if ind else tm(n, o, i)
        if relu:
            vv = ("v", [lambda: g.vector.tensor_scalar(ap(o), ap(i), bias, 0.0, OP.add, OP.max)], tv)
        elif scale == 1.0 and bias == 0.0:
            vv = ("v", [lambda: g.vector.tensor_copy(ap(o), ap(i))], tv)
        elif scale == 1.0:
            vv = ("v", [lambda: g.vector.tensor_scalar(ap(o), ap(i), bias, None, OP.add)], tv)
        else:
            vv = ("v", [lambda: g.vector.tensor_scalar(ap(o), ap(i), scale, bias, OP.mult, OP.add)], tv)
        op([o], [i], sv, vv)

    def cut(t, sign):
        def by_vector():
            sign[0] = 1
            return g.vector.tensor_scalar(ap(t), ap(t), 255.0, -255.0, OP.min, OP.add)

        def by_scalar():
            sign[0] = -1
            return g.scalar.activation(ap(t), ap(t), AF.Relu, bias=255.0, scale=-1.0)
        op([t], [t], ("s", [by_scalar], CY * num(t) + 0.01), ("v", [by_vector], tm(num(t), t)))

    def mm(o, terms, start=True, stop=True, more=()):
        n = len(terms)

        def lhs(t):
            return t[0]() if not isinstance(t[0], tuple) else t[0]
        op([o], [x for t in terms for x in t if isinstance(x, tuple)] + list(more),
           ("t", [lambda k=k: g.tensor.matmul(ap(o), ap(lhs(terms[k])), ap(terms[k][1]), start and k == 0,
                                              stop and k == n - 1) for k in range(n)],
            sum(max(64, num(t[1])) * (4 if SCRATCH[t[1][0]][2] == "float32" else 1) + 25 for t in terms) * PCY * slow[0]))

    def asel(o, i, pat, cmp, base, cm):
        op([o], [i], ("g", [lambda: g.affine_select(ap(o), ap(i), pat, cmp, 0.0, base, cm)], 0.17 + 2 * CY * num(o)))

    def iota(o, pat, base, cm):
        if SCRATCH[o[0]][2] == "int32":
            op([o], [], ("g", [lambda: g.iota(ap(o), pat, base, cm)], 0.13 + 2 * CY * num(o)))
        else:
            op([o], [], ("g", [lambda: g.iota(ap(o), pat, base, cm, allow_small_or_imprecise_dtypes=True)],
                         0.13 + 2 * CY * num(o)))

    def dma(o_ap, i_ap, outs, ins, lat=2.5):
        def emit():
            need("y", outs, ins)
            s = "d%d" % ndma[0]
            ndma[0] += 1
            g.sync.dma_start(o_ap, i_ap).then_inc(T.sem[s], 16)
            note("y", s, 16, outs, ins)
        prog.append(([("y", 0.1, emit)], outs, ins, lat, first[0]))

    peers = {d: T.cores[(rank + d) % N] for d in (1, 2, 3)}
    homes = {d: T.cores[(rank - d) % N] for d in (1, 2, 3)}

    def split(src, dsts):
        away = [c for c in dsts if topo.chip(c) != topo.chip(src)]
        pool = topo.engines(src, away[0])
        n = len(pool) // len(away)
        res = {c: pool[k * n:(k + 1) * n] for k, c in enumerate(away)}
        for c in dsts:
            if c not in res:
                res[c] = [e for e in topo.engines(src, c) if e not in pool]
        return res

    def send(to, piece, sems, guard=()):
        m = split(core, [to[d] for d in (1, 2, 3)])
        sn, sc, dn, dc, w = piece
        tr, ins = [], [R(sn, sc, sc + 3 * w)]
        for d in (1, 2, 3):
            rid, pid, _ = topo.addr(to[d])
            c = (d - 1) * w
            tr.append(RemoteDMATransfer(
                dst_ids=[DstId(rid=rid, pnc=pid)], dma_engine_mask=sum(1 << e for e in m[to[d]]),
                remote_sem=T.sem[sems + str(d)], src=ap(R(sn, sc + c, sc + c + w)), dst=ap(R(dn, dc + c, dc + c + w))))
            local[0] += len(m[to[d]])
        guard = list(guard)

        def emit():
            need("g", guard, ins)
            g.remote_dma_fused(tr, local_sem=T.sem["loc"])
        prog.append(([("g", 1.0, emit)], guard + [("sent" + sems, 0, 1, 1)], ins, None, first[0]))

    def recv(sems, frm, piece):
        for d in (1, 2, 3):
            r = T.rank_of(frm[d])
            s = 1 if frm is homes else -1
            n = len(split(frm[d], [T.cores[(r + s * j) % N] for j in (1, 2, 3)])[core])
            nm, cc, w = piece
            ro = [R(nm, cc + (d - 1) * w, cc + d * w)]
            arrived[sems + str(d)] = n
            prog.append(([("a", 0.0, lambda d=d, n=n, ro=ro: note(None, sems + str(d), n, ro, []))],
                         ro, [("sent" + sems, 0, 1, 1)], TU["EX"], 0.0))

    turn = {}

    def ring(c, n=512):
        turn[c] = (turn.get(c, 0) + 1) % RINGS[c][0]
        return R("%s%d" % (c, turn[c]), 0, n)

    def F(n=512):
        k = turn.get("f", 0)
        k = (k + k % 2 if n > 512 else k) % 6
        turn["f"] = k + (n + 511) // 512
        return R("fr", 512 * k, 512 * k + n)

    def wide(k, on):
        return [k] if k == 4 or not on else [] if k % 2 else [5 + k // 2]

    def mask():
        turn["m"] = (turn.get("m", 0) + 1) % 4
        return R("nm", 512 * turn["m"], 512 * turn["m"] + 512)

    def PQ(pool, n=512):
        turn[pool] = (turn.get(pool, -1) + 1) % len(POOL[pool])
        return R("p%d" % POOL[pool][turn[pool]], 0, n)

    CH = [(512 * k, 512 * k + 512) for k in range(4)] + [(V, W), (0, 1024), (1024, V)]
    LSB = {d: R("ls", 8 * (d - 1), 8 * d) for d in (1, 2, 3)}
    LSA = R("ls", 0, 24)
    THR = R("th32", 0, 1)
    XA, KEY = R("xa", 0, W), R("key", 0, W)
    ONE = R("one", 0, 512)
    ODD, EVEN, CPID, CTB = [R("col", c, c + 1) for c in (40, 41, 42, 43)]

    def M(name, buf="kh"):
        return R(buf, KB[name], KB[name] + 128) if name in KB else R(name, 0, 128)

    def shifted(name, k, buf="kh"):
        if name in KB:
            return R(buf, KB[name] + 16 - k, KB[name] + 144 - k)
        return R(name, 16 - k, 144 - k)

    def lst(l, t, k):
        o = 64 * t if CH[k][0] < 1024 else 192 + 88 * t
        return R("l%d" % l, o + CH[k][0] // 16, o + CH[k][1] // 16)

    def pc(n, t, k):
        a, b = CH[k]
        o = V * t if k != 4 else 3 * V + GH * t
        return R(n, o + a, o + b)

    def every(n, j):
        return R(n, j, V, 4)

    def nodes(parts):
        for pb, a, s in parts:
            nf = F(num(pb))
            lin(nf, pb, 0.5, MG)
            lin(R("n16", a, a + (num(pb) - 1) * s + 1, s), nf, bias=-(MG + NO))

    def node_lists(l, part, ts, bank, mat="cv", s=4):
        a, n = (0, 64) if part == 0 else (64, 88)
        for i, t in enumerate(ts):
            mm(R(bank, n * i, n * i + n),
               [(shifted(mat + str(t), 16 // s * b), R("n16", s * a + b, s * (a + n), s)) for b in range(s)])
        o = 4 * a + n * ts[0]
        vts(R("l%d" % l, o, o + n * len(ts)), R(bank, 0, n * len(ts)), NO, OP.add)

    def tables(parts, ports, halves=True):
        nodes([p[:3] for p in parts] * halves)
        for pb, a, s, own in parts:
            e = a + (own - 1) * s + 1
            lin(R("pf", a, a + (num(pb) - 1) * s + 1, s), pb)
            vtt(R("dp", a, e, s), R("pid", a, e, s), R(pb[0], 0, own), OP.subtract)
        if ports:
            vts(R("lp", 0, C4), R("pf", 0, C4), 0.5, OP.add)

    def chain(l, k, win, q, bias=0.0, bank=None, out=None):
        lin(q, IND(win, lst(l, 0, k)), bias=bias)
        if bank is None:
            for t in (1, 2, 3):
                vtt(out if out and t == 3 else q, IND(win, lst(l, t, k)), q, OP.add)
            return
        h = F(num(q))
        lin(h, IND(win, lst(l, 2, k)))
        vtt(h, IND(win, lst(l, 3, k)), h, OP.add)
        vtt(q, IND(win, lst(l, 1, k)), q, OP.add)
        sact(bank, h)
        vtt(out or q, bank, q, OP.add)

    def flat(mat, src, pool, use):
        for j in range(4):
            u = PQ(pool)
            mm(u, [(R(mat, 128 * j, 128 * j + 128), R(src, 0, 512))])
            use(j, u)

    dma(T.ini[:, 0:304], T.nxt[:], [R("ini", 0, 304)], [], 2.2)
    dma(T.ini[:, 304:328], T.shw[:], [R("ini", 304, 328)], [], 2.2)
    for k in range(2):
        dma(T.x0i[:, 1024 * k:1024 * k + 1024], T.x0[:, 1024 * k:1024 * k + 1024], [R("x0i", 1024 * k, 1024 * k + 1024)], [],
            4.0)
    dma(T.ini[:, 328:329], T.th[:], [R("ini", 328, 329)], [])
    iota(R("pci", 0, 1), [[0, 1]], 0, 1)
    iota(R("nm", 0, 128), [[64, 2], [0, 64]], 0, 0)
    iota(R("nm", 128, 256), [[0, 2], [1, 64]], 0, 0)
    iota(R("col", 0, 33), [[128, 33]], 0, 0)
    vts(R("pci", 1, 2), R("pci", 0, 1), 1, OP.bitwise_and)
    vcopy(ODD, R("pci", 1, 2))
    vts(EVEN, ODD, -1.0, OP.mult, 1.0, OP.add)
    vts(R("col", 0, 33), R("col", 0, 33), EVEN, OP.mult)
    vts(R("nm", 0, 128), R("nm", 0, 128), EVEN, OP.mult)
    vts(R("nm", 128, 256), R("nm", 128, 256), -0.5, OP.add, ODD, OP.mult)
    vtt(R("g3", 0, 128), R("nm", 0, 128), R("nm", 128, 256), OP.add)
    for b in (1, 2, 4, 8, 16, 32):
        n = min(128 * b, P2 - 128 * b)
        sact(R("g3", 128 * b, 128 * b + n), R("g3", 0, n), AF.Identity, bias=R("col", b, b + 1))
    vcopy(R("lw16", 0, 304), R("ini", 0, 304))
    lin(R("nxf", 0, 304), R("ini", 0, 304), bias=-0.5)
    first[0] = 100.0
    vcopy(LSA, R("ini", 304, 328))
    for k in range(2):
        lin(R("xa", 1024 * k, 1024 * k + 1024), R("x0i", 1024 * k, 1024 * k + 1024))
    sact(R("bs", 0, GH), IND(R("xa", 0, V), LSA))
    send(peers, ("bs", 0, "xa", V, B), "ax1_")
    recv("ax1_", homes, ("xa", V, B))
    first[0] = 0.0
    for a, b in zip([0] + TU["SC"], TU["SC"]):
        vcopy(IND(R("fw", 0, P2), R("lw16", a, b)), R("g3", 16 * a, 16 * b))
    vset(ONE, 1.0)
    vset(R("o32", 0, 64), 1.0)
    vset(R("kb", 256, 1552), 0.0)
    vset(R("un", 0, 1028), 0.0)
    vset(R("nw", 0, 144), 0.0)
    o128, o64, o8 = R("one", 0, 128), R("o32", 0, 64), R("one", 0, 8)
    for c in (0, 1):
        for h in (0, 1):
            asel(R("nt%d" % c, h, 128, 2), o64, [[-16, 8], [-2, 4], [1000, 2]], OP.is_equal, -8 * c - h, 1)
    for t in range(4):
        asel(shifted("cv%d" % t, 0, "kb"), o128, [[-16, 8], [1000, 4], [-4, 4]], OP.is_equal, -t, 1)
    lin(R("kh", KB["cv0"], 1264), R("kb", KB["cv0"], 1264))
    for h in (0, 1):
        asel(shifted("pm%d" % h, 0, "kb"), o128, [[-16, 8], [1000, 2], [-2, 8]], OP.is_equal, -h, 1)
    lin(R("kh", 1264, 1552), R("kb", 1264, 1552))
    asel(M("idn", "kb"), o128, [[-1, 128]], OP.is_equal, 0, 1)
    for n, lo in (("wz", 0), ("wq", 2)):
        o = R("kb", KB[n] + 16, KB[n] + 144, 16)
        asel(o, o8, [[-16, 8]], OP.is_ge, -lo, 1)
        asel(o, o, [[16, 8]], OP.is_ge, lo + 1, -1)
    for o, pat in ((M("blk", "kb"), [[-16, 8], [0, 16]]), (shifted("rz", 0, "kb"), [[-16, 8], [-1000, 4], [0, 4]])):
        asel(o, o128, pat, OP.is_ge, 0, 1)
        asel(o, o, [[16, 8], [0, 16]], OP.is_ge, 15, -1)
    lin(R("kh", 0, KB["cv0"]), R("kb", 0, KB["cv0"]))
    for n, i, c in (("neh", "idn", -1.0), ("nqh", "idn", -0.25), ("nhh", "idn", -0.5), ("cw", "idn", 8192.0 * EO), ("pn", "idn", -2.0 ** 30)):
        sact(M(n), M(i, "kb"), scale=c)
    for n, i, c in (("rn", "rz", -1.0), ("ro", "rz", -8192.0), ("eh", "wz", 4096.0)):
        sact(R(n, 0, 144), R("kb", KB[i], KB[i] + 144), scale=c)
    asel(M("bl4"), o128, [[-4, 32], [0, 4]], OP.is_ge, 0, 1)
    asel(M("bl4"), M("bl4"), [[4, 32], [0, 4]], OP.is_ge, 3, -1)
    asel(R("ul", 0, 512), ONE, [[-4, 4], [-16, 8], [0, 16]], OP.is_equal, 0, 1)
    iota(R("vid", 0, 128), [[0, 4], [16, 32]], 0, 0)
    vts(R("pci", 3, 4), R("pci", 0, 1), 15, OP.bitwise_and)
    vcopy(R("col", 44, 45), R("pci", 3, 4))
    sact(R("vid", 0, 128), R("vid", 0, 128), AF.Identity, bias=R("col", 44, 45))
    for s in (0, 1):
        asel(R("un", 4 + 2 * s, 1028, 16), R("one", 0, 64), [[-4, 4], [-1, 2], [-16, 8]], OP.is_equal, -2 * s, 1)
    for h in (0, 1):
        asel(R("swd", h, 128, 2), o64, [[-2, 64]], OP.is_equal, h - 1, 1)
        asel(R("nw", 16 + h, 144, 2), o64, [[-16, 8], [1000, 2], [-4, 4]], OP.is_equal, -h, 1)
    vtt(M("swd"), M("swd"), M("idn", "kb"), OP.subtract)
    iota(R("pid", 0, 512), [[8, 512]], 0, 0)
    vts(R("pci", 2, 3), R("pci", 0, 1), 2, OP.arith_shift_right, 3, OP.bitwise_and)
    vts(CPID, R("pci", 2, 3), 2.0, OP.mult, -0.5, OP.add)
    vts(CPID, CPID, ODD, OP.add)
    vts(CTB, ODD, -1.0, OP.mult, -1.0, OP.add)
    vts(M("hc"), M("swd"), 0.0, OP.max, CTB, OP.mult)
    vtt(M("cw"), M("cw"), M("hc"), OP.add)
    sact(R("pid", 0, 512), R("pid", 0, 512), AF.Identity, bias=CPID)
    vcopy(THR, R("ini", 328, 329))
    iota(R("yw", 4096, P2), [[1, 768]], 4096, 0)

    nodes([(R("nxf", 0, 304), 0, 1)])
    for part in (0, 1):
        node_lists(1, part, (0, 1), "p%d" % (6 + part), "pm", 2)
    for k in (5, 6, 4):
        for t in (0, 1):
            lin(pc("ga", t, k), IND(XA, lst(1, t, k)), bias=-1.5 * (t == 0))
    for c in (0, 1):
        mm(R("p%d" % (4 + c), 0, 304), [(M("nt%d" % c), R("nxf", 0, 304))], stop=False)
        mm(R("p%d" % (4 + c), 0, 304),
           [(shifted("wq", 2 + 4 * (i // 2) + i % 2, "kb"), R("fw", 8 * c + i, P2, 16)) for i in range(8)], start=False)
    tables([(R("p%d" % (4 + c), 0, 304), c, 2, 256) for c in (0, 1)], True)
    for part in (0, 1):
        node_lists(1, part, (2, 3), "p%d" % (6 + part))
    lin(R("fw", 4096, P2), R("g3", 4096, P2))
    vset(R("nm", 0, V), 0.0)
    for d in (1, 2, 3):
        vcopy(IND(R("nm", 0, V), LSB[d]), o128)
    mm(R("p7", 0, 512), [(shifted("rz", 4 * j, "kb"), every("nm", j)) for j in range(4)])
    lin(R("nmq", 0, 512), R("p7", 0, 512), -65.0 / 16, 1.0)

    I1, NI, NQ = M("idn"), M("neh"), M("nqh")
    for l in (1, 2, 3):
        srcs = ["ga"] if l < 3 else ["ga", "gb"]
        gk = "gb" if l < 3 else "g3"
        LW = R("lw%d" % l, 0, 512)
        dl, p0 = "dl%d" % l, "sp%d" % l if l < 3 else "x0i"
        zb, tk = {}, {}

        def gathers(k):
            a, b = CH[k]
            n = b - a
            for c in wide(k, TU["WA"]):
                for t in range(4):
                    if l in TU["DA"] and t == 3 and k < 4:
                        vtt(pc("ga", t, c), IND(XA, lst(l, t, c)), pc("ga", 2, c), OP.subtract)
                    elif l > 1 or t > 1:
                        lin(pc("ga", t, c), IND(XA, lst(l, t, c)), bias=-1.5 * (l < 3 and t == 0))
                    if l == 3:
                        lin(pc("gb", t, c), IND(R("nm", 0, W), lst(l, t, c)), bias=-0.375)
            zb[k] = R("p%d" % k, 0, n)
            mm(zb[k], [(NQ, pc(s, t, k)) for s in srcs for t in (0, 1)], stop=False)
            mm(zb[k], [(M("nhh") if l in TU["DA"] and t == 2 and k < 4 else NQ, pc(s, t, k)) for s in srcs for t in (2, 3)],
               start=False)
            vtt(R("x0i", a, b), zb[k], R("xa", a, b), OP.add)

        def sized(k):
            a, b = CH[k]
            n = b - a
            t = e = tk[k] = R("tk", a, b) if k < 4 else ring("t", n)
            if l > 1:
                e = ring("e", n) if l == 2 else F(n)
            sact(e, R("x0i", a, b), AF.Abs)
            if l > 1:
                vts(t, e, 255.0, OP.min)
            o = PQ("size", n) if k < 4 else R("p5", 0, n)
            mm(o, [(M("blk"), t)])
            lin(R("key", a, b), o, bias=-EO)
            if k < 4:
                vts(zb[k], e, THR, OP.is_ge, 0.25, OP.mult)

        def detail(k):
            a, b = CH[k]
            d, m = R("x0i", a, b), zb[k]
            vtt(R(dl, a, b), m, d, OP.mult)
            vts(d, d, 2, OP.arith_shift_right)
            if l < 3:
                lin(m, m, bias=KP / 4)
            else:
                lin(m, m, -4.0, 1.0)
            vtt(R(p0, a, b), m, d, OP.mult)

        def chosen():
            for t in range(4):
                for c in (5, 6):
                    lin(pc(gk, t, c), IND(KEY, lst(l, t, c)))
            o = R("p4", 0, 512)
            mm(o, [(M("cw"), R("nmq", 0, 512))] + [(M("pn"), R("lw%d" % j, 0, 512)) for j in range(1, l)] +
               [(shifted("ro", 4 * j), every("tk", j)) for j in range(4)], stop=False)
            for t in range(4):
                mm(o, [(shifted("eh", 4 * j + t), R(gk, V * t + j, V * t + V, 4)) for j in range(4)], False, t == 3)
            vtt(R("c01", 0, 512), o, R("dp", 0, 512), OP.is_ge)
            mm(o, [(M("bl4"), R("c01", 0, 512))])
            lin(LW, o, bias=-3.0, relu=True)

        def likeness(k):
            terms = []
            first[0] = TU["BL"] if l < 3 else TU["B3"]
            us = {}
            for x, y in ((0, 0), (0, 1), (1, 0), (1, 1)):
                tn, sign = ring("t"), [1]
                if l in TU["DA"] and x:
                    u = us[y]
                    mm(u, [(I1, pc("ga", 3, k))], start=False)
                else:
                    u = us[y] = PQ("diff" if k < TU["LK"] or l == 3 else "flat")
                    mm(u, [(I1, pc(s, 2 + x, k)) for s in srcs] + [(NI, pc(s, y, k)) for s in srcs], stop=l not in TU["DA"])
                shift = -1.5 if l < 3 and y == 0 else 0.0
                if l == 1:
                    lin(tn, u, bias=shift, relu=True)
                else:
                    sact(tn, u, AF.Abs, bias=shift)
                    cut(tn, sign)
                terms += [(lambda j=j, sign=sign, same=x == y: shifted("rz" if same == (sign[0] > 0) else "rn", 4 * j),
                           R(tn[0], j, 512, 4)) for j in range(4)]
            mm(R("p7", 128 * k, 128 * k + 128), terms, more=[R("kh", KB["rz"], KB["rz"] + 144), R("rn", 0, 144)])
            first[0] = 0.0

        def links():
            o, c = R("p7", 0, 512), R("c01", 0, 512)
            if l in TU["SG"]:
                sact(c, o, AF.Sign, bias=-0.5)
                sact(c, c, AF.Relu)
            else:
                vts(c, o, 0.0, OP.is_gt)
            mm(o, [(M("swd"), R("pf", 0, 512))])
            vtt(o, o, c, OP.mult)
            vtt(o, o, R("dp", 0, 512), OP.subtract)
            vtt(o, o, LW, OP.mult)
            vtt(o, o, R("pid", 0, 512), OP.add)
            lin(R("hi", 0, 512), o)
            vtt(R("lo", 0, 512), o, R("hi", 0, 512), OP.subtract)

        def unwrap(pool):
            for i in range(8):
                bk = PQ(pool)
                mm(bk, [(R("un", 4 + 128 * i - r, 132 + 128 * i - r), R(x, 0, 512))
                        for r, x in ((0, "hi"), (1 if l < 3 else 0, "lo"))])
                if l < 3:
                    lin(R("fw", i, 4096, 8), bk)
                else:
                    lin(R("yw", i, 4096, 8), bk, bias=0.5)

        def own(k):
            a, b = CH[k]
            x = R("xa", a, b)
            if l < 3:
                b1 = PQ("own")
                s = R("sp%d" % l, a, b)
                for c in wide(k, TU["WC"]):
                    chain(l, c, KEY, R("sp%d" % l, *CH[c]), 0.0, b1 if k in TU["HC"] else None)
                z = F()
                lin(z, s, bias=MG * KP / 4)
                lin(b1, z, 4.0 / KP, -MG)
                vtt(x, b1, x, OP.add)
                if l not in TU["LATE"]:
                    b2 = PQ("own")
                    lin(b2, z, bias=-MG * KP / 4)
                    vtt(s, s, b2, OP.subtract)
            else:
                o = PQ("flat", b - a)
                gs = [R("g3", V * t + a, V * t + b) if k < 4 else ring("t", GH) for t in range(4)]
                for c in wide(k, TU["W3"]):
                    for t in range(4):
                        lin(gs[t] if k == 4 else pc("g3", t, c), IND(KEY, lst(l, t, c)))
                mm(o, [(NQ, s) for s in gs])
                if k < 4:
                    vtt(x, x, o, OP.subtract)
                else:
                    lin(R("ss", 0, GH), o, -1.0)

        def sums(j):
            for k in range(4 * (j in TU["LATE"])):
                s, z, b2 = R("sp%d" % j, *CH[k]), F(), PQ("sums")
                lin(z, s, bias=MG * KP / 4)
                lin(b2, z, bias=-MG * KP / 4)
                vtt(s, s, b2, OP.subtract)
            border("sp%d" % j, 1, "rs%d" % j)
            sact(R("sg%d" % j, 0, GH), IND(R("sp%d" % j, 0, V), LSA))

        def border(buf, rc, rs="rs%d" % l):
            for d in (1, 2, 3):
                s, bt = 1 if rs == "rs3" else 2, R("bt", B * rc, B * rc + B)
                vtt(bt, IND(R(buf, 0, V), LSB[d]), R(rs, rc + (d - 1) * s * B, d * s * B, s), OP.add)
                vcopy(IND(R(buf, 0, V), LSB[d]), bt)

        def kept():
            o, s = PQ("kept", 128), F(128)
            mm(o, [(shifted("cv0", 4 * b, "kb"), R(LW[0], b, 512, 4)) for b in range(4)])
            lin(o, o, float(W if l < 3 else -V), float(0 if l < 3 else V))
            vtt(s, o, R("vid", 0, 128), OP.add)
            vcopy(R("s%d" % l, 0, 128), s)

        if l == 3:
            iota(R("nm", 0, V), [[0, V]], 0, 0)
            for src, o in ((R("bs", 0, GH), R("c01", 0, GH)), (R("xa", V, W), R("nm", V, W))):
                t = ring("t", GH)
                lin(t, src)
                vtt(o, src, t, OP.subtract)
                for d in (1, 2, 3) * (o[0] == "c01"):
                    vcopy(IND(R("nm", 0, V), LSB[d]), R("c01", (d - 1) * B, d * B))
        for k in (TU["ORD"] if l > 1 else [0, 1, 2, 4, 3]):
            gathers(k)
            sized(k)
        for k in range(4):
            detail(k)
            if l == 3:
                lin(R("xa", *CH[k]), R("xa", *CH[k]), 0.25)
        chosen()
        for k in range(TU["LK"] * (l < 3)):
            likeness(k)
        iota(R("key", V, W), [[0, GH]], 0, 0)
        flat("ul", LW[0], "flat", lambda j, u: vtt(every("key", j), u, every(p0, j), OP.mult))
        for k in range(TU["LK"], 4 * (l < 3)):
            likeness(k)
        rs = "rs%d" % l
        xg = [R("xa", V, W)]
        if l < 3:
            q, z, b4 = F(GH), F(GH), PQ("own", GH)
            first[0] = TU["BG"]
            chain(l, 4, KEY, q)
            lin(z, q, bias=MG * KP / 4)
            lin(b4, z, bias=-MG * KP / 4)
            lin(R("sh", 0, 768, 2), z, 4.0 / KP, -MG)
            vtt(R("sh", 1, 768, 2), q, b4, OP.subtract)
            send(homes, ("sh", 0, rs, 0, 2 * B), "as%d_" % l, xg)
            first[0] = 0.0
            recv("as%d_" % l, peers, (rs, 0, 2 * B))
            first[0] = TU["BK"]
            links()
            unwrap("flat")
            first[0] = 0.0
            for k in range(4):
                own(k)
            border("xa", 0)
            sact(R("bs", 0, GH), IND(R("xa", 0, V), LSA))
            send(peers, ("bs", 0, "xa", V, B), "ax%d_" % (l + 1))
            recv("ax%d_" % (l + 1), homes, ("xa", V, B))
            for a in range(0, C4, TU["DW"]):
                lin(R("gb", 16 * a, 16 * (a + TU["DW"])), IND(R("fw", 0, P2), R("lp", a, a + TU["DW"])))
            for part, (a, b) in enumerate(((0, 256), (256, C4))):
                bk = R("p%d" % TU["WB4"][part], 0, b - a)
                mm(bk, [(shifted("wz" if i % 4 < 2 else "wq", i), R("gb", 16 * a + i, 16 * b, 16)) for i in range(16)])
                tables([(bk, a, 1, 256)], l < 2 and part == 1)
                node_lists(l + 1, part, range(4), "p%d" % TU["WB4"][2 + part])
            if l not in TU["LATE"]:
                sums(l)
            kept()
            if l == 2:
                bk = PQ("kept", 304)
                mm(bk, [(shifted("nw", 8 * c), R("pf", c, C4, 2)) for c in (0, 1)])
                vts(R("lw16", 0, 304), bk, 0.5, OP.add)
        else:
            own(4)
            send(homes, ("ss", 0, rs, 0, B), "as3_", xg)
            recv("as3_", peers, (rs, 0, B))
            for k in range(4):
                own(k)
            if TU["AC"]:
                iota(R("yw", 0, V), [[0, V]], 0, 0)
                border("yw", 0)
                lin(R("rs3", 0, GH), IND(R("yw", 0, V), LSA))
                vtt(R("bs", 0, GH), IND(R("xa", 0, V), LSA), R("rs3", 0, GH), OP.add)
                for d in (1, 2, 3):
                    vcopy(IND(R("xa", 0, V), LSB[d]), R("bs", (d - 1) * B, d * B))
            else:
                border("xa", 0)
                sact(R("bs", 0, GH), IND(R("xa", 0, V), LSA))
            send(peers, ("bs", 0, "xa", V, B), "ab3_")
            for j in TU["LATE"]:
                sums(j)
            vtt(R("bs", GH, 3 * GH, 2), R("bs", 0, GH), R("sg2", 0, GH), OP.subtract)
            vtt(R("bs", GH + 1, 3 * GH, 2), R("bs", GH, 3 * GH, 2), R("sg1", 0, GH), OP.subtract)
            send(peers, ("bs", GH, "rb", 0, 2 * B), "ab2_")
            recv("ab3_", homes, ("xa", V, B))
            recv("ab2_", homes, ("rb", 0, 2 * B))
            kept()
            lin(R("key", V, W), R("rb", 0, 768, 2))
            slow[0] = TU["PD"]
            for k in range(4):
                likeness(k)
            links()
            unwrap("late")

    def undo(l, src, dst, sp):
        for k in (range(4) if l < 3 else (3, 2, 1, 0)):
            a, b = CH[k]
            y, dl = PQ("undo"), R("dl%d" % l, a, b)
            chain(l, k, R(src, 0, W), F(), -0.375, y if k in TU["HU"][l - 1] else None, R("x0i", a, b))
            lin(y, R("x0i", a, b), 0.25)
            vtt(dl, y, dl, OP.add)
            both = R("dl3", a, V + b) if l == 3 else R(src, a, W + b)
            pick = IND(both, R("s%d" % l, a // 16, b // 16))
            if sp is None:
                lin(R(dst, a, b), pick, 4.0)
                dma(T.yx[:, a:b], ap(R(dst, a, b)), [], [R(dst, a, b)])
            else:
                vtt(R(dst, a, b), pick, R(sp, a, b), OP.subtract)

    undo(3, "xa", "key", "sp2")
    lin(R("xa", V, W), R("rb", 1, 768, 2))
    for nm, a, n in (("dl3", 0, V), ("sp2", V, V), ("rb", 2 * V, 768)):
        for c in range(0, n, 1024):
            e = min(c + 1024, n)
            lin(R(nm, c, e), IND(R("yw", 0, P2), R("lw16", (a + c) // 16, (a + e) // 16)))
        dma(T.yn[:, a:a + n], T[R(nm, 0, n)[0]][0:128:16, 0:n], [], [R(nm, 0, n)])
    undo(2, "key", "xa", "sp1")
    undo(1, "xa", "key", None)

    for emit in ordered(prog):
        emit()

    for e in ("v", "s", "t", "g"):
        g.wait_ge(T.sem[semof[e]], tick[e])
    for k in range(ndma[0]):
        g.wait_ge(T.sem["d%d" % k], 16)
    for s, n in arrived.items():
        g.wait_ge(T.sem[s], n)
    g.wait_ge(T.sem["loc"], local[0])
